import numpy as np, ml_dtypes
CORES = [16,17,18,19,150,151]
N = 6
BF = ml_dtypes.bfloat16
W, P, RO, L = 1408, 1, 5, 256
Q = 1.0
def parts(rng):
    share = rng.choice(np.array([0.015, 0.025, 0.04]), (N, 8, 1, 1)) * Q
    r = np.where(rng.random((N, 8, 16, W)) < share, rng.integers(5, 16, (N, 8, 16, W)), rng.integers(0, 5, (N, 8, 16, W)))
    hot = (rng.random((N, 8, 1, W)) < 0.004 * Q) & (rng.random((N, 8, 16, W)) < 0.7)
    r = np.where(hot, 15, r)
    return r, rng.integers(0, 256, (N, 8, 16, W)), rng.integers(0, W, (N, 8, 16, W)), rng.integers(0, W, (N, 8, 16, L))
def pack(r, x, k, s):
    return {"rec": np.ascontiguousarray(r.reshape(N, 128, W)).astype(np.float32).astype(BF), "wealth": np.ascontiguousarray(x.reshape(N, 128, W)).astype(np.float32).astype(BF),
            "kin": np.ascontiguousarray(k.reshape(N, 128, W)).astype(np.int32), "slips": np.ascontiguousarray(s.reshape(N, 128, L)).astype(np.int32)}
def setup_inputs(rng):
    r, x, k, s = parts(rng)
    return pack(r, x, k, s)
def setup_inputs_spread(rng):
    e = np.exp2(4.3 + 3.9 * rng.random((N, 8, 16, 1))) / Q
    r = np.minimum((16 * rng.random((N, 8, 16, W)) ** e).astype(np.int64), 15)
    x = np.minimum((np.exp2(8 * rng.random((N, 8, 1, W))) * rng.random((N, 8, 16, W))).astype(np.int64), 255)
    k = np.minimum((W * rng.random((N, 8, 16, W)) ** 2).astype(np.int64), W - 1)
    s = np.minimum((W * rng.random((N, 8, 16, L)) ** (1 + rng.random((N, 8, 1, L)))).astype(np.int64), W - 1)
    return pack(r, x, k, s)
def setup_inputs_ends(rng):
    r = 15 * (rng.random((N, 8, 16, W)) < 0.02 * Q)
    r = np.where(rng.random((N, 8, 1, W)) < 0.004 * Q, 15, r)
    w = rng.random((N, 8, 1, W)); x = 255 * np.where(w < 0.4, 0, np.where(w < 0.7, 1, rng.integers(0, 2, (N, 8, 16, W))))
    u = rng.random((N, 8, 16, W))
    k = np.where(u < 0.36, 0, np.where(u < 0.72, W - 1, np.where(u < 0.78, W - 2, rng.integers(0, W, (N, 8, 16, W)))))
    for first, places in ((1, ((2, W - 2), (15, W - 1))), (3, ((4, W - 1), (9, 5), (12, 5))), (6, ((4, 5), (9, W - 1)))):
        c = np.zeros((16, 1), np.int64)
        for m, v in places: c[m, 0] = v
        k[:, :, :, first::8] = c; x[:, :, :, first::8] = 0
    m = (np.arange(W) & 4) == 4
    k[:, 7] = np.where(m & (k[:, 7] == W - 1), 0, k[:, 7])
    a, b = W - 600, W - 344
    k[:, :, :, a:b] = 0; r[:, :, :, a:b] = 0; x[:, :, :, a:b] = 0
    k[:, :, :, W - 40:W - 24] = 0; r[:, :, :, W - 40:W - 24] = 0; x[:, :, :, W - 40:W - 24] = 0; k[:, :, 15, W - 32:W - 24] = W - 1
    r[:, :, :, 0] = 0; r[:, :, :, W - 1] = 15 * (rng.random((N, 8, 16)) < rng.choice(np.array([0.05, 0.15, 0.3]), (N, 8, 1))); r[:, 7, :, W - 1] = 15
    r[:, :, :, W - 2] = 0; r[:, :, :, 5] = 0
    x[:, :, :, 0] = 0; x[:, :, :, W - 1] = 255; x[:, :, :, 5] = 255; x[:, :, :, W - 2] = 255; x[:, :, 15, W - 2] = 254
    u = rng.random((N, 8, 16, L)); s = np.where(u < 0.35, 0, np.where(u < 0.7, W - 1, rng.integers(1, W - 600, (N, 8, 16, L))))
    s[:, :, :, 112:128] = W - 1
    for q in range(2):
        for g in range(8): s[q, g, :, 240:] = a + rng.permutation(256).reshape(16, 16)
    p = np.arange(16); s[N - 1, 7, :, 255] = np.where((p & 1) == 0, W - 40 + (p >> 1), W - 32 + (p >> 1))
    return pack(r, x, k, s)
def setup_inputs_corners(rng):
    r, x, k, s = parts(rng); own = np.arange(W); lane = np.arange(L)
    k[:, :4] = own
    n = rng.choice(np.array([0, 1, 3, 7, 8, 9, 11, 12, 13, 16]), (1, 4, 1, W)); order = np.argsort(rng.random((1, 4, 16, W)), axis=2)
    high = np.where(rng.random((N, 4, 16, W)) < 0.7, 15, rng.integers(6, 16, (N, 4, 16, W)))
    low = np.where(rng.random((N, 4, 16, W)) < 0.15, 5, rng.integers(0, 5, (N, 4, 16, W)))
    high[:, 1] = 6; low[:, 1] = 5; high[:, 2] = 6 + (own & 7); low[:, 2] = 5 + (own & 7)
    r[:, :4] = np.where(order < n, high, low)
    s[:, :2] = lane + 256 * rng.integers(0, W // 256, (N, 2, 16, L))
    s[:, 4] = np.repeat(rng.integers(0, W, (N, 1, 16)), 16, axis=2)
    for q in range(N):
        if (q & 1) == 0: s[q, 5] = rng.integers(0, W)
        else: s[q, 5] = lane + 256 * rng.integers(0, W // 256, (16, L))
    k[:, 6] = rng.choice(np.array([0, W - 1, W // 2]), (N, 1, W))
    z = rng.integers(0, 3, (N, 16, W)); k[:, 7] = np.where(z == 0, 0, np.where(z == 1, W - 1, own))
    r[:, 6:, :, [0, W - 1, W // 2]] = np.where(rng.random((N, 2, 16, 3)) < 0.2, 15, rng.integers(0, 5, (N, 2, 16, 3)))
    s[:, 7] = np.where(rng.random((N, 16, L)) < 0.1, rng.choice(np.array([0, W - 1]), (N, 16, L)), s[:, 7])
    x[:, 1] = 255; x[:, 2] = 255 * rng.integers(0, 2, (N, 1, W))
    return pack(r, x, k, s)
def setup_inputs_alike(rng):
    r, x, k, s = parts(rng)
    pool = np.repeat(rng.integers(0, W, (N, 8, 16, 6)), 16, axis=2)
    few = np.take_along_axis(pool, rng.integers(0, 6, (N, 8, L, 16)), 3).transpose(0, 1, 3, 2)
    s[:, ::2] = few[:, ::2]
    s[:, 1::4, :, 1::2] = np.roll(s[:, 1::4, :, 0::2], 5, axis=2)
    s[:, 3] = W - 1 - rng.integers(0, 40, (N, 16, L))
    k[:, 1::2, 8:] = k[:, 1::2, :8]
    x = np.take_along_axis(rng.choice(np.array([0, 128, 255]), (N, 8, 16, 5)), rng.integers(0, 5, (N, 8, 1, W)), 3)
    return pack(r, x, k, s)
def setup_inputs_full(rng):
    r, x, k, s = parts(rng); own = np.arange(W); lane = np.arange(L); bag = (own >> 4) & 15
    z = 2 * rng.integers(0, 8, N) + 1
    r[:, :3] = rng.integers(0, 5, (N, 3, 16, W))
    even = own[(own & 16) == 0]; r[:, 1, bag[even], even] = 15; k[:, 1] = k[:, 1] | 16
    hot = np.repeat((bag[None, :] == z[:, None])[:, None, :], 8, axis=1)
    hot[:, :2, :256] = False; hot[:, 2, :256:2] = False
    r = np.where(hot[:, :, None, :], 15, r)
    named = np.take_along_axis(hot, k.reshape(N, 8, 16 * W), 2).reshape(N, 8, 16, W); k = np.where(named, k ^ 32, k)
    s[:, :3] = lane + 256 * rng.integers(0, W // 256, (N, 3, 16, L))
    inbag = (lane >> 4)[None, :] == z[:, None]
    first = np.arange(16)[:, None] == ((5 * (lane & 15)) & 15)[None, :]
    s = np.where(inbag[:, None, None, :], lane + 256 * np.where(first, 0, rng.integers(1, W // 256, (N, 8, 16, L))), s)
    return pack(r, x, k, s)
def check_inputs(d):
    bad = []
    for k, lo, hi in (("rec", 0, 15), ("wealth", 0, 255), ("kin", 0, W - 1), ("slips", 0, W - 1)):
        v = np.asarray(d[k]).astype(np.float64)
        if not (np.min(v) >= lo and np.max(v) <= hi): bad.append("range of " + k)
        elif np.any(v != np.floor(v)): bad.append("whole numbers of " + k)
    return bad
def reference(rec, wealth, kin, slips):
    R = rec.astype(np.float32).astype(np.int64).reshape(N, 8, 16, W); X = wealth.astype(np.float32).astype(np.int64).reshape(N, 8, 16, W)
    K = kin.astype(np.int64).reshape(N, 8, 16, W); S = slips.astype(np.int64).reshape(N, 8, 16, L)
    lane = np.arange(L); b = lane >> 4; j = lane & 15; a = np.zeros((N, 16), np.int64)
    lower = lane[None, :] < lane[:, None]
    def picks(tab, ks):
        return np.take_along_axis(tab, ks.reshape(8, 1, 16 * L), 2).reshape(8, 16, 16, L)
    for t in range(RO):
        T = 8 + t; later = []
        for r in range(N):
            o = (a[r][b] + 5 * j + t) & 15
            c = S[r][:, o, lane]
            ci = c[:, None, :]
            counts = ~np.any((c[:, :, None] == c[:, None, :]) & lower[None], axis=2)
            kc = np.take_along_axis(K[r], ci, 2)
            M = np.maximum(np.take_along_axis(R[r], ci, 2), np.max(picks(R[r], kc), axis=2))
            for u in range(P):
                q = (r + 1 + (P * t + u) % (N - 1)) % N
                M = np.maximum(M, np.max(picks(R[q], np.take_along_axis(K[q], ci, 2)), axis=2))
            f = np.sum(M >= T - 2, axis=1)
            bar = (M[:, b, lane] >= T - 3) | (f >= 8)
            barred = counts & bar; inst = counts & ~bar
            torn = inst | (barred & (f >= 12))
            nxt = np.zeros((8, L), bool); nxt[:, :L - 16] = torn[:, 16:]
            moved = barred & (f < 12) & ((f & 1) == 1) & nxt
            sc = np.sum(np.maximum(picks(X[r], kc) - np.take_along_axis(X[r], ci, 2)[:, :, None, :], 0), axis=1)
            best = np.take_along_axis(kc, np.argmax(sc, axis=1)[:, None, :], 1)[:, 0]
            new = np.where(torn | moved, best, c)
            new[:, 16:] = np.where(moved[:, :L - 16], c[:, :L - 16], new[:, 16:])
            later.append((o, c, inst, new))
        for r in range(N):
            o, c, inst, new = later[r]
            S[r][:, o, lane] = new
            gi, li = np.nonzero(inst)
            R[r][gi, b[li], c[gi, li]] = T
            K[r][gi, t, c[gi, li]] = c[gi, li ^ 1]
            a[r] = np.sum(inst.reshape(8, 16, 16), axis=(0, 2))
    return {"yr": R.reshape(N, 128, W).astype(np.float32).astype(BF), "ys": S.reshape(N, 128, L).astype(np.float32)}

@@ -1,0 +1,489 @@
+import numpy as np
+import math
+from concourse.mybir import dt, AluOpType, AxisListType, ActivationFunctionType
+
+W, NR = 1408, 5
+WD = W + 256
+NS = 10
+OWN = ((0, 32), (32, 64), (64, 128), (128, 192), (192, 256))
+PRE, MID = 1, 2
+ASK = ((0, 96), (96, 160), (160, 192), (192, 256))
+ASKV, ASKO = (3,), (3, 0, 1, 2)
+
+SCRATCH = {
+    "Kw": ("sbuf", [128, WD], "int32"), "Vw": ("sbuf", [128, WD], "bfloat16"), "Rw": ("sbuf", [128, WD], "bfloat16"),
+    "Xw": ("sbuf", [128, W], "bfloat16"), "recb": ("sbuf", [128, W], "bfloat16"),
+    "lnb": ("sbuf", [128, W], "float32"), "r24": ("sbuf", [128, W], "bfloat16"),
+    "T0": ("sbuf", [128, 256], "int32"), "T0h": ("sbuf", [128, 256], "float16"), "SLd": ("sbuf", [128, 512], "float16"),
+    "SL": ("sbuf", [128, 256], "float32"),
+    "ones": ("sbuf", [128, 256], "bfloat16"), "L16": ("sbuf", [128, 128], "bfloat16"), "R16b": ("sbuf", [128, 256], "bfloat16"),
+    "R16j": ("sbuf", [128, 256], "bfloat16"), "L8": ("sbuf", [128, 128], "bfloat16"), "Z8": ("sbuf", [128, 144], "bfloat16"),
+    "G88": ("sbuf", [128, 8], "bfloat16"), "Ib": ("sbuf", [128, 128], "bfloat16"), "I16": ("sbuf", [128, 128], "float16"),
+    "E": ("sbuf", [128, 256], "bfloat16"), "BOb": ("sbuf", [128, 128], "bfloat16"), "BO16": ("sbuf", [128, 128], "float16"),
+    "TRb": ("sbuf", [128, 128], "bfloat16"), "TR16": ("sbuf", [128, 128], "float16"), "Zw": ("sbuf", [128, 144], "bfloat16"),
+    "Gs": ("sbuf", [128, 8], "bfloat16"), "G16": ("sbuf", [128, 8], "float16"), "Cm": ("sbuf", [128, 256], "bfloat16"),
+    "Dm": ("sbuf", [128, 256], "bfloat16"), "NDH": ("sbuf", [128, 256], "float32"), "DT": ("sbuf", [128, 1024], "bfloat16"), "DTH": ("sbuf", [128, 1280], "float32"),
+    "D11": ("sbuf", [128, 256], "bfloat16"), "D12": ("sbuf", [128, 256], "bfloat16"),
+    "Dr": ("sbuf", [128, 2048], "float16"), "ND": ("sbuf", [128, 512], "float16"), "LT": ("sbuf", [128, 512], "float16"),
+    "nE": ("sbuf", [128, 16], "float32"), "negE": ("sbuf", [128, 16], "float32"),
+    "seg": ("sbuf", [128, 1024], "bfloat16"),
+    "RL1": ("sbuf", [128, 16], "uint16"), "RL2": ("sbuf", [128, 16], "uint16"),
+    "RL3": ("sbuf", [128, 16], "uint16"), "i1": ("sbuf", [128, 16], "int32"), "i2": ("sbuf", [128, 16], "int32"),
+    "i3": ("sbuf", [128, 16], "int32"), "pm": ("sbuf", [128, 16], "int32"), "pmf": ("sbuf", [128, 16], "float32"),
+    "dq": ("sbuf", [128, 16], "float32"), "dum": ("sbuf", [128, 16], "float32"), "basec": ("sbuf", [128, 1], "float32"),
+    "m16": ("sbuf", [128, 16], "bfloat16"), "mk4": ("sbuf", [128, 16], "float32"),
+    "offs": ("sbuf", [128, 16], "uint16"), "yo": ("sbuf", [128, 2], "int32"),
+    "ca": ("sbuf", [128, 17], "float32"), "cb": ("sbuf", [128, 17], "float32"), "c1": ("sbuf", [128, 16], "float32"),
+    "cE": ("sbuf", [128, 256], "float16"), "crow": ("sbuf", [128, 512], "float16"),
+    "kc": ("sbuf", [128, 256], "uint16"), "kcq": ("sbuf", [128, 256], "uint16"), "kc16": ("sbuf", [128, 256], "float16"),
+    "XC": ("sbuf", [128, 256], "bfloat16"), "XCr": ("sbuf", [128, 4096], "bfloat16"), "VC": ("sbuf", [128, 256], "bfloat16"),
+    "Vg": ("sbuf", [128, 4096], "bfloat16"), "Vq": ("sbuf", [128, 4096], "bfloat16"), "Dx": ("sbuf", [128, 4096], "bfloat16"),
+    "EQ": ("sbuf", [128, 2176], "bfloat16"), "UU": ("sbuf", [128, 768], "bfloat16"), "nK": ("sbuf", [128, 256], "float32"),
+    "nR": ("sbuf", [128, 256], "bfloat16"),
+    "y": ("sbuf", [128, 256], "float32"), "eqn": ("sbuf", [128, 256], "bfloat16"), "neq": ("sbuf", [128, 256], "bfloat16"),
+    "ek": ("sbuf", [128, 256], "float32"), "s2": ("sbuf", [128, 256], "float32"), "Bx": ("sbuf", [128, 256], "float16"),
+    "Bf": ("sbuf", [128, 48], "float32"), "sm": ("sbuf", [128, 256], "float32"), "gq": ("sbuf", [128, 16], "float32"),
+    "wi": ("sbuf", [128, 16], "int32"), "pp": ("sbuf", [128, 16], "int32"), "nirep": ("sbuf", [128, 128], "bfloat16"),
+    "NT": ("sbuf", [128, 17], "float32"), "mv": ("sbuf", [128, 17], "float32"), "nw": ("sbuf", [128, 16], "float32"),
+    "msk": ("sbuf", [128, 256], "float16"), "ltm": ("sbuf", [128, 256], "float16"), "SLz": ("sbuf", [128, 256], "float16"),
+    "nm": ("sbuf", [128, 256], "float16"), "ysb": ("sbuf", [128, 256], "float32"),
+}
+for _t in range(NR):
+    SCRATCH["cu%d" % _t] = ("sbuf", [128, 16], "uint16")
+    SCRATCH["rcv%d" % _t] = ("sbuf", [128, 16], "uint16")
+    SCRATCH["rep%d" % _t] = ("sbuf", [128, 256], "bfloat16")
+    SCRATCH["rrv%d" % _t] = ("sbuf", [128, 256], "bfloat16")
+    SCRATCH["scl%d" % _t] = ("sbuf", [128, 16], "uint16")
+for _k in range(8):
+    SCRATCH["P%d" % _k] = ("psum", [128, 512], "float32")
+SEMAPHORES = ["v", "s", "t", "g", "dsl", "dk", "dr", "dx", "loc", "dout"] + ["rl%d" % t for t in range(NR)] + ["rr%d" % t for t in range(NR)]
+
+
+def rank_program(g, core, T, topo):
+    rank = T.rank_of(core)
+    if rank is None:
+        return
+    A, F = AluOpType, ActivationFunctionType
+    queues = {"v": g.vector, "s": g.scalar, "t": g.tensor, "g": g, "y": g.sync}
+    cnt = {}
+    seen = {q: {} for q in queues}
+    snap = {}
+    lastw, readers, bank = {}, {}, {}
+
+    def wait(q, tok):
+        sem, val = tok
+        if seen[q].get(sem, 0) >= val:
+            return
+        queues[q].wait_ge(T.sem[sem], val)
+        seen[q][sem] = val
+        for s, x in snap.get(tok, {}).items():
+            if seen[q].get(s, 0) < x:
+                seen[q][s] = x
+
+    def deps(q, r, w, bk):
+        need = {}
+
+        def add(tok):
+            if tok is not None and need.get(tok[0], 0) < tok[1]:
+                need[tok[0]] = tok[1]
+        for k in r:
+            tok = lastw.get(k)
+            if tok is not None and not (q == "t" and tok[0] == "t"):
+                add(tok)
+        for k in w:
+            tok = lastw.get(k)
+            if tok is not None and not (q == "t" and tok[0] == "t"):
+                add(tok)
+            for x, tok in readers.get(k, {}).items():
+                if x != q:
+                    add(tok)
+        for b in bk:
+            for x, tok in bank.get(b, {}).items():
+                if x != q:
+                    add(tok)
+        for s in sorted(need):
+            wait(q, (s, need[s]))
+
+    def note(q, tok, r, w, bk):
+        snap[tok] = dict(seen[q])
+        for k in r:
+            readers.setdefault(k, {})[q] = tok
+        for k in w:
+            lastw[k] = tok
+            readers[k] = {}
+        for b in bk:
+            bank.setdefault(b, {})[q] = tok
+
+    def op(q, fn, r=(), w=(), bk=()):
+        deps(q, r, w, bk)
+        fn(queues[q]).then_inc(T.sem[q], 1)
+        cnt[q] = cnt.get(q, 0) + 1
+        note(q, (q, cnt[q]), r, w, bk)
+
+    def dma(q, sem, out, in_, r=(), w=()):
+        deps(q, r, w, ())
+        queues[q].dma_start(out, in_).then_inc(T.sem[sem], 16)
+        cnt[sem] = cnt.get(sem, 0) + 16
+        for k in w:
+            lastw[k] = (sem, cnt[sem])
+
+    def mm(out, lhsT, rhs, start, stop, r=(), w=(), bk=()):
+        op("t", lambda e: e.matmul(out, lhsT, rhs, start, stop), r, w, bk)
+
+    def cp(q, out, in_, r, w, bk=()):
+        if q == "s":
+            op("s", lambda e: e.activation(out, in_, F.Copy), r, w, bk)
+        else:
+            op("v", lambda e: e.tensor_copy(out, in_), r, w, bk)
+
+    def tt(out, a, b, o, r, w, bk=()):
+        op("v", lambda e: e.tensor_tensor(out, a, b, o), r, w, bk)
+
+    def ts(out, a, s1, s2, o0, o1, r, w, bk=()):
+        if o1 is None:
+            op("v", lambda e: e.tensor_scalar(out, a, s1, None, o0), r, w, bk)
+        else:
+            op("v", lambda e: e.tensor_scalar(out, a, s1, s2, o0, o1), r, w, bk)
+
+    def scan(out, a, b, o0, o1, r, w, bk=()):
+        op("v", lambda e: e.tensor_tensor_scan(out, a, b, 0.0, o0, o1), r, w, bk)
+
+    def act(out, in_, f, r, w, bk=(), bias=0.0, scale=1.0):
+        op("s", lambda e: e.activation(out, in_, f, bias=bias, scale=scale), r, w, bk)
+
+    def fill(ap, val, w):
+        op("v", lambda e: e.memset(ap, val), (), w)
+
+    def sel(out, in_, pat, o, base, cm, r, w):
+        op("g", lambda e: e.affine_select(out, in_, pat, o, 0.0, base, cm), r, w)
+
+    def send(out, in_, rsem, dst, r):
+        deps("g", r, (), ())
+        eng = topo.engines(core, dst)[:8]
+        rid, pid = topo.addr(dst, core)
+        g.remote_dma(out, in_, T.sem[rsem], T.sem.loc, pid, rid, sum(1 << e for e in eng))
+        cnt["loc"] = cnt.get("loc", 0) + len(eng)
+
+    for k in range(16):
+        gg, h = k // 2, k % 2
+        dma("y" if h == 0 else "s", "dsl", T.T0[:, 128 * h + 16 * gg:128 * h + 16 * gg + 16],
+            T.slips[16 * gg + 8 * h:16 * gg + 8 * h + 8, :], w=("T0_%d" % k,))
+    dma("y", "dr", T.recb[:], T.rec[:, :], w=("recb",))
+    dma("y", "dk", T.Kw[:, 0:W], T.kin[:, :], w=("Kw",))
+    dma("y", "dx", T.Xw[:], T.wealth[:, :], w=("Xw",))
+
+    fill(T.ones[:], 1.0, ("ones",))
+    sel(T.Ib[:], T.ones[:, 0:128], [[-1, 128]], A.is_equal, 0, 1, ("ones",), ("Ib",))
+    sel(T.L16[0:16, :], T.ones[0:16, 0:128], [[0, 8], [1, 16]], A.is_equal, 0, -1, ("ones",), ("L16",))
+    sel(T.R16j[0:16, :], T.ones[0:16, :], [[0, 16], [1, 16]], A.is_equal, 0, -1, ("ones",), ("R16j",))
+    op("g", lambda e: e.iota(T.i1[:], [[0, 16]], 0, 1), (), ("i1",))
+    sel(T.L8[0:8, :], T.ones[0:8, 0:128], [[1, 8], [0, 16]], A.is_equal, 0, -1, ("ones",), ("L8",))
+    op("g", lambda e: e.iota(T.i2[:], [[1, 16]], 0, 0), (), ("i2",))
+    sel(T.R16b[0:16, :], T.ones[0:16, :], [[1, 16], [0, 16]], A.is_equal, 0, -1, ("ones",), ("R16b",))
+    sel(T.Z8[0:8, :], T.ones[0:8, 0:144], [[1, 144]], A.is_equal, -15, -16, ("ones",), ("Z8",))
+    sel(T.G88[0:8, :], T.ones[0:8, 0:8], [[1, 8]], A.is_equal, 0, -1, ("ones",), ("G88",))
+    op("g", lambda e: e.iota(T.i3[:], [[16, 16]], 15, 0), (), ("i3",))
+    op("g", lambda e: e.iota(T.dq[:], [[16, 16]], W, 0, allow_small_or_imprecise_dtypes=True), (), ("dq",))
+    op("g", lambda e: e.iota(T.Cm[:], [[0, 16], [-1, 16]], 15, 0, allow_small_or_imprecise_dtypes=True), (), ("Cm",))
+
+    fill(T.seg[:], 1.0, ("seg",))
+    fill(T.seg[:, 0:1024:16], 0.0, ("seg",))
+    fill(T.m16[:], -16.0, ("m16",))
+    fill(T.mk4[:], 4096.0, ("mk4",))
+    fill(T.NT[:], 1.0, ("NT",))
+    fill(T.mv[:], 0.0, ("mv",))
+    fill(T.ca[:], 0.0, ("ca",))
+    fill(T.cb[:], 0.0, ("cb",))
+    ts(T.LT[:, 0:256], T.ones[:], 0.0, None, A.mult, None, ("ones",), ("LT",))
+    ts(T.LT[:, 256:512], T.ones[:], 0.0, None, A.mult, None, ("ones",), ("LT",))
+
+    cp("v", T.I16[:], T.Ib[:], ("Ib",), ("I16",))
+    mm(T.P0[:, 0:256], T.L16[0:16, :], T.R16j[0:16, :], True, True, ("L16", "R16j"), ("pE",), ("P0",))
+    cp("v", T.E[:], T.P0[:, 0:256], ("pE",), ("E",), ("P0",))
+    for j in range(16):
+        r = 5 * j % 16
+        ts(T.Dr[:, 128 * r:128 * r + 128], T.I16[:], T.E[:, j:j + 1], None, A.mult, None, ("I16", "E"), ("Dr",))
+    cp("v", T.T0h[:], T.T0[:], tuple("T0_%d" % k for k in range(16)), ("T0h",))
+    for h in range(2):
+        mm(T.P2[:, 128 * h:128 * h + 128], T.T0h[:, 128 * h:128 * h + 128], T.I16[:], True, True, ("T0h", "I16"), ("pT0",), ("P2",))
+    for h in range(2):
+        cp("v", T.SLd[:, 256 * h:256 * h + 256], T.P2[:, 0:256], ("pT0",), ("SLd%d" % h,), ("P2",))
+    for r in range(16):
+        mm(T.P3[:, 0:16], T.Dr[:, 128 * r:128 * r + 128], T.SLd[:, 16 * r:16 * r + 16], r == 0, r == 15, ("Dr", "SLd0"), ("pc0",), ("P3",))
+    cp("v", T.cu0[:], T.P3[:, 0:16], ("pc0",), ("cu0",), ("P3",))
+    send(T.rcv0[:], T.cu0[:], "rl0", T.cores[(rank + 1) % 6], ("cu0",))
+    cp("v", T.ca[:, 1:17], T.P3[:, 0:16], ("pc0",), ("ca",), ("P3",))
+    act(T.Vw[:, 0:W], T.recb[:], F.Exp, ("recb",), ("Vw",), scale=6.0 * math.log(2.0))
+    mm(T.P1[:, 0:128], T.L8[0:8, :], T.L8[0:8, :], True, True, ("L8",), ("pB",), ("P1",))
+    mm(T.P1[:, 128:272], T.L8[0:8, :], T.Z8[0:8, :], True, True, ("L8", "Z8"), ("pB",), ("P1",))
+    mm(T.P1[:, 272:280], T.L8[0:8, :], T.G88[0:8, :], True, True, ("L8", "G88"), ("pB",), ("P1",))
+    mm(T.P0[:, 256:512], T.L16[0:16, :], T.R16b[0:16, :], True, True, ("L16", "R16b"), ("pD",), ("P0",))
+    for r in range(16):
+        mm(T.P5[:, 0:256], T.Dr[:, 128 * r:128 * r + 128], T.SLd[:, 16 * r:16 * r + 256], r == 0, r == 15, ("Dr", "SLd0", "SLd1"), ("pSL",), ("P5",))
+
+    def setup_vector():
+        ts(T.pm[:], T.i1[:], 15, None, A.bitwise_and, None, ("i1",), ("pm",))
+        cp("v", T.RL1[:], T.i2[:], ("i2",), ("RL1",))
+        cp("v", T.BO16[:], T.P1[:, 0:128], ("pB",), ("BO16",), ("P1",))
+        cp("v", T.BOb[:], T.P1[:, 0:128], ("pB",), ("BOb",), ("P1",))
+        sel(T.TRb[:], T.BOb[:], [[-1, 128]], A.is_gt, 0, 1, ("BOb",), ("TRb",))
+        cp("v", T.RL3[:], T.pm[:], ("pm",), ("RL3",))
+        cp("v", T.pmf[:], T.pm[:], ("pm",), ("pmf",))
+        cp("v", T.RL2[:], T.i3[:], ("i3",), ("RL2",))
+        ts(T.Gs[:], T.P1[:, 272:280], 16.0, None, A.mult, None, ("pB",), ("Gs",), ("P1",))
+        cp("v", T.G16[:], T.P1[:, 272:280], ("pB",), ("G16",), ("P1",))
+        cp("v", T.Zw[:], T.P1[:, 128:272], ("pB",), ("Zw",), ("P1",))
+        cp("v", T.Dm[:], T.P0[:, 256:512], ("pD",), ("Dm",), ("P0",))
+        ts(T.NDH[:], T.P0[:, 256:512], -1e29, 1e29, A.mult, A.add, ("pD",), ("NDH",), ("P0",))
+        ts(T.dum[:], T.dq[:], T.pmf[:, 0:1], None, A.add, None, ("dq", "pmf"), ("dum",))
+        ts(T.basec[:], T.pmf[:, 0:1], 2048.0, None, A.add, None, ("pmf",), ("basec",))
+        ts(T.nE[:], T.E[:, 0:16], -1.0, 1.0, A.mult, A.add, ("E",), ("nE",))
+        ts(T.negE[:], T.E[:, 0:16], -1.0, None, A.mult, None, ("E",), ("negE",))
+        cp("v", T.offs[:, 0:1], T.pm[:, 0:1], ("pm",), ("off0",))
+        for t in range(4):
+            cp("v", T.LT[:, 128 * t + t:128 * t + 128:16], T.BO16[:, t:128:16], ("BO16", "LT"), ("LTx",))
+            ts(T.ND[:, 128 * t:128 * t + 128], T.I16[:], T.nE[:, t:t + 1], None, A.mult, None, ("I16", "nE"), ("ND",))
+        cp("v", T.TR16[:], T.TRb[:], ("TRb",), ("TR16",))
+
+    def bar_of_own_office(t):
+        act(T.DTH[:, 256 * t:256 * t + 256], T.NDH[:], F.Copy, ("NDH",), ("DTH%d" % t,), bias=2.0 ** (6 * (8 + t - 3)))
+
+    def setup_scalar():
+        for t in range(4):
+            act(T.DT[:, 256 * t:256 * t + 256], T.Dm[:], F.Copy, ("Dm",), ("DT%d" % t,), scale=2.0 ** (6 * (8 + t)))
+        for t, n in ((11, "D11"), (12, "D12")):
+            act(T[n][:], T.Dm[:], F.Copy, ("Dm",), (n,), scale=float(t))
+
+    for t in range(NR):
+        last = t == NR - 1
+        cn = "ca" if t % 2 == 0 else "cb"
+        C = T[cn]
+        c, cprev = C[:, 1:17], C[:, 0:16]
+        cu, rcv, scl = T["cu%d" % t], T["rcv%d" % t], T["scl%d" % t]
+        cuk, rcvk, sclk = "cu%d" % t, "rcv%d" % t, "scl%d" % t
+        p = T.cores[(rank - 1 - t % 5) % 6]
+        rep, repk = T["rep%d" % t], "rep%d" % t
+        lastw[rcvk] = ("rl%d" % t, 8)
+        lastw["rrv%d" % t] = ("rr%d" % t, 8)
+        KB = ("P2", "P7")
+        eqpos = [256]
+        for b in range(15):
+            eqpos.append(eqpos[b] + 16 * (15 - b))
+
+        def ask(k):
+            a, b = ASK[k]
+            cp("v" if k in ASKV else "s", T.Vq[:, 16 * a:16 * b], T.Vw[:, 0:W].indirect(T.kcq[:, a:b]), ("Vw", "kcq"), ("Vq%d" % k,))
+
+        def ask_mm(k):
+            a, b = ASK[k]
+            for m in range(16):
+                mm(T.P1[:, a:b], T.Ib[:], T.Vq[:, 16 * a + m:16 * b:16], m == 0, m == 15, ("Ib", "Vq%d" % k), ("pA%d" % k,), ("P1",))
+
+        def own(k):
+            a, b = OWN[k]
+            cp("s", T.Vg[:, 16 * a:16 * b], T.Vw[:, 0:W].indirect(T.kc[:, a:b]), ("Vw", "kc"), ("Vg%d" % k,))
+
+        def own_mm(k):
+            a, b = OWN[k]
+            for m in range(16):
+                mm(T.P0[:, a:b], T.Ib[:], T.Vg[:, 16 * a + m:16 * b:16], False, False, ("Ib", "Vg%d" % k), ("pS",), ("P0",))
+
+        def wealth(h):
+            tt(T.Dx[:, 2048 * h:2048 * h + 2048], T.Xw[:].indirect(T.kc[:, 128 * h:128 * h + 128]), T.XCr[:, 2048 * h:2048 * h + 2048],
+               A.max, ("Xw", "kc") + tuple("XCr%d" % m for m in range(16)), ("Dx%d" % h,))
+
+        def key(h, m=None):
+            if m is None:
+                return T.P2[:, 0:128] if h == 0 else T.P7[:, 0:128]
+            return T.P2[:, m:128:16] if h == 0 else T.P7[:, m:128:16]
+
+        def score_mm(h):
+            mm(key(h), T.Ib[:], T.Cm[:, 128 * h:128 * h + 128], True, False, ("Ib", "Cm"), ("pKey%d" % h,), (KB[h],))
+            for m in range(16):
+                mm(key(h, m), T.Dx[:, 2048 * h + m:2048 * h + 2048:16], T.Gs[:], False, m == 15,
+                   ("Dx%d" % h, "Gs"), ("pKey%d" % h,), (KB[h],))
+
+        def eq_v():
+            for b in range(15):
+                ts(T.EQ[:, eqpos[b]:eqpos[b + 1]], T.crow[:, 16 * b + 16:256], T.c1[:, b:b + 1], None, A.is_equal, None, ("crow", "c1"), ("EQ%d" % b,))
+
+        def eq_mm():
+            for b in range(15):
+                mm(T.P5[:, 16 * b + 16:256], T.BOb[:], T.EQ[:, eqpos[b]:eqpos[b + 1]], False, b == 14, ("BOb", "EQ%d" % b), ("pcnt",), ("P5",))
+
+        def best_a(h):
+            a, b = 128 * h, 128 * h + 128
+            scan(T.y[:, a:b], T.seg[:, 0:128], key(h), A.mult, A.max, ("seg", "pKey%d" % h), ("y%d" % h,), (KB[h],))
+            tt(T.eqn[:, a:b], key(h), T.y[:, a:b], A.is_equal, ("pKey%d" % h, "y%d" % h), ("eqn%d" % h,), (KB[h],))
+            tt(T.neq[:, a:b], key(h), T.y[:, a:b], A.not_equal, ("pKey%d" % h, "y%d" % h), ("neq%d" % h,), (KB[h],))
+
+        def best_b(h):
+            a, b = 128 * h, 128 * h + 128
+            tt(T.ek[:, a:b], T.P3[:, a:b], T.eqn[:, a:b], A.mult, ("pkc", "eqn%d" % h), ("ek%d" % h,), ("P3",))
+            scan(T.s2[:, a:b], T.neq[:, a:b], T.ek[:, a:b], A.mult, A.add, ("neq%d" % h, "ek%d" % h), ("s2_%d" % h,))
+
+        def best_c(h):
+            a, b = 128 * h, 128 * h + 128
+            tt(T.Bx[:, a:b], T.s2[:, a:b].indirect(T.RL2[:, 0:8]), T.E[:, a:b], A.mult, ("s2_%d" % h, "RL2", "E"), ("Bx%d" % h,))
+
+        def best_mm(h):
+            mm(T.P4[:, 8 * h:8 * h + 8], T.Bx[:, 128 * h:128 * h + 128], T.G16[:], True, True, ("Bx%d" % h, "G16"), ("pBest",), ("P4",))
+
+        if t == 0:
+            setup_vector()
+        cp("v", T.kc[:], T.Kw[:, 0:W].indirect(cu[:]), ("Kw", cuk), ("kc",))
+        if t > 0:
+            tt(T.Vw[:].indirect(T["scl%d" % (t - 1)][:]), T.VC[:], T.DT[:, 256 * (t - 1):256 * t], A.add, ("VC", "DT%d" % (t - 1), "scl%d" % (t - 1)), ("Vw",))
+        if last:
+            cp("v", T.SL[:].indirect(T.offs[:, 2 * t:2 * t + 1]), T.mk4[:], ("mk4", "off%d" % t, cn, cuk), ("SL",))
+            for h in range(2):
+                cp("v", T.SLd[:, 256 * h:256 * h + 256], T.SL[:], ("SL",), ("SLd%d" % h,))
+            for r in range(16):
+                x = 16 * ((16 - r) % 16)
+                mm(T.P6[:, 256:512], T.Dr[:, 128 * r:128 * r + 128], T.SLd[:, x:x + 256], r == 0, r == 15, ("Dr", "SLd0", "SLd1"), ("pSU",), ("P6",))
+        cp("s", T.XC[:], T.Xw[:].indirect(cu[:]), ("Xw", cuk), ("XC",))
+        for m in range(NS):
+            cp("s", T.XCr[:, m:4096:16], T.XC[:], ("XC",), ("XCr%d" % m,))
+        cp("s", T.VC[:], T.Vw[:, 0:W].indirect(cu[:]), ("Vw", cuk), ("VC",))
+        ts(T.c1[:], c, 1.0, None, A.add, None, (cn,), ("c1",))
+        cp("v", T.kc16[:], T.kc[:], ("kc",), ("kc16",))
+        tt(T.cE[:], T.c1[:].indirect(T.RL1[:]), T.E[:], A.mult, ("c1", "RL1", "E"), ("cE",))
+        for m in range(NS, 16):
+            cp("v", T.XCr[:, m:4096:16], T.XC[:], ("XC",), ("XCr%d" % m,))
+        cp("v", T.kcq[:], T.Kw[:, 0:W].indirect(rcv[:]), ("Kw", rcvk), ("kcq",))
+        for k in range(PRE):
+            own(k)
+        for k in ASKO:
+            ask(k)
+        mm(T.P4[:, 0:256], T.BO16[:], T.cE[:], True, True, ("BO16", "cE"), ("pcrow",), ("P4",))
+        mm(T.P4[:, 256:512], T.TR16[:], T.cE[:], True, True, ("TR16", "cE"), ("pcrow",), ("P4",))
+        for h in range(2):
+            mm(T.P3[:, 128 * h:128 * h + 128], T.kc16[:, 128 * h:128 * h + 128], T.I16[:], True, True, ("kc16", "I16"), ("pkc",), ("P3",))
+        if not last:
+            mm(T.P3[:, 256:512], T.ND[:, 128 * t:128 * t + 128], T.kc16[:], True, False, ("ND", "kc16"), ("pnK",), ("P3",))
+            mm(T.P3[:, 256:512:2], T.LT[:, 128 * t:128 * t + 128], T.cE[:, 1:256:2], False, False, ("LTx", "cE"), ("pnK",), ("P3",))
+            mm(T.P3[:, 257:512:2], T.LT[:, 128 * t:128 * t + 128], T.cE[:, 0:256:2], False, True, ("LTx", "cE"), ("pnK",), ("P3",))
+        if last:
+            ts(T.Rw[:, 0:W], T.r24[:], 16.0, None, A.subtract, None, ("r24",), ("Rw",))
+            tt(T.nR[:], T.Rw[:, 0:W].indirect(T.cu3[:]), T.D11[:], A.max, ("Rw", "cu3", "D11"), ("nR",))
+
+        mm(T.P0[:, 0:256], T.Ib[:], T.VC[:], True, False, ("Ib", "VC"), ("pS",), ("P0",))
+        for k in range(PRE):
+            own_mm(k)
+        for k in ASKO:
+            ask_mm(k)
+        for k in range(PRE, MID):
+            own(k)
+        cp("s", rep[:], T.P1[:, 0:256], tuple("pA%d" % k for k in ASKO), (repk,), ("P1",))
+        send(T["rrv%d" % t][:], rep[:], "rr%d" % t, p, (repk,))
+        wealth(0)
+        cp("v", T.crow[:], T.P4[:], ("pcrow",), ("crow",), ("P4",))
+        tt(T.EQ[:, 0:256], T.c1[:].indirect(T.RL1[:]), T.crow[:, 256:512], A.is_equal, ("c1", "RL1", "crow"), ("EQin",))
+        eq_v()
+        score_mm(0)
+        if t == 0:
+            cp("v", T.SL[:], T.P5[:, 0:256], ("pSL",), ("SL",), ("P5",))
+        mm(T.P5[:, 0:256], T.BOb[:], T.EQ[:, 0:256], True, False, ("BOb", "EQin"), ("pcnt",), ("P5",))
+        eq_mm()
+        for k in range(PRE, MID):
+            own_mm(k)
+        wealth(1)
+        own(MID)
+        own_mm(MID)
+        score_mm(1)
+        for k in range(MID + 1, len(OWN)):
+            own(k)
+        act(T.UU[:, 512:768], T.P5[:, 0:256], F.Copy, ("pcnt",), ("UUn",), ("P5",), scale=4.0)
+        if not last:
+            bar_of_own_office(t + 1)
+        if t == 0:
+            bar_of_own_office(0)
+        best_a(0)
+        best_b(0)
+        best_c(0)
+        for k in range(MID + 1, len(OWN)):
+            own_mm(k)
+        if t == 3:
+            act(T.lnb[:], T.Vw[:, 0:W], F.Ln, ("Vw",), ("lnb",), scale=2.0 ** -48)
+            act(T.r24[:], T.lnb[:], F.Copy, ("lnb",), ("r24",), scale=1.0 / (6.0 * math.log(2.0)), bias=24.0)
+        if last:
+            cp("v", T.Rw[:].indirect(T.scl3[:]), T.nR[:], ("nR", "scl3", "Rw"), ("Rw",))
+            tt(T.nR[:], T.Rw[:, 0:W].indirect(cu[:]), T.D12[:], A.max, ("Rw", cuk, "D12"), ("nR",))
+            ts(T.msk[:], T.P6[:, 256:512], 4096.0, None, A.is_ge, None, ("pSU",), ("msk",), ("P6",))
+            ts(T.ltm[:], T.P6[:, 256:512], 4096.0, None, A.is_lt, None, ("pSU",), ("ltm",), ("P6",))
+            tt(T.SLz[:], T.P6[:, 256:512], T.ltm[:], A.mult, ("pSU", "ltm"), ("SLz",), ("P6",))
+        best_a(1)
+        mm(T.P0[:, 0:256], T.Ib[:], T["rrv%d" % t][:], False, True, ("Ib", "rrv%d" % t), ("pS",), ("P0",))
+        ts(T.UU[:, 0:256], T.P0[:, 0:256], 2.0 ** (6 * (8 + t - 2)), None, A.is_ge, None, ("pS",), ("UU2",), ("P0",))
+        tt(T.UU[:, 256:512], T.P0[:, 0:256], T.DTH[:, 256 * t:256 * t + 256], A.is_ge, ("pS", "DTH%d" % t), ("UU3",), ("P0",))
+        for j in range(16):
+            mm(T.P6[:, 0:48], T.Zw[:, 15 - j:143 - j], T.UU[:, j:768:16], j == 0, j == 15, ("Zw", "UU2", "UU3", "UUn"), ("pF",), ("P6",))
+        best_b(1)
+        if not last:
+            act(T.nK[:], T.P3[:, 256:512], F.Identity, ("pnK", "negE"), ("nK",), ("P3",), bias=T.negE[:, t:t + 1])
+        if t == 0:
+            setup_scalar()
+        best_c(1)
+        best_mm(0)
+        best_mm(1)
+        cp("v", T.Bf[:], T.P6[:, 0:48], ("pF",), ("Bf",), ("P6",))
+        sm = [T.sm[:, 16 * k:16 * k + 16] for k in range(16)]
+        tt(T.wi[:], T.Bf[:, 0:16], T.Bf[:, 32:48], A.add, ("Bf",), ("wi",))
+        ts(sm[0], T.Bf[:, 16:32], 8.0, None, A.mult, None, ("Bf",), ("d8",))
+        tt(T.gq[:], T.wi[:], sm[0], A.max, ("wi", "d8"), ("gq",))
+        ts(T.pp[:], T.wi[:], 1, None, A.bitwise_and, None, ("wi",), ("pp",))
+        ts(sm[1], T.wi[:], 12.0, None, A.is_lt, None, ("wi",), ("lt12",))
+        if not last:
+            ts(T.nirep[:], T.gq[:].indirect(T.RL3[:, 0:8]), 8.0, None, A.is_ge, None, ("gq", "RL3"), ("nirep",))
+            mm(T.P6[:, 64:65], T.nirep[:], T.m16[:, 0:1], True, True, ("nirep", "m16"), ("pOff",), ("P6",))
+        ts(sm[2], T.gq[:], 8.0, None, A.is_ge, None, ("gq",), ("ni",))
+        ts(sm[3], T.wi[:], 64.0, None, A.is_lt, None, ("wi",), ("lt64",))
+        tt(sm[4], T.pp[:], sm[1], A.mult, ("pp", "lt12"), ("m1",))
+        tt(sm[6], sm[2], T.dum[:], A.mult, ("ni", "dum"), ("nd",))
+        tt(sm[7], sm[3], sm[1], A.subtract, ("lt64", "lt12"), ("tb",))
+        tt(sm[5], sm[4], sm[2], A.mult, ("m1", "ni"), ("m2",))
+        tt(sm[8], sm[6], c, A.max, ("nd", cn), ("lst",))
+        tt(T.NT[:, 0:16], sm[2], sm[7], A.subtract, ("ni", "tb", "NT"), ("NT",))
+        cp("v", scl[:], sm[8], ("lst",), (sclk,))
+        tt(T.mv[:, 1:17], sm[5], T.NT[:, 1:17], A.is_gt, ("m2", "NT", "mv"), ("mv",))
+        if last:
+            cp("v", T.Rw[:].indirect(scl[:]), T.nR[:], ("nR", sclk, "Rw"), ("Rw",))
+            dma("y", "dout", T.yr[:, :], T.Rw[:, 0:W], r=("Rw",))
+        else:
+            ts(T.yo[:, 0:1], T.P6[:, 64:65], T.basec[:, 0:1], float(16 * (t + 1)), A.add, A.add, ("pOff", "basec"), ("yo",), ("P6",))
+        tt(sm[9], T.NT[:, 0:16], T.mv[:, 1:17], A.is_gt, ("NT", "mv"), ("NM",))
+        tt(sm[11], T.mv[:, 0:16], cprev, A.mult, ("mv", cn), ("R2",))
+        if not last:
+            ts(T.yo[:, 1:2], T.yo[:, 0:1], 255, None, A.bitwise_and, None, ("yo",), ("ya",))
+        tt(sm[10], sm[9], c, A.mult, ("NM", cn), ("R1",))
+        tt(sm[12], sm[9], T.mv[:, 0:16], A.add, ("NM", "mv"), ("q1",))
+        tt(sm[13], sm[10], sm[11], A.add, ("R1", "R2"), ("R12",))
+        ts(sm[14], sm[12], -1.0, 1.0, A.mult, A.add, ("q1",), ("Bm",))
+        if not last:
+            cp("v", T.offs[:, 2 * t + 2:2 * t + 3], T.yo[:, 1:2], ("ya",), ("off%d" % (t + 1),))
+        tt(sm[15], T.P4[:, 0:16], sm[14], A.mult, ("pBest", "Bm"), ("xb",), ("P4",))
+        tt(T.nw[:], sm[15], sm[13], A.add, ("xb", "R12"), ("nw",))
+        if not last:
+            cp("v", T.SL[:].indirect(T.offs[:, 2 * t:2 * t + 1]), T.nw[:], ("nw", "off%d" % t, "SL"), ("SL",))
+            n = t + 1
+            nn = "cb" if t % 2 == 0 else "ca"
+            cp("v", T["cu%d" % n][:], T.SL[:].indirect(T.offs[:, 2 * n:2 * n + 1]), ("SL", "off%d" % n), ("cu%d" % n,))
+            send(T["rcv%d" % n][:], T["cu%d" % n][:], "rl%d" % n, T.cores[(rank + 1 + n % 5) % 6], ("cu%d" % n,))
+            cp("v", T[nn][:, 1:17], T.SL[:].indirect(T.offs[:, 2 * n:2 * n + 1]), ("SL", "off%d" % n, nn), (nn,))
+            cp("v", T.Kw[:].indirect(scl[:]), T.nK[:], ("nK", sclk, "Kw"), ("Kw",))
+        else:
+            tt(T.nm[:], T.nw[:].indirect(T.RL3[:]), T.msk[:], A.mult, ("nw", "RL3", "msk"), ("nm",))
+            for h in range(2):
+                a, b = 256 + 128 * h, 384 + 128 * h
+                mm(T.P4[:, a:b], T.SLz[:, 128 * h:128 * h + 128], T.I16[:], True, False, ("SLz", "I16"), ("pY",), ("P4",))
+                mm(T.P4[:, a:b], T.nm[:, 128 * h:128 * h + 128], T.I16[:], False, True, ("nm", "I16"), ("pY",), ("P4",))
+            cp("v", T.ysb[:], T.P4[:, 256:512], ("pY",), ("ysb",), ("P4",))
+            for k in range(16):
+                gg, h = k // 2, k % 2
+                dma("y" if h == 0 else "s", "dout", T.ys[16 * gg + 8 * h:16 * gg + 8 * h + 8, :],
+                    T.ysb[:, 128 * h + 16 * gg:128 * h + 16 * gg + 16], r=("ysb",))
+    for s in ("v", "s", "t", "g", "dsl", "dk", "dr", "dx", "loc", "dout"):
+        wait("g", (s, cnt[s]))
+    for t in range(NR):
+        wait("g", ("rl%d" % t, 8))
+        wait("g", ("rr%d" % t, 8))

@@ -1,61 +1,52 @@
-import numpy as np
 import math
 from concourse.mybir import dt, AluOpType, AxisListType, ActivationFunctionType
 
-W, NR = 1408, 5
-WD = W + 256
-NS = 10
-OWN = ((0, 32), (32, 64), (64, 128), (128, 192), (192, 256))
-PRE, MID = 1, 2
+W, NR, O = 1408, 5, 32
+WT = O + W
+WD = WT + 256
+NG = 7
+OWN = ((0, 48), (48, 128), (128, 208), (208, 256))
+PRE = 1
 ASK = ((0, 96), (96, 160), (160, 192), (192, 256))
 ASKV, ASKO = (3,), (3, 0, 1, 2)
 
+
+def power(r):
+    return math.exp(4.0 * r + 3.0)
+
+
+def sb(dtype, *shape):
+    return ("sbuf", [128] + list(shape), dtype)
+
+
 SCRATCH = {
-    "Kw": ("sbuf", [128, WD], "int32"), "Vw": ("sbuf", [128, WD], "bfloat16"), "Rw": ("sbuf", [128, WD], "bfloat16"),
-    "Xw": ("sbuf", [128, W], "bfloat16"), "recb": ("sbuf", [128, W], "bfloat16"),
-    "lnb": ("sbuf", [128, W], "float32"), "r24": ("sbuf", [128, W], "bfloat16"),
-    "T0": ("sbuf", [128, 256], "int32"), "T0h": ("sbuf", [128, 256], "float16"), "SLd": ("sbuf", [128, 512], "float16"),
-    "SL": ("sbuf", [128, 256], "float32"),
-    "ones": ("sbuf", [128, 256], "bfloat16"), "L16": ("sbuf", [128, 128], "bfloat16"), "R16b": ("sbuf", [128, 256], "bfloat16"),
-    "R16j": ("sbuf", [128, 256], "bfloat16"), "L8": ("sbuf", [128, 128], "bfloat16"), "Z8": ("sbuf", [128, 144], "bfloat16"),
-    "G88": ("sbuf", [128, 8], "bfloat16"), "Ib": ("sbuf", [128, 128], "bfloat16"), "I16": ("sbuf", [128, 128], "float16"),
-    "E": ("sbuf", [128, 256], "bfloat16"), "BOb": ("sbuf", [128, 128], "bfloat16"), "BO16": ("sbuf", [128, 128], "float16"),
-    "TRb": ("sbuf", [128, 128], "bfloat16"), "TR16": ("sbuf", [128, 128], "float16"), "Zw": ("sbuf", [128, 144], "bfloat16"),
-    "Gs": ("sbuf", [128, 8], "bfloat16"), "G16": ("sbuf", [128, 8], "float16"), "Cm": ("sbuf", [128, 256], "bfloat16"),
-    "Dm": ("sbuf", [128, 256], "bfloat16"), "NDH": ("sbuf", [128, 256], "float32"), "DT": ("sbuf", [128, 1024], "bfloat16"), "DTH": ("sbuf", [128, 1280], "float32"),
-    "D11": ("sbuf", [128, 256], "bfloat16"), "D12": ("sbuf", [128, 256], "bfloat16"),
-    "Dr": ("sbuf", [128, 2048], "float16"), "ND": ("sbuf", [128, 512], "float16"), "LT": ("sbuf", [128, 512], "float16"),
-    "nE": ("sbuf", [128, 16], "float32"), "negE": ("sbuf", [128, 16], "float32"),
-    "seg": ("sbuf", [128, 1024], "bfloat16"),
-    "RL1": ("sbuf", [128, 16], "uint16"), "RL2": ("sbuf", [128, 16], "uint16"),
-    "RL3": ("sbuf", [128, 16], "uint16"), "i1": ("sbuf", [128, 16], "int32"), "i2": ("sbuf", [128, 16], "int32"),
-    "i3": ("sbuf", [128, 16], "int32"), "pm": ("sbuf", [128, 16], "int32"), "pmf": ("sbuf", [128, 16], "float32"),
-    "dq": ("sbuf", [128, 16], "float32"), "dum": ("sbuf", [128, 16], "float32"), "basec": ("sbuf", [128, 1], "float32"),
-    "m16": ("sbuf", [128, 16], "bfloat16"), "mk4": ("sbuf", [128, 16], "float32"),
-    "offs": ("sbuf", [128, 16], "uint16"), "yo": ("sbuf", [128, 2], "int32"),
-    "ca": ("sbuf", [128, 17], "float32"), "cb": ("sbuf", [128, 17], "float32"), "c1": ("sbuf", [128, 16], "float32"),
-    "cE": ("sbuf", [128, 256], "float16"), "crow": ("sbuf", [128, 512], "float16"),
-    "kc": ("sbuf", [128, 256], "uint16"), "kcq": ("sbuf", [128, 256], "uint16"), "kc16": ("sbuf", [128, 256], "float16"),
-    "XC": ("sbuf", [128, 256], "bfloat16"), "XCr": ("sbuf", [128, 4096], "bfloat16"), "VC": ("sbuf", [128, 256], "bfloat16"),
-    "Vg": ("sbuf", [128, 4096], "bfloat16"), "Vq": ("sbuf", [128, 4096], "bfloat16"), "Dx": ("sbuf", [128, 4096], "bfloat16"),
-    "EQ": ("sbuf", [128, 2176], "bfloat16"), "UU": ("sbuf", [128, 768], "bfloat16"), "nK": ("sbuf", [128, 256], "float32"),
-    "nR": ("sbuf", [128, 256], "bfloat16"),
-    "y": ("sbuf", [128, 256], "float32"), "eqn": ("sbuf", [128, 256], "bfloat16"), "neq": ("sbuf", [128, 256], "bfloat16"),
-    "ek": ("sbuf", [128, 256], "float32"), "s2": ("sbuf", [128, 256], "float32"), "Bx": ("sbuf", [128, 256], "float16"),
-    "Bf": ("sbuf", [128, 48], "float32"), "sm": ("sbuf", [128, 256], "float32"), "gq": ("sbuf", [128, 16], "float32"),
-    "wi": ("sbuf", [128, 16], "int32"), "pp": ("sbuf", [128, 16], "int32"), "nirep": ("sbuf", [128, 128], "bfloat16"),
-    "NT": ("sbuf", [128, 17], "float32"), "mv": ("sbuf", [128, 17], "float32"), "nw": ("sbuf", [128, 16], "float32"),
-    "msk": ("sbuf", [128, 256], "float16"), "ltm": ("sbuf", [128, 256], "float16"), "SLz": ("sbuf", [128, 256], "float16"),
-    "nm": ("sbuf", [128, 256], "float16"), "ysb": ("sbuf", [128, 256], "float32"),
+    "K0": sb("int32", WT), "Kw": sb("float32", WD), "Vw": sb("float32", WD), "Xw": sb("bfloat16", WT), "Id": sb("float32", WT),
+    "recb": sb("bfloat16", W), "lnb": sb("bfloat16", W), "Rw": sb("bfloat16", WD),
+    "S0": sb("int32", 256), "Sh": sb("float16", 256), "Si": sb("float16", 256), "St": sb("float16", 8, 2, 16), "Su": sb("float16", 8, 2, 16),
+    "SL": sb("float32", 256), "ysb": sb("float32", 256),
+    "pi": sb("int32", 4), "col": sb("float32", 16), "bas": sb("bfloat16", 8), "Rb": sb("float32", 256),
+    "Ib": sb("bfloat16", 4, 2, 16), "Wc": sb("bfloat16", 8, 32), "Wr": sb("bfloat16", 16, 128), "Ax": sb("bfloat16", 4, 4, 2, 16),
+    "E16": sb("float32", 16), "nE": sb("float32", 16), "Dm": sb("bfloat16", 256), "D12": sb("bfloat16", 256), "NDH": sb("float32", 256),
+    "DTH": sb("float32", NR, 256), "Iv": sb("bfloat16", 4, 128), "ND": sb("bfloat16", 4, 128), "LT": sb("bfloat16", 4, 128),
+    "Zw": sb("bfloat16", 144), "Z16": sb("bfloat16", 144), "BO4": sb("bfloat16", 128), "W4": sb("bfloat16", 128),
+    "Cm": sb("bfloat16", 128), "seg": sb("bfloat16", 128), "RL": sb("uint16", 8), "offs": sb("uint16", 16),
+    "kc": sb("uint16", 256), "kcq": sb("uint16", 256), "kc16": sb("float16", 256), "kt": sb("float16", 8, 2, 16), "crow": sb("float16", 256),
+    "XC": sb("bfloat16", 256), "XCr": sb("bfloat16", 4096), "VC": sb("bfloat16", 256),
+    "Vg": sb("bfloat16", 4096), "Vq": sb("bfloat16", 4096), "Dx": sb("bfloat16", 8, 512),
+    "EQ": sb("bfloat16", 16, 256), "cn": sb("bfloat16", 256), "NC": sb("bfloat16", 32), "UU": sb("bfloat16", 512),
+    "nK": sb("float32", 256), "nV": sb("float32", 256), "nR": sb("bfloat16", 256),
+    "y": sb("float32", 256), "eqn": sb("bfloat16", 256), "neq": sb("bfloat16", 256), "ek": sb("float16", 256), "s2": sb("float16", 2, 128),
+    "A0": sb("float32", 32), "A1": sb("float32", 32), "Ao": sb("float32", 32),
+    "B0": sb("float32", 52), "B1": sb("float32", 52), "Bo": sb("float32", 48),
+    "sm": sb("float32", 64), "torn": sb("float32", 17), "fi": sb("int32", 32), "kk": sb("int32", 1), "nirep": sb("bfloat16", 128),
 }
 for _t in range(NR):
-    SCRATCH["cu%d" % _t] = ("sbuf", [128, 16], "uint16")
-    SCRATCH["rcv%d" % _t] = ("sbuf", [128, 16], "uint16")
-    SCRATCH["rep%d" % _t] = ("sbuf", [128, 256], "bfloat16")
-    SCRATCH["rrv%d" % _t] = ("sbuf", [128, 256], "bfloat16")
-    SCRATCH["scl%d" % _t] = ("sbuf", [128, 16], "uint16")
+    for _n in ("cu", "rcv", "scl"):
+        SCRATCH["%s%d" % (_n, _t)] = sb("uint16", 16)
+    for _n in ("rep", "rrv"):
+        SCRATCH["%s%d" % (_n, _t)] = sb("bfloat16", 256)
 for _k in range(8):
-    SCRATCH["P%d" % _k] = ("psum", [128, 512], "float32")
+    SCRATCH["P%d" % _k] = ("psum", [128, 16, 2, 16] if _k == 3 else [128, 512], "float32")
 SEMAPHORES = ["v", "s", "t", "g", "dsl", "dk", "dr", "dx", "loc", "dout"] + ["rl%d" % t for t in range(NR)] + ["rr%d" % t for t in range(NR)]
 
 
@@ -115,373 +106,328 @@ def rank_program(g, core, T, topo):
             bank.setdefault(b, {})[q] = tok
 
     def op(q, fn, r=(), w=(), bk=()):
+        r, w, bk = r.split(), w.split(), bk.split()
         deps(q, r, w, bk)
         fn(queues[q]).then_inc(T.sem[q], 1)
         cnt[q] = cnt.get(q, 0) + 1
         note(q, (q, cnt[q]), r, w, bk)
 
-    def dma(q, sem, out, in_, r=(), w=()):
-        deps(q, r, w, ())
+    def dma(q, sem, out, in_, r="", w=""):
+        deps(q, r.split(), w.split(), ())
         queues[q].dma_start(out, in_).then_inc(T.sem[sem], 16)
         cnt[sem] = cnt.get(sem, 0) + 16
-        for k in w:
+        for k in w.split():
             lastw[k] = (sem, cnt[sem])
 
-    def mm(out, lhsT, rhs, start, stop, r=(), w=(), bk=()):
+    def mm(out, lhsT, rhs, start, stop, r, w, bk):
         op("t", lambda e: e.matmul(out, lhsT, rhs, start, stop), r, w, bk)
 
-    def cp(q, out, in_, r, w, bk=()):
+    def cp(q, out, in_, r, w, bk=""):
         if q == "s":
             op("s", lambda e: e.activation(out, in_, F.Copy), r, w, bk)
+        elif q == "g":
+            op("g", lambda e: e.affine_select(out, in_, [[0, 256]], A.is_gt, 0.0, 1, 0), r, w, bk)
         else:
             op("v", lambda e: e.tensor_copy(out, in_), r, w, bk)
 
-    def tt(out, a, b, o, r, w, bk=()):
+    def tt(out, a, b, o, r, w, bk=""):
         op("v", lambda e: e.tensor_tensor(out, a, b, o), r, w, bk)
 
-    def ts(out, a, s1, s2, o0, o1, r, w, bk=()):
+    def ts(out, a, s1, o0, r, w, bk="", s2=None, o1=None):
         if o1 is None:
             op("v", lambda e: e.tensor_scalar(out, a, s1, None, o0), r, w, bk)
         else:
             op("v", lambda e: e.tensor_scalar(out, a, s1, s2, o0, o1), r, w, bk)
 
-    def scan(out, a, b, o0, o1, r, w, bk=()):
+    def scan(out, a, b, o0, o1, r, w, bk=""):
         op("v", lambda e: e.tensor_tensor_scan(out, a, b, 0.0, o0, o1), r, w, bk)
 
-    def act(out, in_, f, r, w, bk=(), bias=0.0, scale=1.0):
+    def act(out, in_, f, r, w, bk="", bias=0.0, scale=1.0):
         op("s", lambda e: e.activation(out, in_, f, bias=bias, scale=scale), r, w, bk)
 
-    def fill(ap, val, w):
-        op("v", lambda e: e.memset(ap, val), (), w)
+    def scatter(out, in_, r, w):
+        op("s", lambda e: e.activation(out, in_, F.Silu), r, w, "")
 
-    def sel(out, in_, pat, o, base, cm, r, w):
-        op("g", lambda e: e.affine_select(out, in_, pat, o, 0.0, base, cm), r, w)
+    def fill(ap, val, w):
+        op("v", lambda e: e.memset(ap, val), "", w, "")
+
+    def iota(out, pat, base, cm, w):
+        if out.dtype == dt.int32:
+            op("g", lambda e: e.iota(out, pat, base, cm), "", w, "")
+        else:
+            op("g", lambda e: e.iota(out, pat, base, cm, allow_small_or_imprecise_dtypes=True), "", w, "")
+
+    def turn(out, in_, r, w):
+        op("v", lambda e: e.transpose(out, in_), r, w, "")
 
     def send(out, in_, rsem, dst, r):
-        deps("g", r, (), ())
+        deps("g", r.split(), (), ())
         eng = topo.engines(core, dst)[:8]
         rid, pid = topo.addr(dst, core)
         g.remote_dma(out, in_, T.sem[rsem], T.sem.loc, pid, rid, sum(1 << e for e in eng))
         cnt["loc"] = cnt.get("loc", 0) + len(eng)
 
-    for k in range(16):
-        gg, h = k // 2, k % 2
-        dma("y" if h == 0 else "s", "dsl", T.T0[:, 128 * h + 16 * gg:128 * h + 16 * gg + 16],
-            T.slips[16 * gg + 8 * h:16 * gg + 8 * h + 8, :], w=("T0_%d" % k,))
-    dma("y", "dr", T.recb[:], T.rec[:, :], w=("recb",))
-    dma("y", "dk", T.Kw[:, 0:W], T.kin[:, :], w=("Kw",))
-    dma("y", "dx", T.Xw[:], T.wealth[:, :], w=("Xw",))
+    PK, Ib = T.P3, T.Ib[:]
 
-    fill(T.ones[:], 1.0, ("ones",))
-    sel(T.Ib[:], T.ones[:, 0:128], [[-1, 128]], A.is_equal, 0, 1, ("ones",), ("Ib",))
-    sel(T.L16[0:16, :], T.ones[0:16, 0:128], [[0, 8], [1, 16]], A.is_equal, 0, -1, ("ones",), ("L16",))
-    sel(T.R16j[0:16, :], T.ones[0:16, :], [[0, 16], [1, 16]], A.is_equal, 0, -1, ("ones",), ("R16j",))
-    op("g", lambda e: e.iota(T.i1[:], [[0, 16]], 0, 1), (), ("i1",))
-    sel(T.L8[0:8, :], T.ones[0:8, 0:128], [[1, 8], [0, 16]], A.is_equal, 0, -1, ("ones",), ("L8",))
-    op("g", lambda e: e.iota(T.i2[:], [[1, 16]], 0, 0), (), ("i2",))
-    sel(T.R16b[0:16, :], T.ones[0:16, :], [[1, 16], [0, 16]], A.is_equal, 0, -1, ("ones",), ("R16b",))
-    sel(T.Z8[0:8, :], T.ones[0:8, 0:144], [[1, 144]], A.is_equal, -15, -16, ("ones",), ("Z8",))
-    sel(T.G88[0:8, :], T.ones[0:8, 0:8], [[1, 8]], A.is_equal, 0, -1, ("ones",), ("G88",))
-    op("g", lambda e: e.iota(T.i3[:], [[16, 16]], 15, 0), (), ("i3",))
-    op("g", lambda e: e.iota(T.dq[:], [[16, 16]], W, 0, allow_small_or_imprecise_dtypes=True), (), ("dq",))
-    op("g", lambda e: e.iota(T.Cm[:], [[0, 16], [-1, 16]], 15, 0, allow_small_or_imprecise_dtypes=True), (), ("Cm",))
+    def swap(src, key):
+        for z in range(2):
+            for y in range(2):
+                mm(PK[:, 0:8, z, :], T.Ax[:, 2 * z + y], src[:, :, y, :], y == 0, y == 1, "Ax%d %s" % (2 * z + y, key), "pK", "P3")
 
-    fill(T.seg[:], 1.0, ("seg",))
-    fill(T.seg[:, 0:1024:16], 0.0, ("seg",))
-    fill(T.m16[:], -16.0, ("m16",))
-    fill(T.mk4[:], 4096.0, ("mk4",))
-    fill(T.NT[:], 1.0, ("NT",))
-    fill(T.mv[:], 0.0, ("mv",))
-    fill(T.ca[:], 0.0, ("ca",))
-    fill(T.cb[:], 0.0, ("cb",))
-    ts(T.LT[:, 0:256], T.ones[:], 0.0, None, A.mult, None, ("ones",), ("LT",))
-    ts(T.LT[:, 256:512], T.ones[:], 0.0, None, A.mult, None, ("ones",), ("LT",))
+    def rotate(src, key, back):
+        for j in range(16):
+            r = (-5 * j if back else 5 * j) % 16
+            mm(T.P1[:, j:256:16], T.Wr[:, r] if r else Ib, src[:, j:256:16], True, True, "Ib Wr%d %s" % (r, key), "pA", "P1")
 
-    cp("v", T.I16[:], T.Ib[:], ("Ib",), ("I16",))
-    mm(T.P0[:, 0:256], T.L16[0:16, :], T.R16j[0:16, :], True, True, ("L16", "R16j"), ("pE",), ("P0",))
-    cp("v", T.E[:], T.P0[:, 0:256], ("pE",), ("E",), ("P0",))
-    for j in range(16):
-        r = 5 * j % 16
-        ts(T.Dr[:, 128 * r:128 * r + 128], T.I16[:], T.E[:, j:j + 1], None, A.mult, None, ("I16", "E"), ("Dr",))
-    cp("v", T.T0h[:], T.T0[:], tuple("T0_%d" % k for k in range(16)), ("T0h",))
-    for h in range(2):
-        mm(T.P2[:, 128 * h:128 * h + 128], T.T0h[:, 128 * h:128 * h + 128], T.I16[:], True, True, ("T0h", "I16"), ("pT0",), ("P2",))
-    for h in range(2):
-        cp("v", T.SLd[:, 256 * h:256 * h + 256], T.P2[:, 0:256], ("pT0",), ("SLd%d" % h,), ("P2",))
-    for r in range(16):
-        mm(T.P3[:, 0:16], T.Dr[:, 128 * r:128 * r + 128], T.SLd[:, 16 * r:16 * r + 16], r == 0, r == 15, ("Dr", "SLd0"), ("pc0",), ("P3",))
-    cp("v", T.cu0[:], T.P3[:, 0:16], ("pc0",), ("cu0",), ("P3",))
-    send(T.rcv0[:], T.cu0[:], "rl0", T.cores[(rank + 1) % 6], ("cu0",))
-    cp("v", T.ca[:, 1:17], T.P3[:, 0:16], ("pc0",), ("ca",), ("P3",))
-    act(T.Vw[:, 0:W], T.recb[:], F.Exp, ("recb",), ("Vw",), scale=6.0 * math.log(2.0))
-    mm(T.P1[:, 0:128], T.L8[0:8, :], T.L8[0:8, :], True, True, ("L8",), ("pB",), ("P1",))
-    mm(T.P1[:, 128:272], T.L8[0:8, :], T.Z8[0:8, :], True, True, ("L8", "Z8"), ("pB",), ("P1",))
-    mm(T.P1[:, 272:280], T.L8[0:8, :], T.G88[0:8, :], True, True, ("L8", "G88"), ("pB",), ("P1",))
-    mm(T.P0[:, 256:512], T.L16[0:16, :], T.R16b[0:16, :], True, True, ("L16", "R16b"), ("pD",), ("P0",))
-    for r in range(16):
-        mm(T.P5[:, 0:256], T.Dr[:, 128 * r:128 * r + 128], T.SLd[:, 16 * r:16 * r + 256], r == 0, r == 15, ("Dr", "SLd0", "SLd1"), ("pSL",), ("P5",))
+    dma("y", "dsl", T.S0[:], T.slips[:, :], w="S0")
+    dma("y", "dr", T.recb[:], T.rec[:, :], w="recb")
+    dma("y", "dk", T.K0[:, O:WT], T.kin[:, :], w="K0")
+    dma("y", "dx", T.Xw[:, O:WT], T.wealth[:, :], w="Xw")
 
-    def setup_vector():
-        ts(T.pm[:], T.i1[:], 15, None, A.bitwise_and, None, ("i1",), ("pm",))
-        cp("v", T.RL1[:], T.i2[:], ("i2",), ("RL1",))
-        cp("v", T.BO16[:], T.P1[:, 0:128], ("pB",), ("BO16",), ("P1",))
-        cp("v", T.BOb[:], T.P1[:, 0:128], ("pB",), ("BOb",), ("P1",))
-        sel(T.TRb[:], T.BOb[:], [[-1, 128]], A.is_gt, 0, 1, ("BOb",), ("TRb",))
-        cp("v", T.RL3[:], T.pm[:], ("pm",), ("RL3",))
-        cp("v", T.pmf[:], T.pm[:], ("pm",), ("pmf",))
-        cp("v", T.RL2[:], T.i3[:], ("i3",), ("RL2",))
-        ts(T.Gs[:], T.P1[:, 272:280], 16.0, None, A.mult, None, ("pB",), ("Gs",), ("P1",))
-        cp("v", T.G16[:], T.P1[:, 272:280], ("pB",), ("G16",), ("P1",))
-        cp("v", T.Zw[:], T.P1[:, 128:272], ("pB",), ("Zw",), ("P1",))
-        cp("v", T.Dm[:], T.P0[:, 256:512], ("pD",), ("Dm",), ("P0",))
-        ts(T.NDH[:], T.P0[:, 256:512], -1e29, 1e29, A.mult, A.add, ("pD",), ("NDH",), ("P0",))
-        ts(T.dum[:], T.dq[:], T.pmf[:, 0:1], None, A.add, None, ("dq", "pmf"), ("dum",))
-        ts(T.basec[:], T.pmf[:, 0:1], 2048.0, None, A.add, None, ("pmf",), ("basec",))
-        ts(T.nE[:], T.E[:, 0:16], -1.0, 1.0, A.mult, A.add, ("E",), ("nE",))
-        ts(T.negE[:], T.E[:, 0:16], -1.0, None, A.mult, None, ("E",), ("negE",))
-        cp("v", T.offs[:, 0:1], T.pm[:, 0:1], ("pm",), ("off0",))
-        for t in range(4):
-            cp("v", T.LT[:, 128 * t + t:128 * t + 128:16], T.BO16[:, t:128:16], ("BO16", "LT"), ("LTx",))
-            ts(T.ND[:, 128 * t:128 * t + 128], T.I16[:], T.nE[:, t:t + 1], None, A.mult, None, ("I16", "nE"), ("ND",))
-        cp("v", T.TR16[:], T.TRb[:], ("TRb",), ("TR16",))
+    cP, cM, cG, cZ, cW, cT, cK, cD, c1 = [T.col[:, k:k + 1] for k in range(9)]
+    iota(T.pi[:, 0:2], [[0, 2]], 0, 1, "pi")
+    iota(T.Id[:, 0:256], [[1, 256]], 0, 0, "Id0")
+    iota(T.Rb[:], [[1, 16], [0, 16]], 0, 0, "Rb")
+    iota(T.Id[:, 256:WT], [[1, WT - 256]], 256, 0, "Id")
+    for n in ("K0", "Kw", "Vw", "Xw", "Rw"):
+        fill(T[n][:, 0:O], 0 if n == "K0" else 32.0, n + "p")
+    fill(T.seg[:], 1.0, "seg")
+    fill(T.A0[:], 0.0, "A0")
+    fill(T.B0[:], 0.0, "mv UB")
+    fill(T.B1[:], 0.0, "c")
+    fill(T.torn[:], 0.0, "torn")
+    fill(T.seg[:, 0:128:16], 0.0, "seg")
+    cp("v", cP, T.pi[:, 0:1], "pi", "cP")
+    ts(T.pi[:, 2:3], T.pi[:, 0:1], 15, A.bitwise_and, "pi", "pm")
+    fill(T.Ax[:], 0.0, "Ax0 Ax1 Ax2 Ax3")
+    ts(Ib, T.Id[:, 0:128], cP, A.is_equal, "Id0 cP", "Ib")
+    cp("v", cM, T.pi[:, 2:3], "pm", "cM")
+    for k in range(2):
+        cp("v", T.Wc[:, :, 16 * k:16 * k + 16], Ib, "Ib", "Wc%d" % k)
+    for r in range(1, 16):
+        cp("s" if r % 2 == 0 else "v", T.Wr[:, r], T.Wc[:, :, r:r + 16], "Wc0 Wc1", "Wr%d" % r)
+    ts(T.Sh[:], T.S0[:], float(O), A.add, "S0", "Sh")
+    rotate(T.Sh, "Sh", False)
+    for k in range(4):
+        cp("v", T.Ax[:, k, :, k % 2, :], T.Ib[:, :, k // 2, :], "Ib", "Ax%d" % k)
+    ts(T.E16[:], T.Id[:, 0:16], cM, A.is_equal, "Id0 cM", "E16")
+    tt(cZ, cP, cM, A.subtract, "cP cM", "cZ")
+    cp("v", T.Si[:], T.P1[:, 0:256], "pA", "Si", "P1")
+    turn(T.St[:], T.Si[:], "Si", "St")
+    swap(T.St, "St")
+    ts(T.Dm[:], T.Rb[:], cM, A.is_equal, "Rb cM", "Dm")
+    cp("v", T.cu0[:], PK[:, 0:8, :, 0], "pK", "cu0", "P3")
+    send(T.rcv0[:], T.cu0[:], "rl0", T.cores[(rank + 1) % 6], "cu0")
+    cp("v", T.B1[:, 5:52:3], PK[:, 0:8, :, 0], "pK", "c", "P3")
+    cp("v", T.SL[:], PK[:, 0:8], "pK", "SL", "P3")
+    iota(T.Cm[:], [[0, 8], [-1, 16]], 15, 0, "Cm")
+    act(cW, cM, F.Exp, "cM", "cW", scale=-math.log(4.0))
+    act(T.Vw[:, O:WT], T.recb[:], F.Exp, "recb Vwp", "Vw", scale=4.0, bias=3.0)
+    ts(cG, cZ, 1.0 / 16, A.mult, "cZ", "cG")
+    ts(cZ, cZ, 15.0, A.add, "cZ", "cZ")
+    ts(cD, cM, float(WT), A.add, "cM", "cD")
+    ts(cK, cM, 16.0, A.mult, "cM", "cK", s2=7.5, o1=A.add)
+    ts(T.NDH[:], T.Dm[:], -9e28, A.mult, "Dm", "NDH", s2=9e28, o1=A.add)
+    ts(T.nE[:], T.E16[:], -1.0, A.mult, "E16", "nE", s2=1.0, o1=A.add)
+    ts(T.Zw[:], T.Id[:, 0:144], cZ, A.is_equal, "Id0 cZ", "Zw")
+    ts(T.Z16[:], T.Id[:, 0:144], cZ, A.is_equal, "Id0 cZ", "Z16", s2=16.0, o1=A.mult)
+    ts(T.BO4[:], T.Rb[:, 0:128], cG, A.is_equal, "Rb cG", "BO4", s2=4.0, o1=A.mult)
+    ts(T.W4[:], T.Rb[:, 0:128], cG, A.is_equal, "Rb cG cW", "W4", s2=cW, o1=A.mult)
+    ts(cT, cW, 32.0, A.mult, "cW", "cT")
+    ts(T.A1[:, 1:32:2], T.Id[:, 0:256:16], cD, A.add, "Id0 cD", "dum")
+    ts(T.offs[:, 0:1], cM, 16.0, A.mult, "cM", "off0")
+    ts(T.bas[:], T.Id[:, 0:8], cK, A.add, "Id0 cK", "bas", s2=-7.5, o1=A.add)
+    ts(T.sm[:, 0:8], T.Id[:, 0:8], 0.0, A.mult, "Id0 cM", "h", s2=cM, o1=A.add)
+    ts(T.RL[:], T.sm[:, 0:8], 2.0, A.mult, "h", "RL", s2=1.0, o1=A.add)
+    for t in range(4):
+        ts(T.LT[:, t], Ib, T.E16[:, t:t + 1], A.mult, "Ib E16", "LT%d" % t)
+        ts(T.ND[:, t], Ib, T.nE[:, t:t + 1], A.mult, "Ib nE", "ND%d" % t)
+    for t in range(NR):
+        act(T.DTH[:, t], T.NDH[:], F.Silu, "NDH", "DTH%d" % t, bias=0.8 * power(8 + t - 3))
+    for t in range(4):
+        act(T.Iv[:, t], T.Ib[:], F.Copy, "Ib", "Iv%d" % t, scale=power(8 + t))
+    act(T.D12[:], T.Dm[:], F.Copy, "Dm", "D12", scale=12.0)
 
-    def bar_of_own_office(t):
-        act(T.DTH[:, 256 * t:256 * t + 256], T.NDH[:], F.Copy, ("NDH",), ("DTH%d" % t,), bias=2.0 ** (6 * (8 + t - 3)))
-
-    def setup_scalar():
-        for t in range(4):
-            act(T.DT[:, 256 * t:256 * t + 256], T.Dm[:], F.Copy, ("Dm",), ("DT%d" % t,), scale=2.0 ** (6 * (8 + t)))
-        for t, n in ((11, "D11"), (12, "D12")):
-            act(T[n][:], T.Dm[:], F.Copy, ("Dm",), (n,), scale=float(t))
-
+    c = T.B1[:, 5:52:3]
+    inst, dum = T.A0[:, 1:32:2], T.A1[:, 1:32:2]
+    Pc, Pf, Po, Py = T.P6[:, 0:16], T.P6[:, 32:48], T.P6[:, 48:64], T.P6[:, 64:65]
+    XALL = " ".join("XCr%d" % m for m in range(16))
     for t in range(NR):
         last = t == NR - 1
-        cn = "ca" if t % 2 == 0 else "cb"
-        C = T[cn]
-        c, cprev = C[:, 1:17], C[:, 0:16]
-        cu, rcv, scl = T["cu%d" % t], T["rcv%d" % t], T["scl%d" % t]
-        cuk, rcvk, sclk = "cu%d" % t, "rcv%d" % t, "scl%d" % t
+        cu, rcv, scl, rep, rrv = [T["%s%d" % (n, t)] for n in ("cu", "rcv", "scl", "rep", "rrv")]
+        cuk, rcvk, sclk, repk, rrvk = ["%s%d" % (n, t) for n in ("cu", "rcv", "scl", "rep", "rrv")]
         p = T.cores[(rank - 1 - t % 5) % 6]
-        rep, repk = T["rep%d" % t], "rep%d" % t
         lastw[rcvk] = ("rl%d" % t, 8)
-        lastw["rrv%d" % t] = ("rr%d" % t, 8)
+        lastw[rrvk] = ("rr%d" % t, 8)
         KB = ("P2", "P7")
-        eqpos = [256]
-        for b in range(15):
-            eqpos.append(eqpos[b] + 16 * (15 - b))
+
+        def kin(out, lst, r, w):
+            if t == 0:
+                ts(out, T.K0[:].indirect(lst), float(O), A.add, "K0 K0p " + r, w)
+            else:
+                ts(out, T.Kw[:, 0:WT].indirect(lst), 0.25, A.add, "Kw " + r, w)
 
         def ask(k):
             a, b = ASK[k]
-            cp("v" if k in ASKV else "s", T.Vq[:, 16 * a:16 * b], T.Vw[:, 0:W].indirect(T.kcq[:, a:b]), ("Vw", "kcq"), ("Vq%d" % k,))
+            cp("v" if k in ASKV else "s", T.Vq[:, 16 * a:16 * b], T.Vw[:, 0:WT].indirect(T.kcq[:, a:b]), "Vw kcq", "Vq%d" % k)
 
         def ask_mm(k):
             a, b = ASK[k]
             for m in range(16):
-                mm(T.P1[:, a:b], T.Ib[:], T.Vq[:, 16 * a + m:16 * b:16], m == 0, m == 15, ("Ib", "Vq%d" % k), ("pA%d" % k,), ("P1",))
+                mm(T.P1[:, a:b], T.Ib[:], T.Vq[:, 16 * a + m:16 * b:16], m == 0, m == 15, "Ib Vq%d" % k, "pA", "P1")
 
         def own(k):
             a, b = OWN[k]
-            cp("s", T.Vg[:, 16 * a:16 * b], T.Vw[:, 0:W].indirect(T.kc[:, a:b]), ("Vw", "kc"), ("Vg%d" % k,))
+            cp("s", T.Vg[:, 16 * a:16 * b], T.Vw[:, 0:WT].indirect(T.kc[:, a:b]), "Vw kc", "Vg%d" % k)
 
         def own_mm(k):
             a, b = OWN[k]
             for m in range(16):
-                mm(T.P0[:, a:b], T.Ib[:], T.Vg[:, 16 * a + m:16 * b:16], False, False, ("Ib", "Vg%d" % k), ("pS",), ("P0",))
+                mm(T.P0[:, a:b], T.Ib[:], T.Vg[:, 16 * a + m:16 * b:16], False, False, "Ib Vg%d" % k, "pS", "P0")
 
         def wealth(h):
-            tt(T.Dx[:, 2048 * h:2048 * h + 2048], T.Xw[:].indirect(T.kc[:, 128 * h:128 * h + 128]), T.XCr[:, 2048 * h:2048 * h + 2048],
-               A.max, ("Xw", "kc") + tuple("XCr%d" % m for m in range(16)), ("Dx%d" % h,))
+            for B in range(4 * h, 4 * h + 4):
+                tt(T.Dx[:, B], T.Xw[:].indirect(T.kc[:, 32 * B:32 * B + 32]), T.XCr[:, 512 * B:512 * B + 512], A.max, "Xw kc " + XALL, "Dx%d" % B)
 
-        def key(h, m=None):
-            if m is None:
-                return T.P2[:, 0:128] if h == 0 else T.P7[:, 0:128]
-            return T.P2[:, m:128:16] if h == 0 else T.P7[:, m:128:16]
+        def key(h):
+            return T[KB[h]][:, 0:128]
+
+        def kin_mm():
+            for h in range(2):
+                for z in range(2):
+                    for y in range(2):
+                        mm(PK[:, 4 * h + 2 * z:4 * h + 2 * z + 2], T.Ax[:, 2 * z + y], T.kt[:, 4 * h:4 * h + 4, y, :], y == 0, y == 1,
+                           "Ax%d kt" % (2 * z + y), "pK", "P3")
 
         def score_mm(h):
-            mm(key(h), T.Ib[:], T.Cm[:, 128 * h:128 * h + 128], True, False, ("Ib", "Cm"), ("pKey%d" % h,), (KB[h],))
-            for m in range(16):
-                mm(key(h, m), T.Dx[:, 2048 * h + m:2048 * h + 2048:16], T.Gs[:], False, m == 15,
-                   ("Dx%d" % h, "Gs"), ("pKey%d" % h,), (KB[h],))
+            mm(key(h), T.Ib[:], T.Cm[:], True, False, "Ib Cm", "pKey%d" % h, KB[h])
+            for j in range(16):
+                for z in range(2):
+                    mm(T[KB[h]][:, 64 * z:64 * z + 64], T.Z16[:, 15 - j:143 - j], T.Dx[:, 4 * h:4 * h + 4, 256 * z + 16 * j:256 * z + 16 * j + 16],
+                       False, j == 15 and z == 1, "Z16 Dx%d" % (4 * h + 3), "pKey%d" % h, KB[h])
 
-        def eq_v():
-            for b in range(15):
-                ts(T.EQ[:, eqpos[b]:eqpos[b + 1]], T.crow[:, 16 * b + 16:256], T.c1[:, b:b + 1], None, A.is_equal, None, ("crow", "c1"), ("EQ%d" % b,))
-
-        def eq_mm():
-            for b in range(15):
-                mm(T.P5[:, 16 * b + 16:256], T.BOb[:], T.EQ[:, eqpos[b]:eqpos[b + 1]], False, b == 14, ("BOb", "EQ%d" % b), ("pcnt",), ("P5",))
-
-        def best_a(h):
+        def best(h):
             a, b = 128 * h, 128 * h + 128
-            scan(T.y[:, a:b], T.seg[:, 0:128], key(h), A.mult, A.max, ("seg", "pKey%d" % h), ("y%d" % h,), (KB[h],))
-            tt(T.eqn[:, a:b], key(h), T.y[:, a:b], A.is_equal, ("pKey%d" % h, "y%d" % h), ("eqn%d" % h,), (KB[h],))
-            tt(T.neq[:, a:b], key(h), T.y[:, a:b], A.not_equal, ("pKey%d" % h, "y%d" % h), ("neq%d" % h,), (KB[h],))
+            scan(T.y[:, a:b], T.seg[:], key(h), A.mult, A.max, "seg pKey%d" % h, "y%d" % h, KB[h])
+            tt(T.eqn[:, a:b], key(h), T.y[:, a:b], A.is_equal, "pKey%d y%d" % (h, h), "eqn%d" % h, KB[h])
+            tt(T.ek[:, a:b], PK[:, 4 * h:4 * h + 4], T.eqn[:, a:b], A.mult, "pK eqn%d" % h, "ek%d" % h, "P3")
+            ts(T.neq[:, a:b], T.eqn[:, a:b], -1.0, A.mult, "eqn%d" % h, "neq%d" % h, s2=1.0, o1=A.add)
+            scan(T.s2[:, h], T.neq[:, a:b], T.ek[:, a:b], A.mult, A.add, "neq%d ek%d" % (h, h), "s2_%d" % h)
 
-        def best_b(h):
-            a, b = 128 * h, 128 * h + 128
-            tt(T.ek[:, a:b], T.P3[:, a:b], T.eqn[:, a:b], A.mult, ("pkc", "eqn%d" % h), ("ek%d" % h,), ("P3",))
-            scan(T.s2[:, a:b], T.neq[:, a:b], T.ek[:, a:b], A.mult, A.add, ("neq%d" % h, "ek%d" % h), ("s2_%d" % h,))
-
-        def best_c(h):
-            a, b = 128 * h, 128 * h + 128
-            tt(T.Bx[:, a:b], T.s2[:, a:b].indirect(T.RL2[:, 0:8]), T.E[:, a:b], A.mult, ("s2_%d" % h, "RL2", "E"), ("Bx%d" % h,))
-
-        def best_mm(h):
-            mm(T.P4[:, 8 * h:8 * h + 8], T.Bx[:, 128 * h:128 * h + 128], T.G16[:], True, True, ("Bx%d" % h, "G16"), ("pBest",), ("P4",))
-
-        if t == 0:
-            setup_vector()
-        cp("v", T.kc[:], T.Kw[:, 0:W].indirect(cu[:]), ("Kw", cuk), ("kc",))
+        kin(T.kc[:], cu[:], cuk, "kc")
+        cp("s", T.XC[:], T.Xw[:].indirect(cu[:]), "Xw Xwp " + cuk, "XC")
         if t > 0:
-            tt(T.Vw[:].indirect(T["scl%d" % (t - 1)][:]), T.VC[:], T.DT[:, 256 * (t - 1):256 * t], A.add, ("VC", "DT%d" % (t - 1), "scl%d" % (t - 1)), ("Vw",))
-        if last:
-            cp("v", T.SL[:].indirect(T.offs[:, 2 * t:2 * t + 1]), T.mk4[:], ("mk4", "off%d" % t, cn, cuk), ("SL",))
-            for h in range(2):
-                cp("v", T.SLd[:, 256 * h:256 * h + 256], T.SL[:], ("SL",), ("SLd%d" % h,))
-            for r in range(16):
-                x = 16 * ((16 - r) % 16)
-                mm(T.P6[:, 256:512], T.Dr[:, 128 * r:128 * r + 128], T.SLd[:, x:x + 256], r == 0, r == 15, ("Dr", "SLd0", "SLd1"), ("pSU",), ("P6",))
-        cp("s", T.XC[:], T.Xw[:].indirect(cu[:]), ("Xw", cuk), ("XC",))
-        for m in range(NS):
-            cp("s", T.XCr[:, m:4096:16], T.XC[:], ("XC",), ("XCr%d" % m,))
-        cp("s", T.VC[:], T.Vw[:, 0:W].indirect(cu[:]), ("Vw", cuk), ("VC",))
-        ts(T.c1[:], c, 1.0, None, A.add, None, (cn,), ("c1",))
-        cp("v", T.kc16[:], T.kc[:], ("kc",), ("kc16",))
-        tt(T.cE[:], T.c1[:].indirect(T.RL1[:]), T.E[:], A.mult, ("c1", "RL1", "E"), ("cE",))
-        for m in range(NS, 16):
-            cp("v", T.XCr[:, m:4096:16], T.XC[:], ("XC",), ("XCr%d" % m,))
-        cp("v", T.kcq[:], T.Kw[:, 0:W].indirect(rcv[:]), ("Kw", rcvk), ("kcq",))
+            scatter(T.Vw[:].indirect(T["scl%d" % (t - 1)][:]), T.nV[:], "nV scl%d" % (t - 1), "Vw")
+        cp("s", T.VC[:], T.Vw[:, 0:WT].indirect(cu[:]), "Vw " + cuk, "VC")
+        for m in range(NG):
+            cp("g", T.XCr[:, m:4096:16], T.XC[:], "XC", "XCr%d" % m)
+        cp("v", T.crow[:], T.Id[:].indirect(cu[:]), "Id Id0 " + cuk, "crow")
+        cp("v", T.kc16[:], T.kc[:], "kc", "kc16")
+        tt(T.A1[:, 0:32:2], c, dum, A.subtract, "c dum", "dc")
+        turn(T.kt[:], T.kc16[:], "kc16", "kt")
+        for b in range(16):
+            ts(T.EQ[:, b, 0:256 - 16 * b], T.crow[:, 16 * b:256], T.B1[:, 5 + 3 * b:6 + 3 * b], A.is_equal, "crow c", "EQ%d" % b)
+        kin(T.kcq[:], rcv[:], rcvk, "kcq")
         for k in range(PRE):
             own(k)
         for k in ASKO:
             ask(k)
-        mm(T.P4[:, 0:256], T.BO16[:], T.cE[:], True, True, ("BO16", "cE"), ("pcrow",), ("P4",))
-        mm(T.P4[:, 256:512], T.TR16[:], T.cE[:], True, True, ("TR16", "cE"), ("pcrow",), ("P4",))
-        for h in range(2):
-            mm(T.P3[:, 128 * h:128 * h + 128], T.kc16[:, 128 * h:128 * h + 128], T.I16[:], True, True, ("kc16", "I16"), ("pkc",), ("P3",))
+        kin_mm()
+        mm(T.P0[:, 0:256], T.Ib[:], T.VC[:], True, False, "Ib VC", "pS", "P0")
         if not last:
-            mm(T.P3[:, 256:512], T.ND[:, 128 * t:128 * t + 128], T.kc16[:], True, False, ("ND", "kc16"), ("pnK",), ("P3",))
-            mm(T.P3[:, 256:512:2], T.LT[:, 128 * t:128 * t + 128], T.cE[:, 1:256:2], False, False, ("LTx", "cE"), ("pnK",), ("P3",))
-            mm(T.P3[:, 257:512:2], T.LT[:, 128 * t:128 * t + 128], T.cE[:, 0:256:2], False, True, ("LTx", "cE"), ("pnK",), ("P3",))
-        if last:
-            ts(T.Rw[:, 0:W], T.r24[:], 16.0, None, A.subtract, None, ("r24",), ("Rw",))
-            tt(T.nR[:], T.Rw[:, 0:W].indirect(T.cu3[:]), T.D11[:], A.max, ("Rw", "cu3", "D11"), ("nR",))
-
-        mm(T.P0[:, 0:256], T.Ib[:], T.VC[:], True, False, ("Ib", "VC"), ("pS",), ("P0",))
+            mm(T.P4[:, 0:256], T.ND[:, t], T.kc16[:], True, False, "ND%d kc16" % t, "pnK", "P4")
+            mm(T.P4[:, 0:256:2], T.LT[:, t], T.crow[:, 1:256:2], False, False, "LT%d crow" % t, "pnK", "P4")
+            mm(T.P4[:, 1:256:2], T.LT[:, t], T.crow[:, 0:256:2], False, True, "LT%d crow" % t, "pnK", "P4")
+            mm(T.P4[:, 256:512], T.Ib[:], T.VC[:], True, False, "Ib VC", "pnV", "P4")
+            mm(T.P4[:, 256:512], T.Iv[:, t], T.Dm[:], False, True, "Iv%d Dm" % t, "pnV", "P4")
+        mm(T.P5[:, 0:256], T.W4[:], T.EQ[:, :, 0:16], True, False, "W4 EQ15", "pcnt", "P5")
+        for b in range(15):
+            mm(T.P5[:, 16 * b + 16:256], T.BO4[:], T.EQ[:, b, 16:256 - 16 * b], False, b == 14, "BO4 EQ15", "pcnt", "P5")
         for k in range(PRE):
             own_mm(k)
         for k in ASKO:
             ask_mm(k)
-        for k in range(PRE, MID):
-            own(k)
-        cp("s", rep[:], T.P1[:, 0:256], tuple("pA%d" % k for k in ASKO), (repk,), ("P1",))
-        send(T["rrv%d" % t][:], rep[:], "rr%d" % t, p, (repk,))
+        cp("s", rep[:], T.P1[:, 0:256], "pA", repk, "P1")
+        send(T[rrvk][:], rep[:], "rr%d" % t, p, repk)
+        for m in range(NG, 16):
+            cp("v", T.XCr[:, m:4096:16], T.XC[:], "XC", "XCr%d" % m)
+        cp("s", T.cn[:], T.P5[:, 0:256], "pcnt", "cn", "P5")
         wealth(0)
-        cp("v", T.crow[:], T.P4[:], ("pcrow",), ("crow",), ("P4",))
-        tt(T.EQ[:, 0:256], T.c1[:].indirect(T.RL1[:]), T.crow[:, 256:512], A.is_equal, ("c1", "RL1", "crow"), ("EQin",))
-        eq_v()
-        score_mm(0)
-        if t == 0:
-            cp("v", T.SL[:], T.P5[:, 0:256], ("pSL",), ("SL",), ("P5",))
-        mm(T.P5[:, 0:256], T.BOb[:], T.EQ[:, 0:256], True, False, ("BOb", "EQin"), ("pcnt",), ("P5",))
-        eq_mm()
-        for k in range(PRE, MID):
-            own_mm(k)
-        wealth(1)
-        own(MID)
-        own_mm(MID)
-        score_mm(1)
-        for k in range(MID + 1, len(OWN)):
-            own(k)
-        act(T.UU[:, 512:768], T.P5[:, 0:256], F.Copy, ("pcnt",), ("UUn",), ("P5",), scale=4.0)
-        if not last:
-            bar_of_own_office(t + 1)
-        if t == 0:
-            bar_of_own_office(0)
-        best_a(0)
-        best_b(0)
-        best_c(0)
-        for k in range(MID + 1, len(OWN)):
-            own_mm(k)
-        if t == 3:
-            act(T.lnb[:], T.Vw[:, 0:W], F.Ln, ("Vw",), ("lnb",), scale=2.0 ** -48)
-            act(T.r24[:], T.lnb[:], F.Copy, ("lnb",), ("r24",), scale=1.0 / (6.0 * math.log(2.0)), bias=24.0)
-        if last:
-            cp("v", T.Rw[:].indirect(T.scl3[:]), T.nR[:], ("nR", "scl3", "Rw"), ("Rw",))
-            tt(T.nR[:], T.Rw[:, 0:W].indirect(cu[:]), T.D12[:], A.max, ("Rw", cuk, "D12"), ("nR",))
-            ts(T.msk[:], T.P6[:, 256:512], 4096.0, None, A.is_ge, None, ("pSU",), ("msk",), ("P6",))
-            ts(T.ltm[:], T.P6[:, 256:512], 4096.0, None, A.is_lt, None, ("pSU",), ("ltm",), ("P6",))
-            tt(T.SLz[:], T.P6[:, 256:512], T.ltm[:], A.mult, ("pSU", "ltm"), ("SLz",), ("P6",))
-        best_a(1)
-        mm(T.P0[:, 0:256], T.Ib[:], T["rrv%d" % t][:], False, True, ("Ib", "rrv%d" % t), ("pS",), ("P0",))
-        ts(T.UU[:, 0:256], T.P0[:, 0:256], 2.0 ** (6 * (8 + t - 2)), None, A.is_ge, None, ("pS",), ("UU2",), ("P0",))
-        tt(T.UU[:, 256:512], T.P0[:, 0:256], T.DTH[:, 256 * t:256 * t + 256], A.is_ge, ("pS", "DTH%d" % t), ("UU3",), ("P0",))
         for j in range(16):
-            mm(T.P6[:, 0:48], T.Zw[:, 15 - j:143 - j], T.UU[:, j:768:16], j == 0, j == 15, ("Zw", "UU2", "UU3", "UUn"), ("pF",), ("P6",))
-        best_b(1)
-        if not last:
-            act(T.nK[:], T.P3[:, 256:512], F.Identity, ("pnK", "negE"), ("nK",), ("P3",), bias=T.negE[:, t:t + 1])
+            mm(Pc, T.Zw[:, 15 - j:143 - j], T.cn[:, j:256:16], j == 0, j == 15, "Zw cn", "pC", "P6")
+        own(PRE)
+        score_mm(0)
+        own_mm(PRE)
+        wealth(1)
+        for k in range(PRE + 1, len(OWN)):
+            own(k)
+        ts(T.NC[:, 0:16], Pc, cT, A.is_ge, "pC cT", "NC", "P6", s2=-64.0, o1=A.mult)
+        ts(T.NC[:, 16:32], Pc, cT, A.is_ge, "pC cT", "NC1", "P6")
+        own_mm(PRE + 1)
+        score_mm(1)
+        mm(T.P6[:, 32:64], T.Ib[:], T.NC[:], True, False, "Ib NC NC1", "pF", "P6")
+        for k in range(PRE + 2, len(OWN)):
+            own_mm(k)
         if t == 0:
-            setup_scalar()
-        best_c(1)
-        best_mm(0)
-        best_mm(1)
-        cp("v", T.Bf[:], T.P6[:, 0:48], ("pF",), ("Bf",), ("P6",))
-        sm = [T.sm[:, 16 * k:16 * k + 16] for k in range(16)]
-        tt(T.wi[:], T.Bf[:, 0:16], T.Bf[:, 32:48], A.add, ("Bf",), ("wi",))
-        ts(sm[0], T.Bf[:, 16:32], 8.0, None, A.mult, None, ("Bf",), ("d8",))
-        tt(T.gq[:], T.wi[:], sm[0], A.max, ("wi", "d8"), ("gq",))
-        ts(T.pp[:], T.wi[:], 1, None, A.bitwise_and, None, ("wi",), ("pp",))
-        ts(sm[1], T.wi[:], 12.0, None, A.is_lt, None, ("wi",), ("lt12",))
+            ts(T.Kw[:, O:WT], T.K0[:, O:WT], float(O), A.add, "K0 Kwp", "Kw")
+        best(0)
+        best(1)
         if not last:
-            ts(T.nirep[:], T.gq[:].indirect(T.RL3[:, 0:8]), 8.0, None, A.is_ge, None, ("gq", "RL3"), ("nirep",))
-            mm(T.P6[:, 64:65], T.nirep[:], T.m16[:, 0:1], True, True, ("nirep", "m16"), ("pOff",), ("P6",))
-        ts(sm[2], T.gq[:], 8.0, None, A.is_ge, None, ("gq",), ("ni",))
-        ts(sm[3], T.wi[:], 64.0, None, A.is_lt, None, ("wi",), ("lt64",))
-        tt(sm[4], T.pp[:], sm[1], A.mult, ("pp", "lt12"), ("m1",))
-        tt(sm[6], sm[2], T.dum[:], A.mult, ("ni", "dum"), ("nd",))
-        tt(sm[7], sm[3], sm[1], A.subtract, ("lt64", "lt12"), ("tb",))
-        tt(sm[5], sm[4], sm[2], A.mult, ("m1", "ni"), ("m2",))
-        tt(sm[8], sm[6], c, A.max, ("nd", cn), ("lst",))
-        tt(T.NT[:, 0:16], sm[2], sm[7], A.subtract, ("ni", "tb", "NT"), ("NT",))
-        cp("v", scl[:], sm[8], ("lst",), (sclk,))
-        tt(T.mv[:, 1:17], sm[5], T.NT[:, 1:17], A.is_gt, ("m2", "NT", "mv"), ("mv",))
+            cp("s", T.nK[:], T.P4[:, 0:256], "pnK", "nK", "P4")
+            cp("s", T.nV[:], T.P4[:, 256:512], "pnV", "nV", "P4")
+        else:
+            act(T.lnb[:], T.Vw[:, O:WT], F.Ln, "Vw", "lnb", scale=math.exp(-33.0))
+        for z in range(2):
+            bk = T.s2[:, :, 64 * z + 15:64 * z + 64:16]
+            tt(T.B1[:, 4 + 3 * z:51:6], bk, T.B1[:, 5 + 3 * z:52:6], A.subtract, "s2_0 s2_1 c", "d1%d" % z)
+            tt(T.B1[:, 3 + 3 * z:50:6], T.B1[:, 2 + 3 * z:48:6], bk, A.subtract, "s2_0 s2_1 c", "d2%d" % z)
+        mm(T.P0[:, 0:256], T.Ib[:], rrv[:], False, True, "Ib " + rrvk, "pS", "P0")
+        ts(T.UU[:, 0:256], T.P0[:, 0:256], 0.8 * power(8 + t - 2), A.is_ge, "pS", "UU2", "P0")
+        tt(T.UU[:, 256:512], T.P0[:, 0:256], T.DTH[:, t], A.is_ge, "pS DTH%d" % t, "UU3", "P0")
+        for j in range(16):
+            mm(T.P6[:, 32:64], T.Zw[:, 15 - j:143 - j], T.UU[:, j:512:16], False, j == 15, "Zw UU2 UU3", "pF", "P6")
         if last:
-            cp("v", T.Rw[:].indirect(scl[:]), T.nR[:], ("nR", sclk, "Rw"), ("Rw",))
-            dma("y", "dout", T.yr[:, :], T.Rw[:, 0:W], r=("Rw",))
-        else:
-            ts(T.yo[:, 0:1], T.P6[:, 64:65], T.basec[:, 0:1], float(16 * (t + 1)), A.add, A.add, ("pOff", "basec"), ("yo",), ("P6",))
-        tt(sm[9], T.NT[:, 0:16], T.mv[:, 1:17], A.is_gt, ("NT", "mv"), ("NM",))
-        tt(sm[11], T.mv[:, 0:16], cprev, A.mult, ("mv", cn), ("R2",))
+            ts(T.Rw[:, O:WT], T.lnb[:], 30.0, A.add, "lnb Rwp", "Rw", s2=0.25, o1=A.mult)
+        h, t12, cand = T.sm[:, 0:16], T.sm[:, 16:32], T.sm[:, 32:48]
+        ts(h, Pf, 8.0, A.is_lt, "pF", "h", "P6")
+        ts(t12, Pf, 12.0, A.is_ge, "pF", "t12", "P6")
+        tt(inst, h, Po, A.is_gt, "h pF A0", "inst", "P6")
+        cp("v", T.fi[:, 0:16], Pf, "pF", "fi", "P6")
         if not last:
-            ts(T.yo[:, 1:2], T.yo[:, 0:1], 255, None, A.bitwise_and, None, ("yo",), ("ya",))
-        tt(sm[10], sm[9], c, A.mult, ("NM", cn), ("R1",))
-        tt(sm[12], sm[9], T.mv[:, 0:16], A.add, ("NM", "mv"), ("q1",))
-        tt(sm[13], sm[10], sm[11], A.add, ("R1", "R2"), ("R12",))
-        ts(sm[14], sm[12], -1.0, 1.0, A.mult, A.add, ("q1",), ("Bm",))
+            cp("s", T.nirep[:], T.A0[:].indirect(T.RL[:]), "inst RL", "nirep")
+            mm(Py, T.Ib[:], T.bas[:, t + 1:t + 2], True, False, "Ib bas", "pY", "P6")
+            mm(Py, T.nirep[:], T.seg[:, 1:2], False, True, "nirep seg", "pY", "P6")
+        scan(T.Ao[:], T.A0[:], T.A1[:], A.mult, A.add, "inst dc dum", "Ao")
+        tt(T.torn[:, 0:16], t12, inst, A.add, "t12 inst", "torn")
+        ts(T.fi[:, 16:32], T.fi[:, 0:16], -31, A.bitwise_and, "fi", "odd")
+        cp("v", scl[:], T.Ao[:, 1:32:2], "Ao", sclk)
+        tt(cand, T.fi[:, 16:32], T.torn[:, 0:16], A.is_gt, "odd torn", "cand")
         if not last:
-            cp("v", T.offs[:, 2 * t + 2:2 * t + 3], T.yo[:, 1:2], ("ya",), ("off%d" % (t + 1),))
-        tt(sm[15], T.P4[:, 0:16], sm[14], A.mult, ("pBest", "Bm"), ("xb",), ("P4",))
-        tt(T.nw[:], sm[15], sm[13], A.add, ("xb", "R12"), ("nw",))
+            scatter(T.Kw[:].indirect(scl[:]), T.nK[:], "nK " + sclk, "Kw")
+        tt(T.B0[:, 4:52:3], cand, T.torn[:, 1:17], A.mult, "cand torn", "mv")
         if not last:
-            cp("v", T.SL[:].indirect(T.offs[:, 2 * t:2 * t + 1]), T.nw[:], ("nw", "off%d" % t, "SL"), ("SL",))
+            ts(T.kk[:], Py, cK, A.subtract, "pY cK", "kk", "P6", s2=1.0 / 16, o1=A.mult)
+        tt(T.B0[:, 2:48:3], T.torn[:, 0:16], T.B0[:, 4:52:3], A.add, "torn mv", "UB")
+        if not last:
+            ts(T.offs[:, 2 * t + 2:2 * t + 3], T.kk[:], -16.0, A.mult, "kk pY", "off%d" % (t + 1), "P6", s2=Py, o1=A.add)
+        scan(T.Bo[:], T.B0[:, 0:48], T.B1[:, 3:51], A.mult, A.add, "mv UB c d10 d11 d20 d21", "Bo")
+        cp("v", T.SL[:].indirect(T.offs[:, 2 * t:2 * t + 1]), T.Bo[:, 2:48:3], "Bo off%d" % t, "SL")
+        if not last:
             n = t + 1
-            nn = "cb" if t % 2 == 0 else "ca"
-            cp("v", T["cu%d" % n][:], T.SL[:].indirect(T.offs[:, 2 * n:2 * n + 1]), ("SL", "off%d" % n), ("cu%d" % n,))
-            send(T["rcv%d" % n][:], T["cu%d" % n][:], "rl%d" % n, T.cores[(rank + 1 + n % 5) % 6], ("cu%d" % n,))
-            cp("v", T[nn][:, 1:17], T.SL[:].indirect(T.offs[:, 2 * n:2 * n + 1]), ("SL", "off%d" % n, nn), (nn,))
-            cp("v", T.Kw[:].indirect(scl[:]), T.nK[:], ("nK", sclk, "Kw"), ("Kw",))
+            cp("v", T["cu%d" % n][:], T.SL[:].indirect(T.offs[:, 2 * n:2 * n + 1]), "SL off%d" % n, "cu%d" % n)
+            send(T["rcv%d" % n][:], T["cu%d" % n][:], "rl%d" % n, T.cores[(rank + 1 + n % 5) % 6], "cu%d" % n)
+            cp("v", c, T.SL[:].indirect(T.offs[:, 2 * n:2 * n + 1]), "SL off%d" % n, "c")
         else:
-            tt(T.nm[:], T.nw[:].indirect(T.RL3[:]), T.msk[:], A.mult, ("nw", "RL3", "msk"), ("nm",))
-            for h in range(2):
-                a, b = 256 + 128 * h, 384 + 128 * h
-                mm(T.P4[:, a:b], T.SLz[:, 128 * h:128 * h + 128], T.I16[:], True, False, ("SLz", "I16"), ("pY",), ("P4",))
-                mm(T.P4[:, a:b], T.nm[:, 128 * h:128 * h + 128], T.I16[:], False, True, ("nm", "I16"), ("pY",), ("P4",))
-            cp("v", T.ysb[:], T.P4[:, 256:512], ("pY",), ("ysb",), ("P4",))
-            for k in range(16):
-                gg, h = k // 2, k % 2
-                dma("y" if h == 0 else "s", "dout", T.ys[16 * gg + 8 * h:16 * gg + 8 * h + 8, :],
-                    T.ysb[:, 128 * h + 16 * gg:128 * h + 16 * gg + 16], r=("ysb",))
+            cp("v", T.Su[:], T.SL[:], "SL", "Su")
+            swap(T.Su, "Su")
+            tt(T.nR[:], T.Rw[:, 0:WT].indirect(cu[:]), T.D12[:], A.max, "Rw D12 " + cuk, "nR")
+            cp("v", T.Si[:], PK[:, 0:8], "pK", "Si", "P3")
+            turn(T.Sh[:], T.Si[:], "Si", "Sh")
+            rotate(T.Sh, "Sh", True)
+            cp("v", T.Rw[:].indirect(scl[:]), T.nR[:], "nR " + sclk, "Rw")
+            act(T.ysb[:], T.P1[:, 0:256], F.Copy, "pA", "ysb", "P1", bias=-float(O))
+            dma("s", "dout", T.ys[:, :], T.ysb[:], r="ysb")
+            dma("y", "dout", T.yr[:, :], T.Rw[:, O:WT], r="Rw")
     for s in ("v", "s", "t", "g", "dsl", "dk", "dr", "dx", "loc", "dout"):
         wait("g", (s, cnt[s]))
     for t in range(NR):

@@ -4,11 +4,12 @@ from concourse.mybir import dt, AluOpType, AxisListType, ActivationFunctionType
 W, NR, O = 1408, 5, 32
 WT = O + W
 WD = WT + 256
-NG = 7
-OWN = ((0, 48), (48, 128), (128, 208), (208, 256))
-PRE = 1
-ASK = ((0, 96), (96, 160), (160, 192), (192, 256))
-ASKV, ASKO = (3,), (3, 0, 1, 2)
+OWN = ((0, 64), (64, 112), (112, 192), (192, 256))
+LA = OWN[-1][0]
+ASKS = ((192, 256), (0, 64), (64, 128), (128, 192))
+ASKF = ((232, 256), (0, 80), (80, 160), (160, 232))
+ASKL = ((160, 256), (0, 64), (64, 128), (128, 160))
+EQA, EQB = 8, 10
 
 
 def power(r):
@@ -22,23 +23,23 @@ def sb(dtype, *shape):
 SCRATCH = {
     "K0": sb("int32", WT), "Kw": sb("float32", WD), "Vw": sb("float32", WD), "Xw": sb("bfloat16", WT), "Id": sb("float32", WT),
     "recb": sb("bfloat16", W), "lnb": sb("bfloat16", W), "Rw": sb("bfloat16", WD),
-    "S0": sb("int32", 256), "Sh": sb("float16", 256), "Si": sb("float16", 256), "St": sb("float16", 8, 2, 16), "Su": sb("float16", 8, 2, 16),
+    "S0": sb("int32", 256), "Sh": sb("float16", 256), "Si": sb("float16", 256), "St": sb("float16", 8, 2, 16),
     "SL": sb("float32", 256), "ysb": sb("float32", 256),
-    "pi": sb("int32", 4), "col": sb("float32", 16), "bas": sb("bfloat16", 8), "Rb": sb("float32", 256),
+    "pi": sb("int32", 4), "col": sb("float32", 16), "bas": sb("bfloat16", 8), "Rb": sb("float32", 256), "Rj": sb("float32", 256),
     "Ib": sb("bfloat16", 4, 2, 16), "Wc": sb("bfloat16", 8, 32), "Wr": sb("bfloat16", 16, 128), "Ax": sb("bfloat16", 4, 4, 2, 16),
-    "E16": sb("float32", 16), "nE": sb("float32", 16), "Dm": sb("bfloat16", 256), "D12": sb("bfloat16", 256), "NDH": sb("float32", 256),
-    "DTH": sb("float32", NR, 256), "Iv": sb("bfloat16", 4, 128), "ND": sb("bfloat16", 4, 128), "LT": sb("bfloat16", 4, 128),
-    "Zw": sb("bfloat16", 144), "Z16": sb("bfloat16", 144), "BO4": sb("bfloat16", 128), "W4": sb("bfloat16", 128),
-    "Cm": sb("bfloat16", 128), "seg": sb("bfloat16", 128), "RL": sb("uint16", 8), "offs": sb("uint16", 16),
-    "kc": sb("uint16", 256), "kcq": sb("uint16", 256), "kc16": sb("float16", 256), "kt": sb("float16", 8, 2, 16), "crow": sb("float16", 256),
-    "XC": sb("bfloat16", 256), "XCr": sb("bfloat16", 4096), "VC": sb("bfloat16", 256),
-    "Vg": sb("bfloat16", 4096), "Vq": sb("bfloat16", 4096), "Dx": sb("bfloat16", 8, 512),
+    "zero": sb("bfloat16", 128), "E": sb("bfloat16", 256), "Dm": sb("bfloat16", 256), "D12": sb("bfloat16", 256),
+    "NDH": sb("float32", 256), "DTH": sb("float32", NR, 256), "Iv": sb("bfloat16", 4, 128), "ND": sb("bfloat16", 4, 128),
+    "LT": sb("bfloat16", 4, 128), "Zw": sb("bfloat16", 144), "BO4": sb("bfloat16", 128), "W4": sb("bfloat16", 128),
+    "Gs": sb("bfloat16", 8), "G1": sb("bfloat16", 8), "K16": sb("bfloat16", 32), "Cm": sb("bfloat16", 256), "seg": sb("bfloat16", 256),
+    "RL": sb("uint16", 8), "RL2": sb("uint16", 16), "offs": sb("uint16", 16),
+    "kc": sb("uint16", 256), "kcq": sb("uint16", 256), "kts": sb("uint16", 256), "kc16": sb("float16", 256), "kt": sb("float16", 8, 2, 16),
+    "crow": sb("float16", 256), "XC": sb("bfloat16", 256), "VC": sb("bfloat16", 256),
+    "Vg": sb("bfloat16", 4096), "Vq": sb("bfloat16", 4096), "Dx": sb("bfloat16", 16, 256),
     "EQ": sb("bfloat16", 16, 256), "cn": sb("bfloat16", 256), "NC": sb("bfloat16", 32), "UU": sb("bfloat16", 512),
     "nK": sb("float32", 256), "nV": sb("float32", 256), "nR": sb("bfloat16", 256),
-    "y": sb("float32", 256), "eqn": sb("bfloat16", 256), "neq": sb("bfloat16", 256), "ek": sb("float16", 256), "s2": sb("float16", 2, 128),
-    "A0": sb("float32", 32), "A1": sb("float32", 32), "Ao": sb("float32", 32),
-    "B0": sb("float32", 52), "B1": sb("float32", 52), "Bo": sb("float32", 48),
-    "sm": sb("float32", 64), "torn": sb("float32", 17), "fi": sb("int32", 32), "kk": sb("int32", 1), "nirep": sb("bfloat16", 128),
+    "y": sb("float32", 256), "eqn": sb("bfloat16", 256), "neq": sb("bfloat16", 256), "ek": sb("float16", 256), "s2": sb("float32", 256),
+    "Bx": sb("float16", 256), "Z": sb("float32", 160), "A1": sb("float32", 32), "Ao": sb("float32", 32), "Bo": sb("float32", 48),
+    "sm": sb("float32", 64), "fi": sb("int32", 32), "kk": sb("int32", 1), "nirep": sb("bfloat16", 128),
 }
 for _t in range(NR):
     for _n in ("cu", "rcv", "scl"):
@@ -105,7 +106,7 @@ def rank_program(g, core, T, topo):
         for b in bk:
             bank.setdefault(b, {})[q] = tok
 
-    def op(q, fn, r=(), w=(), bk=()):
+    def op(q, fn, r, w, bk):
         r, w, bk = r.split(), w.split(), bk.split()
         deps(q, r, w, bk)
         fn(queues[q]).then_inc(T.sem[q], 1)
@@ -125,8 +126,6 @@ def rank_program(g, core, T, topo):
     def cp(q, out, in_, r, w, bk=""):
         if q == "s":
             op("s", lambda e: e.activation(out, in_, F.Copy), r, w, bk)
-        elif q == "g":
-            op("g", lambda e: e.affine_select(out, in_, [[0, 256]], A.is_gt, 0.0, 1, 0), r, w, bk)
         else:
             op("v", lambda e: e.tensor_copy(out, in_), r, w, bk)
 
@@ -157,6 +156,9 @@ def rank_program(g, core, T, topo):
         else:
             op("g", lambda e: e.iota(out, pat, base, cm, allow_small_or_imprecise_dtypes=True), "", w, "")
 
+    def select(out, in_, pat, o, other, base, cm, r, w):
+        op("g", lambda e: e.affine_select(out, in_, pat, o, other, base, cm), r, w, "")
+
     def turn(out, in_, r, w):
         op("v", lambda e: e.transpose(out, in_), r, w, "")
 
@@ -169,248 +171,283 @@ def rank_program(g, core, T, topo):
 
     PK, Ib = T.P3, T.Ib[:]
 
-    def swap(src, key):
+    def swap():
         for z in range(2):
             for y in range(2):
-                mm(PK[:, 0:8, z, :], T.Ax[:, 2 * z + y], src[:, :, y, :], y == 0, y == 1, "Ax%d %s" % (2 * z + y, key), "pK", "P3")
+                mm(PK[:, 0:8, z, :], T.Ax[:, 2 * z + y], T.St[:, :, y, :], y == 0, y == 1, "Ax%d St" % (2 * z + y), "pK", "P3")
 
-    def rotate(src, key, back):
+    def rotate(back):
         for j in range(16):
             r = (-5 * j if back else 5 * j) % 16
-            mm(T.P1[:, j:256:16], T.Wr[:, r] if r else Ib, src[:, j:256:16], True, True, "Ib Wr%d %s" % (r, key), "pA", "P1")
+            mm(T.P1[:, j:256:16], T.Wr[:, r] if r else Ib, T.Sh[:, j:256:16], True, True, "Ib Wr%d Sh" % r, "pA", "P1")
 
     dma("y", "dsl", T.S0[:], T.slips[:, :], w="S0")
     dma("y", "dr", T.recb[:], T.rec[:, :], w="recb")
     dma("y", "dk", T.K0[:, O:WT], T.kin[:, :], w="K0")
     dma("y", "dx", T.Xw[:, O:WT], T.wealth[:, :], w="Xw")
 
-    cP, cM, cG, cZ, cW, cT, cK, cD, c1 = [T.col[:, k:k + 1] for k in range(9)]
+    cP, cM, cG, cZ, cW, cT, cK, cD = [T.col[:, k:k + 1] for k in range(8)]
+    A0, torn, B0, B1 = 0, 32, 52, 104
     iota(T.pi[:, 0:2], [[0, 2]], 0, 1, "pi")
     iota(T.Id[:, 0:256], [[1, 256]], 0, 0, "Id0")
     iota(T.Rb[:], [[1, 16], [0, 16]], 0, 0, "Rb")
     iota(T.Id[:, 256:WT], [[1, WT - 256]], 256, 0, "Id")
     for n in ("K0", "Kw", "Vw", "Xw", "Rw"):
         fill(T[n][:, 0:O], 0 if n == "K0" else 32.0, n + "p")
-    fill(T.seg[:], 1.0, "seg")
-    fill(T.A0[:], 0.0, "A0")
-    fill(T.B0[:], 0.0, "mv UB")
-    fill(T.B1[:], 0.0, "c")
-    fill(T.torn[:], 0.0, "torn")
-    fill(T.seg[:, 0:128:16], 0.0, "seg")
+    fill(T.Ax[:], 0.0, "Ax0 Ax1 Ax2 Ax3")
+    fill(T.zero[:], 0.0, "zero")
     cp("v", cP, T.pi[:, 0:1], "pi", "cP")
     ts(T.pi[:, 2:3], T.pi[:, 0:1], 15, A.bitwise_and, "pi", "pm")
-    fill(T.Ax[:], 0.0, "Ax0 Ax1 Ax2 Ax3")
     ts(Ib, T.Id[:, 0:128], cP, A.is_equal, "Id0 cP", "Ib")
     cp("v", cM, T.pi[:, 2:3], "pm", "cM")
     for k in range(2):
         cp("v", T.Wc[:, :, 16 * k:16 * k + 16], Ib, "Ib", "Wc%d" % k)
     for r in range(1, 16):
-        cp("s" if r % 2 == 0 else "v", T.Wr[:, r], T.Wc[:, :, r:r + 16], "Wc0 Wc1", "Wr%d" % r)
+        cp("s" if r % 3 == 0 else "v", T.Wr[:, r], T.Wc[:, :, r:r + 16], "Wc0 Wc1", "Wr%d" % r)
     ts(T.Sh[:], T.S0[:], float(O), A.add, "S0", "Sh")
-    rotate(T.Sh, "Sh", False)
+    rotate(False)
     for k in range(4):
         cp("v", T.Ax[:, k, :, k % 2, :], T.Ib[:, :, k // 2, :], "Ib", "Ax%d" % k)
-    ts(T.E16[:], T.Id[:, 0:16], cM, A.is_equal, "Id0 cM", "E16")
+    fill(T.Z[:], 0.0, "inst torn mv UB c")
     tt(cZ, cP, cM, A.subtract, "cP cM", "cZ")
     cp("v", T.Si[:], T.P1[:, 0:256], "pA", "Si", "P1")
     turn(T.St[:], T.Si[:], "Si", "St")
-    swap(T.St, "St")
+    swap()
     ts(T.Dm[:], T.Rb[:], cM, A.is_equal, "Rb cM", "Dm")
     cp("v", T.cu0[:], PK[:, 0:8, :, 0], "pK", "cu0", "P3")
     send(T.rcv0[:], T.cu0[:], "rl0", T.cores[(rank + 1) % 6], "cu0")
-    cp("v", T.B1[:, 5:52:3], PK[:, 0:8, :, 0], "pK", "c", "P3")
+    c = T.Z[:, B1 + 5:B1 + 52:3]
+    cp("v", c, PK[:, 0:8, :, 0], "pK", "c", "P3")
     cp("v", T.SL[:], PK[:, 0:8], "pK", "SL", "P3")
-    iota(T.Cm[:], [[0, 8], [-1, 16]], 15, 0, "Cm")
+    iota(T.Cm[:], [[0, 16], [-1, 16]], 15, 0, "Cm")
+    iota(T.Rj[:], [[0, 16], [1, 16]], 0, 0, "Rj")
+    for n in range(NR - 1):
+        select(T.LT[:, n], Ib, [[0, 8], [1, 16]], A.is_equal, 0.0, -n, 0, "Ib", "LT%d" % n)
+        select(T.ND[:, n], Ib, [[0, 8], [1, 16]], A.not_equal, 0.0, -n, 0, "Ib", "ND%d" % n)
+        select(T.Iv[:, n], T.zero[:], [[-1, 128]], A.not_equal, power(8 + n), 0, 1, "zero", "Iv%d" % n)
     act(cW, cM, F.Exp, "cM", "cW", scale=-math.log(4.0))
     act(T.Vw[:, O:WT], T.recb[:], F.Exp, "recb Vwp", "Vw", scale=4.0, bias=3.0)
-    ts(cG, cZ, 1.0 / 16, A.mult, "cZ", "cG")
-    ts(cZ, cZ, 15.0, A.add, "cZ", "cZ")
-    ts(cD, cM, float(WT), A.add, "cM", "cD")
-    ts(cK, cM, 16.0, A.mult, "cM", "cK", s2=7.5, o1=A.add)
     ts(T.NDH[:], T.Dm[:], -9e28, A.mult, "Dm", "NDH", s2=9e28, o1=A.add)
-    ts(T.nE[:], T.E16[:], -1.0, A.mult, "E16", "nE", s2=1.0, o1=A.add)
-    ts(T.Zw[:], T.Id[:, 0:144], cZ, A.is_equal, "Id0 cZ", "Zw")
-    ts(T.Z16[:], T.Id[:, 0:144], cZ, A.is_equal, "Id0 cZ", "Z16", s2=16.0, o1=A.mult)
+    ts(cG, cZ, 1.0 / 16, A.mult, "cZ", "cG")
+    ts(cD, cM, float(WT), A.add, "cM", "cD")
     ts(T.BO4[:], T.Rb[:, 0:128], cG, A.is_equal, "Rb cG", "BO4", s2=4.0, o1=A.mult)
     ts(T.W4[:], T.Rb[:, 0:128], cG, A.is_equal, "Rb cG cW", "W4", s2=cW, o1=A.mult)
-    ts(cT, cW, 32.0, A.mult, "cW", "cT")
     ts(T.A1[:, 1:32:2], T.Id[:, 0:256:16], cD, A.add, "Id0 cD", "dum")
-    ts(T.offs[:, 0:1], cM, 16.0, A.mult, "cM", "off0")
-    ts(T.bas[:], T.Id[:, 0:8], cK, A.add, "Id0 cK", "bas", s2=-7.5, o1=A.add)
-    ts(T.sm[:, 0:8], T.Id[:, 0:8], 0.0, A.mult, "Id0 cM", "h", s2=cM, o1=A.add)
-    ts(T.RL[:], T.sm[:, 0:8], 2.0, A.mult, "h", "RL", s2=1.0, o1=A.add)
-    for t in range(4):
-        ts(T.LT[:, t], Ib, T.E16[:, t:t + 1], A.mult, "Ib E16", "LT%d" % t)
-        ts(T.ND[:, t], Ib, T.nE[:, t:t + 1], A.mult, "Ib nE", "ND%d" % t)
-    for t in range(NR):
-        act(T.DTH[:, t], T.NDH[:], F.Silu, "NDH", "DTH%d" % t, bias=0.8 * power(8 + t - 3))
-    for t in range(4):
-        act(T.Iv[:, t], T.Ib[:], F.Copy, "Ib", "Iv%d" % t, scale=power(8 + t))
-    act(T.D12[:], T.Dm[:], F.Copy, "Dm", "D12", scale=12.0)
 
-    c = T.B1[:, 5:52:3]
-    inst, dum = T.A0[:, 1:32:2], T.A1[:, 1:32:2]
-    Pc, Pf, Po, Py = T.P6[:, 0:16], T.P6[:, 32:48], T.P6[:, 48:64], T.P6[:, 64:65]
-    XALL = " ".join("XCr%d" % m for m in range(16))
+    def late_constants():
+        ts(cZ, cZ, 15.0, A.add, "cZ", "cZ")
+        ts(cK, cM, 16.0, A.mult, "cM", "cK", s2=7.5, o1=A.add)
+        ts(T.Gs[:], T.Id[:, 0:8], cG, A.is_equal, "Id0 cG", "Gs", s2=16.0, o1=A.mult)
+        ts(T.Zw[:], T.Id[:, 0:144], cZ, A.is_equal, "Id0 cZ", "Zw")
+        ts(T.G1[:], T.Id[:, 0:8], cG, A.is_equal, "Id0 cG", "G1")
+        ts(T.RL2[:], T.Id[:, 0:256:16], 15.0, A.add, "Id0", "RL2")
+        ts(cT, cW, 32.0, A.mult, "cW", "cT")
+        ts(T.offs[:, 0:1], cM, 16.0, A.mult, "cM", "off0")
+        ts(T.bas[:], T.Id[:, 0:8], cK, A.add, "Id0 cK", "bas", s2=-7.5, o1=A.add)
+        ts(T.sm[:, 0:8], T.Id[:, 0:8], 0.0, A.mult, "Id0 cM", "h", s2=cM, o1=A.add)
+        ts(T.K16[:], T.Id[:, 0:32], LA / 16.0, A.is_lt, "Id0", "K16", s2=16.0, o1=A.mult)
+        ts(T.RL[:], T.sm[:, 0:8], 2.0, A.mult, "h", "RL", s2=1.0, o1=A.add)
+        fill(T.seg[:], 1.0, "seg")
+        ts(T.E[:], T.Rj[:], cM, A.is_equal, "Rj cM", "E")
+        fill(T.seg[:, 0:256:16], 0.0, "seg")
+
+    def constants(n):
+        act(T.DTH[:, n], T.NDH[:], F.Silu, "NDH", "DTH%d" % n, bias=0.8 * power(8 + n - 3))
+        if n == NR - 1:
+            act(T.D12[:], T.Dm[:], F.Copy, "Dm", "D12", scale=12.0)
+
+    inst, dum = T.Z[:, A0 + 1:A0 + 32:2], T.A1[:, 1:32:2]
+    Pc, Pf, Po, Py, Pb = T.P6[:, 0:16], T.P6[:, 32:48], T.P6[:, 48:64], T.P1[:, 256:257], T.P7[:, 0:16]
+    SUMS = ((T.P0, 0, 0, LA, "pS", "P0"), (T.P5, 256, LA, 256, "pT", "P5"))
     for t in range(NR):
-        last = t == NR - 1
+        first, last = t == 0, t == NR - 1
         cu, rcv, scl, rep, rrv = [T["%s%d" % (n, t)] for n in ("cu", "rcv", "scl", "rep", "rrv")]
         cuk, rcvk, sclk, repk, rrvk = ["%s%d" % (n, t) for n in ("cu", "rcv", "scl", "rep", "rrv")]
         p = T.cores[(rank - 1 - t % 5) % 6]
         lastw[rcvk] = ("rl%d" % t, 8)
         lastw[rrvk] = ("rr%d" % t, 8)
-        KB = ("P2", "P7")
+        ASK = ASKF if first else ASKL if last else ASKS
 
         def kin(out, lst, r, w):
-            if t == 0:
+            if first:
                 ts(out, T.K0[:].indirect(lst), float(O), A.add, "K0 K0p " + r, w)
             else:
                 ts(out, T.Kw[:, 0:WT].indirect(lst), 0.25, A.add, "Kw " + r, w)
 
         def ask(k):
             a, b = ASK[k]
-            cp("v" if k in ASKV else "s", T.Vq[:, 16 * a:16 * b], T.Vw[:, 0:WT].indirect(T.kcq[:, a:b]), "Vw kcq", "Vq%d" % k)
+            cp("s" if k else "v", T.Vq[:, 16 * a:16 * b], T.Vw[:, 0:WT].indirect(T.kcq[:, a:b]), "Vw kcq", "Vq%d" % k)
 
         def ask_mm(k):
             a, b = ASK[k]
             for m in range(16):
-                mm(T.P1[:, a:b], T.Ib[:], T.Vq[:, 16 * a + m:16 * b:16], m == 0, m == 15, "Ib Vq%d" % k, "pA", "P1")
+                mm(T.P1[:, a:b], Ib, T.Vq[:, 16 * a + m:16 * b:16], m == 0, m == 15, "Ib Vq%d" % k, "pA", "P1")
 
         def own(k):
             a, b = OWN[k]
             cp("s", T.Vg[:, 16 * a:16 * b], T.Vw[:, 0:WT].indirect(T.kc[:, a:b]), "Vw kc", "Vg%d" % k)
 
+        def add(x, a, b, rhs, start, stop, r):
+            P, o, _, _, key, bk = SUMS[x]
+            mm(P[:, o + a:o + b], Ib, rhs, start, stop, "Ib " + r, key, bk)
+
         def own_mm(k):
             a, b = OWN[k]
+            x = 1 if a == LA else 0
+            if a in (0, LA):
+                add(x, a, SUMS[x][3], T.VC[:, a:SUMS[x][3]], True, False, "VC")
             for m in range(16):
-                mm(T.P0[:, a:b], T.Ib[:], T.Vg[:, 16 * a + m:16 * b:16], False, False, "Ib Vg%d" % k, "pS", "P0")
+                add(x, a, b, T.Vg[:, 16 * a + m:16 * b:16], False, False, "Vg%d" % k)
 
-        def wealth(h):
-            for B in range(4 * h, 4 * h + 4):
-                tt(T.Dx[:, B], T.Xw[:].indirect(T.kc[:, 32 * B:32 * B + 32]), T.XCr[:, 512 * B:512 * B + 512], A.max, "Xw kc " + XALL, "Dx%d" % B)
+        def bars(x):
+            P, o, a, b, key, bk = SUMS[x]
+            add(x, a, b, rrv[:, a:b], False, True, rrvk)
+            bar = 0.8 * power(8 + t - 2)
+            tt(T.UU[:, 256 + a:256 + b], P[:, o + a:o + b], T.DTH[:, t, a:b], A.is_ge, key + " DTH%d" % t, "U3%d" % x, bk)
+            if x == 0:
+                act(T.UU[:, a:b], P[:, o + a:o + b], F.Sign, key, "U20", bk, scale=1.0 / bar, bias=-1.0)
+            else:
+                ts(T.UU[:, a:b], P[:, o + a:o + b], bar, A.is_ge, key, "U21", bk, s2=2.0, o1=A.mult)
 
-        def key(h):
-            return T[KB[h]][:, 0:128]
-
-        def kin_mm():
-            for h in range(2):
+        def kins():
+            kin(T.kc[:], cu[:], cuk, "kc")
+            cp("v", T.kc16[:], T.kc[:], "kc", "kc16")
+            tt(T.A1[:, 0:32:2], c, dum, A.subtract, "c dum", "dc")
+            turn(T.kt[:], T.kc16[:], "kc16", "kt")
+            for B in range(8):
                 for z in range(2):
                     for y in range(2):
-                        mm(PK[:, 4 * h + 2 * z:4 * h + 2 * z + 2], T.Ax[:, 2 * z + y], T.kt[:, 4 * h:4 * h + 4, y, :], y == 0, y == 1,
-                           "Ax%d kt" % (2 * z + y), "pK", "P3")
+                        mm(PK[:, 8:16, :, 2 * B + z], T.Ax[:, 2 * z + y], T.kt[:, B, y, :], y == 0, y == 1, "Ax%d kt" % (2 * z + y), "pM", "P3")
 
-        def score_mm(h):
-            mm(key(h), T.Ib[:], T.Cm[:], True, False, "Ib Cm", "pKey%d" % h, KB[h])
-            for j in range(16):
-                for z in range(2):
-                    mm(T[KB[h]][:, 64 * z:64 * z + 64], T.Z16[:, 15 - j:143 - j], T.Dx[:, 4 * h:4 * h + 4, 256 * z + 16 * j:256 * z + 16 * j + 16],
-                       False, j == 15 and z == 1, "Z16 Dx%d" % (4 * h + 3), "pKey%d" % h, KB[h])
+        def equal(b0, b1):
+            for b in range(b0, b1):
+                ts(T.EQ[:, b, 0:256 - 16 * b], T.crow[:, 16 * b:256], T.Z[:, B1 + 5 + 3 * b:B1 + 6 + 3 * b], A.is_equal, "crow c", "EQ%d" % b)
 
-        def best(h):
-            a, b = 128 * h, 128 * h + 128
-            scan(T.y[:, a:b], T.seg[:], key(h), A.mult, A.max, "seg pKey%d" % h, "y%d" % h, KB[h])
-            tt(T.eqn[:, a:b], key(h), T.y[:, a:b], A.is_equal, "pKey%d y%d" % (h, h), "eqn%d" % h, KB[h])
-            tt(T.ek[:, a:b], PK[:, 4 * h:4 * h + 4], T.eqn[:, a:b], A.mult, "pK eqn%d" % h, "ek%d" % h, "P3")
-            ts(T.neq[:, a:b], T.eqn[:, a:b], -1.0, A.mult, "eqn%d" % h, "neq%d" % h, s2=1.0, o1=A.add)
-            scan(T.s2[:, h], T.neq[:, a:b], T.ek[:, a:b], A.mult, A.add, "neq%d ek%d" % (h, h), "s2_%d" % h)
+        def equal_mm():
+            mm(T.P5[:, 0:256], T.W4[:], T.EQ[:, :, 0:16], True, False, "W4 EQ15", "pcnt", "P5")
+            for b in range(15):
+                mm(T.P5[:, 16 * b + 16:256], T.BO4[:], T.EQ[:, b, 16:256 - 16 * b], False, b == 14, "BO4 EQ15", "pcnt", "P5")
 
-        kin(T.kc[:], cu[:], cuk, "kc")
-        cp("s", T.XC[:], T.Xw[:].indirect(cu[:]), "Xw Xwp " + cuk, "XC")
-        if t > 0:
-            scatter(T.Vw[:].indirect(T["scl%d" % (t - 1)][:]), T.nV[:], "nV scl%d" % (t - 1), "Vw")
-        cp("s", T.VC[:], T.Vw[:, 0:WT].indirect(cu[:]), "Vw " + cuk, "VC")
-        for m in range(NG):
-            cp("g", T.XCr[:, m:4096:16], T.XC[:], "XC", "XCr%d" % m)
-        cp("v", T.crow[:], T.Id[:].indirect(cu[:]), "Id Id0 " + cuk, "crow")
-        cp("v", T.kc16[:], T.kc[:], "kc", "kc16")
-        tt(T.A1[:, 0:32:2], c, dum, A.subtract, "c dum", "dc")
-        turn(T.kt[:], T.kc16[:], "kc16", "kt")
-        for b in range(16):
-            ts(T.EQ[:, b, 0:256 - 16 * b], T.crow[:, 16 * b:256], T.B1[:, 5 + 3 * b:6 + 3 * b], A.is_equal, "crow c", "EQ%d" % b)
-        kin(T.kcq[:], rcv[:], rcvk, "kcq")
-        for k in range(PRE):
-            own(k)
-        for k in ASKO:
-            ask(k)
-        kin_mm()
-        mm(T.P0[:, 0:256], T.Ib[:], T.VC[:], True, False, "Ib VC", "pS", "P0")
-        if not last:
+        def riches():
+            cp("s", T.XC[:], T.Xw[:].indirect(cu[:]), "Xw Xwp " + cuk, "XC")
+
+        def new_mm():
             mm(T.P4[:, 0:256], T.ND[:, t], T.kc16[:], True, False, "ND%d kc16" % t, "pnK", "P4")
             mm(T.P4[:, 0:256:2], T.LT[:, t], T.crow[:, 1:256:2], False, False, "LT%d crow" % t, "pnK", "P4")
             mm(T.P4[:, 1:256:2], T.LT[:, t], T.crow[:, 0:256:2], False, True, "LT%d crow" % t, "pnK", "P4")
-            mm(T.P4[:, 256:512], T.Ib[:], T.VC[:], True, False, "Ib VC", "pnV", "P4")
+            mm(T.P4[:, 256:512], Ib, T.VC[:], True, False, "Ib VC", "pnV", "P4")
             mm(T.P4[:, 256:512], T.Iv[:, t], T.Dm[:], False, True, "Iv%d Dm" % t, "pnV", "P4")
-        mm(T.P5[:, 0:256], T.W4[:], T.EQ[:, :, 0:16], True, False, "W4 EQ15", "pcnt", "P5")
-        for b in range(15):
-            mm(T.P5[:, 16 * b + 16:256], T.BO4[:], T.EQ[:, b, 16:256 - 16 * b], False, b == 14, "BO4 EQ15", "pcnt", "P5")
-        for k in range(PRE):
-            own_mm(k)
-        for k in ASKO:
+
+        def score_mm(m0, m1):
+            if m0 == 0:
+                mm(T.P2[:, 0:256], Ib, T.Cm[:], True, False, "Ib Cm", "pKey", "P2")
+            for m in range(m0, m1):
+                for h in range(2):
+                    mm(T.P2[:, 128 * h + m:128 * h + 128:16], T.Dx[:, m, 128 * h:128 * h + 128], T.Gs[:], False, m == 15 and h == 1,
+                       "Gs Dx%d" % m, "pKey", "P2")
+
+        cp("v", T.crow[:], T.Id[:].indirect(cu[:]), "Id Id0 " + cuk, "crow")
+        if first:
+            constants(0)
+            equal(0, 16)
+            kins()
+            late_constants()
+        else:
+            kins()
+            equal(0, EQA)
+        cp("v", T.kts[:], PK[:, 8:16], "pM", "kts", "P3")
+        cp("s", T.VC[:], T.Vw[:, 0:WT].indirect(cu[:]), "Vw " + cuk, "VC")
+        if not first:
+            riches()
+            equal(EQA, EQB)
+        kin(T.kcq[:], rcv[:], rcvk, "kcq")
+        own(0)
+        if first:
+            riches()
+            own(1)
+        for k in range(4):
+            ask(k)
+        if not first:
+            equal(EQB, 16)
+        for h in range(2):
+            mm(PK[:, 4 * h:4 * h + 4], T.kc16[:, 128 * h:128 * h + 128], Ib, True, True, "kc16 Ib", "pK", "P3")
+        if not last:
+            new_mm()
+        own_mm(0)
+        ask_mm(0)
+        equal_mm()
+        for k in range(1, 4):
             ask_mm(k)
-        cp("s", rep[:], T.P1[:, 0:256], "pA", repk, "P1")
-        send(T[rrvk][:], rep[:], "rr%d" % t, p, repk)
-        for m in range(NG, 16):
-            cp("v", T.XCr[:, m:4096:16], T.XC[:], "XC", "XCr%d" % m)
         cp("s", T.cn[:], T.P5[:, 0:256], "pcnt", "cn", "P5")
-        wealth(0)
+        cp("s", rep[:], T.P1[:, 0:256], "pA", repk, "P1")
+        send(rrv[:], rep[:], "rr%d" % t, p, repk)
+        if last:
+            act(T.lnb[:], T.Vw[:, O:WT], F.Ln, "Vw", "lnb", scale=math.exp(-33.0))
+        for m in range(16):
+            tt(T.Dx[:, m], T.Xw[:].indirect(T.kts[:, 16 * m:16 * m + 16]), T.XC[:], A.max, "Xw kts XC", "Dx%d" % m)
         for j in range(16):
             mm(Pc, T.Zw[:, 15 - j:143 - j], T.cn[:, j:256:16], j == 0, j == 15, "Zw cn", "pC", "P6")
-        own(PRE)
-        score_mm(0)
-        own_mm(PRE)
-        wealth(1)
-        for k in range(PRE + 1, len(OWN)):
+        for k in range(2 if first else 1, 4):
             own(k)
-        ts(T.NC[:, 0:16], Pc, cT, A.is_ge, "pC cT", "NC", "P6", s2=-64.0, o1=A.mult)
+        score_mm(0, 8)
+        own_mm(1)
+        score_mm(8, 16)
+        ts(T.NC[:, 0:16], Pc, cT, A.is_ge, "pC cT", "NC", "P6", s2=-128.0, o1=A.mult)
         ts(T.NC[:, 16:32], Pc, cT, A.is_ge, "pC cT", "NC1", "P6")
-        own_mm(PRE + 1)
-        score_mm(1)
-        mm(T.P6[:, 32:64], T.Ib[:], T.NC[:], True, False, "Ib NC NC1", "pF", "P6")
-        for k in range(PRE + 2, len(OWN)):
-            own_mm(k)
-        if t == 0:
+        own_mm(2)
+        mm(T.P6[:, 32:64], Ib, T.K16[:], True, False, "Ib K16", "pF", "P6")
+        mm(T.P6[:, 32:64], Ib, T.NC[:], False, False, "Ib NC NC1", "pF", "P6")
+        if first:
             ts(T.Kw[:, O:WT], T.K0[:, O:WT], float(O), A.add, "K0 Kwp", "Kw")
-        best(0)
-        best(1)
+        if last:
+            ts(T.Rw[:, O:WT], T.lnb[:], 30.0, A.add, "lnb Rwp", "Rw", s2=0.25, o1=A.mult)
+        key = T.P2[:, 0:256]
+        scan(T.y[:], T.seg[:], key, A.mult, A.max, "seg pKey", "y", "P2")
+        if last:
+            tt(T.nR[:], T.Rw[:, 0:WT].indirect(cu[:]), T.D12[:], A.max, "Rw D12 " + cuk, "nR")
+        tt(T.eqn[:], key, T.y[:], A.is_equal, "pKey y", "eqn", "P2")
+        tt(T.ek[:], PK[:, 0:8], T.eqn[:], A.mult, "pK eqn", "ek", "P3")
+        ts(T.neq[:], T.eqn[:], -1.0, A.mult, "eqn", "neq", s2=1.0, o1=A.add)
+        bars(0)
+        own_mm(3)
+        scan(T.s2[:], T.neq[:], T.ek[:], A.mult, A.add, "neq ek", "s2")
         if not last:
             cp("s", T.nK[:], T.P4[:, 0:256], "pnK", "nK", "P4")
             cp("s", T.nV[:], T.P4[:, 256:512], "pnV", "nV", "P4")
-        else:
-            act(T.lnb[:], T.Vw[:, O:WT], F.Ln, "Vw", "lnb", scale=math.exp(-33.0))
-        for z in range(2):
-            bk = T.s2[:, :, 64 * z + 15:64 * z + 64:16]
-            tt(T.B1[:, 4 + 3 * z:51:6], bk, T.B1[:, 5 + 3 * z:52:6], A.subtract, "s2_0 s2_1 c", "d1%d" % z)
-            tt(T.B1[:, 3 + 3 * z:50:6], T.B1[:, 2 + 3 * z:48:6], bk, A.subtract, "s2_0 s2_1 c", "d2%d" % z)
-        mm(T.P0[:, 0:256], T.Ib[:], rrv[:], False, True, "Ib " + rrvk, "pS", "P0")
-        ts(T.UU[:, 0:256], T.P0[:, 0:256], 0.8 * power(8 + t - 2), A.is_ge, "pS", "UU2", "P0")
-        tt(T.UU[:, 256:512], T.P0[:, 0:256], T.DTH[:, t], A.is_ge, "pS DTH%d" % t, "UU3", "P0")
+            constants(t + 1)
+        bars(1)
         for j in range(16):
-            mm(T.P6[:, 32:64], T.Zw[:, 15 - j:143 - j], T.UU[:, j:512:16], False, j == 15, "Zw UU2 UU3", "pF", "P6")
-        if last:
-            ts(T.Rw[:, O:WT], T.lnb[:], 30.0, A.add, "lnb Rwp", "Rw", s2=0.25, o1=A.mult)
+            mm(T.P6[:, 32:64], T.Zw[:, 15 - j:143 - j], T.UU[:, j:512:16], False, j == 15, "Zw U20 U21 U30 U31", "pF", "P6")
+        tt(T.Bx[:], T.s2[:].indirect(T.RL2[:]), T.E[:], A.mult, "s2 RL2 E", "Bx")
+        for h in range(2):
+            mm(T.P7[:, 8 * h:8 * h + 8], T.Bx[:, 128 * h:128 * h + 128], T.G1[:], True, True, "Bx G1", "pB", "P7")
         h, t12, cand = T.sm[:, 0:16], T.sm[:, 16:32], T.sm[:, 32:48]
-        ts(h, Pf, 8.0, A.is_lt, "pF", "h", "P6")
-        ts(t12, Pf, 12.0, A.is_ge, "pF", "t12", "P6")
-        tt(inst, h, Po, A.is_gt, "h pF A0", "inst", "P6")
-        cp("v", T.fi[:, 0:16], Pf, "pF", "fi", "P6")
+        tn, tnext, moved = T.Z[:, torn:torn + 16], T.Z[:, torn + 1:torn + 17], T.Z[:, B0 + 4:B0 + 52:3]
+        ts(h, Pf, 16.0, A.is_lt, "pF", "h", "P6")
+        ts(t12, Pf, 24.0, A.is_ge, "pF", "t12", "P6")
+        tt(inst, h, Po, A.is_gt, "h pF", "inst", "P6")
+        ts(T.fi[:, 0:16], Pf, 0.5, A.mult, "pF", "fi", "P6")
         if not last:
-            cp("s", T.nirep[:], T.A0[:].indirect(T.RL[:]), "inst RL", "nirep")
-            mm(Py, T.Ib[:], T.bas[:, t + 1:t + 2], True, False, "Ib bas", "pY", "P6")
-            mm(Py, T.nirep[:], T.seg[:, 1:2], False, True, "nirep seg", "pY", "P6")
-        scan(T.Ao[:], T.A0[:], T.A1[:], A.mult, A.add, "inst dc dum", "Ao")
-        tt(T.torn[:, 0:16], t12, inst, A.add, "t12 inst", "torn")
-        ts(T.fi[:, 16:32], T.fi[:, 0:16], -31, A.bitwise_and, "fi", "odd")
+            cp("s", T.nirep[:], T.Z[:, A0:A0 + 32].indirect(T.RL[:]), "inst RL", "nirep")
+            mm(Py, Ib, T.bas[:, t + 1:t + 2], True, False, "Ib bas", "pY", "P1")
+            mm(Py, T.nirep[:], T.seg[:, 1:2], False, True, "nirep seg", "pY", "P1")
+        scan(T.Ao[:], T.Z[:, A0:A0 + 32], T.A1[:], A.mult, A.add, "inst dc dum", "Ao")
+        tt(tn, t12, inst, A.add, "t12 inst", "torn")
         cp("v", scl[:], T.Ao[:, 1:32:2], "Ao", sclk)
-        tt(cand, T.fi[:, 16:32], T.torn[:, 0:16], A.is_gt, "odd torn", "cand")
+        ts(T.fi[:, 16:32], T.fi[:, 0:16], -31, A.bitwise_and, "fi", "odd")
         if not last:
             scatter(T.Kw[:].indirect(scl[:]), T.nK[:], "nK " + sclk, "Kw")
-        tt(T.B0[:, 4:52:3], cand, T.torn[:, 1:17], A.mult, "cand torn", "mv")
+            scatter(T.Vw[:].indirect(scl[:]), T.nV[:], "nV " + sclk, "Vw")
+        tt(T.Z[:, B1 + 4:B1 + 51:3], Pb, c, A.subtract, "pB c", "d1", "P7")
+        tt(cand, T.fi[:, 16:32], tn, A.is_gt, "odd torn", "cand")
+        tt(T.Z[:, B1 + 3:B1 + 50:3], T.Z[:, B1 + 2:B1 + 48:3], Pb, A.subtract, "pB c", "d2", "P7")
+        tt(moved, cand, tnext, A.mult, "cand torn", "mv")
         if not last:
-            ts(T.kk[:], Py, cK, A.subtract, "pY cK", "kk", "P6", s2=1.0 / 16, o1=A.mult)
-        tt(T.B0[:, 2:48:3], T.torn[:, 0:16], T.B0[:, 4:52:3], A.add, "torn mv", "UB")
+            ts(T.kk[:], Py, cK, A.subtract, "pY cK", "kk", "P1", s2=1.0 / 16, o1=A.mult)
+        tt(T.Z[:, B0 + 2:B0 + 48:3], tn, moved, A.add, "torn mv", "UB")
         if not last:
-            ts(T.offs[:, 2 * t + 2:2 * t + 3], T.kk[:], -16.0, A.mult, "kk pY", "off%d" % (t + 1), "P6", s2=Py, o1=A.add)
-        scan(T.Bo[:], T.B0[:, 0:48], T.B1[:, 3:51], A.mult, A.add, "mv UB c d10 d11 d20 d21", "Bo")
+            ts(T.offs[:, 2 * t + 2:2 * t + 3], T.kk[:], -16.0, A.mult, "kk pY", "off%d" % (t + 1), "P1", s2=Py, o1=A.add)
+        scan(T.Bo[:], T.Z[:, B0:B0 + 48], T.Z[:, B1 + 3:B1 + 51], A.mult, A.add, "mv UB c d1 d2", "Bo")
         cp("v", T.SL[:].indirect(T.offs[:, 2 * t:2 * t + 1]), T.Bo[:, 2:48:3], "Bo off%d" % t, "SL")
         if not last:
             n = t + 1
@@ -418,16 +455,15 @@ def rank_program(g, core, T, topo):
             send(T["rcv%d" % n][:], T["cu%d" % n][:], "rl%d" % n, T.cores[(rank + 1 + n % 5) % 6], "cu%d" % n)
             cp("v", c, T.SL[:].indirect(T.offs[:, 2 * n:2 * n + 1]), "SL off%d" % n, "c")
         else:
-            cp("v", T.Su[:], T.SL[:], "SL", "Su")
-            swap(T.Su, "Su")
-            tt(T.nR[:], T.Rw[:, 0:WT].indirect(cu[:]), T.D12[:], A.max, "Rw D12 " + cuk, "nR")
+            cp("v", T.St[:], T.SL[:], "SL", "St")
+            swap()
+            cp("v", T.Rw[:].indirect(scl[:]), T.nR[:], "nR " + sclk, "Rw")
+            dma("y", "dout", T.yr[:, :], T.Rw[:, O:WT], r="Rw")
             cp("v", T.Si[:], PK[:, 0:8], "pK", "Si", "P3")
             turn(T.Sh[:], T.Si[:], "Si", "Sh")
-            rotate(T.Sh, "Sh", True)
-            cp("v", T.Rw[:].indirect(scl[:]), T.nR[:], "nR " + sclk, "Rw")
+            rotate(True)
             act(T.ysb[:], T.P1[:, 0:256], F.Copy, "pA", "ysb", "P1", bias=-float(O))
             dma("s", "dout", T.ys[:, :], T.ysb[:], r="ysb")
-            dma("y", "dout", T.yr[:, :], T.Rw[:, O:WT], r="Rw")
     for s in ("v", "s", "t", "g", "dsl", "dk", "dr", "dx", "loc", "dout"):
         wait("g", (s, cnt[s]))
     for t in range(NR):

@@ -4,12 +4,12 @@ from concourse.mybir import dt, AluOpType, AxisListType, ActivationFunctionType
 W, NR, O = 1408, 5, 32
 WT = O + W
 WD = WT + 256
-OWN = ((0, 64), (64, 112), (112, 192), (192, 256))
+OWN = ((0, 96), (96, 128), (128, 192), (192, 256))
 LA = OWN[-1][0]
-ASKS = ((192, 256), (0, 64), (64, 128), (128, 192))
-ASKF = ((232, 256), (0, 80), (80, 160), (160, 232))
-ASKL = ((160, 256), (0, 64), (64, 128), (128, 160))
-EQA, EQB = 8, 10
+NB, MB = 256 - LA, 12
+ASK = ((0, 80), (80, 136), (136, LA), (LA, 256))
+EQA = 10
+H = W // 2
 
 
 def power(r):
@@ -25,20 +25,21 @@ SCRATCH = {
     "recb": sb("bfloat16", W), "lnb": sb("bfloat16", W), "Rw": sb("bfloat16", WD),
     "S0": sb("int32", 256), "Sh": sb("float16", 256), "Si": sb("float16", 256), "St": sb("float16", 8, 2, 16),
     "SL": sb("float32", 256), "ysb": sb("float32", 256),
-    "pi": sb("int32", 4), "col": sb("float32", 16), "bas": sb("bfloat16", 8), "Rb": sb("float32", 256), "Rj": sb("float32", 256),
+    "pi": sb("int32", 4), "col": sb("float32", 16), "bas": sb("bfloat16", 8), "Rb": sb("float32", 256), "Rj": sb("float32", 128),
     "Ib": sb("bfloat16", 4, 2, 16), "Wc": sb("bfloat16", 8, 32), "Wr": sb("bfloat16", 16, 128), "Ax": sb("bfloat16", 4, 4, 2, 16),
-    "zero": sb("bfloat16", 128), "E": sb("bfloat16", 256), "Dm": sb("bfloat16", 256), "D12": sb("bfloat16", 256),
-    "NDH": sb("float32", 256), "DTH": sb("float32", NR, 256), "Iv": sb("bfloat16", 4, 128), "ND": sb("bfloat16", 4, 128),
+    "zero": sb("bfloat16", 256), "E": sb("bfloat16", 128), "Dm": sb("bfloat16", 256), "D12": sb("bfloat16", 256),
+    "NDH": sb("float32", 256), "DTH": sb("float32", 256), "Is": sb("bfloat16", 4, 128), "Iv": sb("bfloat16", 4, 128), "ND": sb("bfloat16", 4, 128),
     "LT": sb("bfloat16", 4, 128), "Zw": sb("bfloat16", 144), "BO4": sb("bfloat16", 128), "W4": sb("bfloat16", 128),
-    "Gs": sb("bfloat16", 8), "G1": sb("bfloat16", 8), "K16": sb("bfloat16", 32), "Cm": sb("bfloat16", 256), "seg": sb("bfloat16", 256),
-    "RL": sb("uint16", 8), "RL2": sb("uint16", 16), "offs": sb("uint16", 16),
-    "kc": sb("uint16", 256), "kcq": sb("uint16", 256), "kts": sb("uint16", 256), "kc16": sb("float16", 256), "kt": sb("float16", 8, 2, 16),
-    "crow": sb("float16", 256), "XC": sb("bfloat16", 256), "VC": sb("bfloat16", 256),
-    "Vg": sb("bfloat16", 4096), "Vq": sb("bfloat16", 4096), "Dx": sb("bfloat16", 16, 256),
-    "EQ": sb("bfloat16", 16, 256), "cn": sb("bfloat16", 256), "NC": sb("bfloat16", 32), "UU": sb("bfloat16", 512),
+    "Gs": sb("bfloat16", 8), "Zj": sb("bfloat16", 240), "In": sb("bfloat16", 128), "K16": sb("bfloat16", 32),
+    "Cm": sb("bfloat16", 256), "seg": sb("bfloat16", 256), "RL": sb("uint16", 8), "RL2": sb("uint16", 8), "offs": sb("uint16", 16),
+    "kc": sb("uint16", 256), "kcq": sb("uint16", 256), "kts": sb("uint16", 256), "ktb": sb("uint16", NB),
+    "kc16": sb("float16", 256), "kt": sb("float16", 8, 2, 16),
+    "crow": sb("float16", 256), "XC": sb("bfloat16", 1024), "VC": sb("bfloat16", 256),
+    "Vg": sb("bfloat16", 4096), "Vq": sb("bfloat16", 4096), "Dx": sb("bfloat16", 4, 1024),
+    "EQ": sb("bfloat16", 16, 256), "cn": sb("bfloat16", 256), "NC": sb("bfloat16", 16), "UU": sb("bfloat16", 512),
     "nK": sb("float32", 256), "nV": sb("float32", 256), "nR": sb("bfloat16", 256),
     "y": sb("float32", 256), "eqn": sb("bfloat16", 256), "neq": sb("bfloat16", 256), "ek": sb("float16", 256), "s2": sb("float32", 256),
-    "Bx": sb("float16", 256), "Z": sb("float32", 160), "A1": sb("float32", 32), "Ao": sb("float32", 32), "Bo": sb("float32", 48),
+    "Bx": sb("float16", 128), "Z": sb("float32", 160), "A1": sb("float32", 32), "Ao": sb("float32", 32), "Bo": sb("float32", 48),
     "sm": sb("float32", 64), "fi": sb("int32", 32), "kk": sb("int32", 1), "nirep": sb("bfloat16", 128),
 }
 for _t in range(NR):
@@ -48,7 +49,8 @@ for _t in range(NR):
         SCRATCH["%s%d" % (_n, _t)] = sb("bfloat16", 256)
 for _k in range(8):
     SCRATCH["P%d" % _k] = ("psum", [128, 16, 2, 16] if _k == 3 else [128, 512], "float32")
-SEMAPHORES = ["v", "s", "t", "g", "dsl", "dk", "dr", "dx", "loc", "dout"] + ["rl%d" % t for t in range(NR)] + ["rr%d" % t for t in range(NR)]
+REMOTE = ["r%s%d" % (x, t) for t in range(NR) for x in "lab"]
+SEMAPHORES = ["v", "s", "t", "g", "dsl", "dk", "dr", "dx", "loc", "dout"] + REMOTE
 
 
 def rank_program(g, core, T, topo):
@@ -186,7 +188,7 @@ def rank_program(g, core, T, topo):
     dma("y", "dk", T.K0[:, O:WT], T.kin[:, :], w="K0")
     dma("y", "dx", T.Xw[:, O:WT], T.wealth[:, :], w="Xw")
 
-    cP, cM, cG, cZ, cW, cT, cK, cD = [T.col[:, k:k + 1] for k in range(8)]
+    cP, cM, cG, cZ, cY, cW, cT, cK, cX, cD, cH = [T.col[:, k:k + 1] for k in range(11)]
     A0, torn, B0, B1 = 0, 32, 52, 104
     iota(T.pi[:, 0:2], [[0, 2]], 0, 1, "pi")
     iota(T.Id[:, 0:256], [[1, 256]], 0, 0, "Id0")
@@ -195,7 +197,6 @@ def rank_program(g, core, T, topo):
     for n in ("K0", "Kw", "Vw", "Xw", "Rw"):
         fill(T[n][:, 0:O], 0 if n == "K0" else 32.0, n + "p")
     fill(T.Ax[:], 0.0, "Ax0 Ax1 Ax2 Ax3")
-    fill(T.zero[:], 0.0, "zero")
     cp("v", cP, T.pi[:, 0:1], "pi", "cP")
     ts(T.pi[:, 2:3], T.pi[:, 0:1], 15, A.bitwise_and, "pi", "pm")
     ts(Ib, T.Id[:, 0:128], cP, A.is_equal, "Id0 cP", "Ib")
@@ -204,12 +205,13 @@ def rank_program(g, core, T, topo):
         cp("v", T.Wc[:, :, 16 * k:16 * k + 16], Ib, "Ib", "Wc%d" % k)
     for r in range(1, 16):
         cp("s" if r % 3 == 0 else "v", T.Wr[:, r], T.Wc[:, :, r:r + 16], "Wc0 Wc1", "Wr%d" % r)
+    fill(T.zero[:], 0.0, "zero")
+    tt(cZ, cP, cM, A.subtract, "cP cM", "cZ")
+    fill(T.Z[:], 0.0, "inst torn mv UB c")
     ts(T.Sh[:], T.S0[:], float(O), A.add, "S0", "Sh")
     rotate(False)
     for k in range(4):
         cp("v", T.Ax[:, k, :, k % 2, :], T.Ib[:, :, k // 2, :], "Ib", "Ax%d" % k)
-    fill(T.Z[:], 0.0, "inst torn mv UB c")
-    tt(cZ, cP, cM, A.subtract, "cP cM", "cZ")
     cp("v", T.Si[:], T.P1[:, 0:256], "pA", "Si", "P1")
     turn(T.St[:], T.Si[:], "Si", "St")
     swap()
@@ -219,54 +221,57 @@ def rank_program(g, core, T, topo):
     c = T.Z[:, B1 + 5:B1 + 52:3]
     cp("v", c, PK[:, 0:8, :, 0], "pK", "c", "P3")
     cp("v", T.SL[:], PK[:, 0:8], "pK", "SL", "P3")
+    iota(T.Rj[:], [[0, 16], [1, 8]], 0, 0, "Rj")
     iota(T.Cm[:], [[0, 16], [-1, 16]], 15, 0, "Cm")
-    iota(T.Rj[:], [[0, 16], [1, 16]], 0, 0, "Rj")
-    for n in range(NR - 1):
-        select(T.LT[:, n], Ib, [[0, 8], [1, 16]], A.is_equal, 0.0, -n, 0, "Ib", "LT%d" % n)
-        select(T.ND[:, n], Ib, [[0, 8], [1, 16]], A.not_equal, 0.0, -n, 0, "Ib", "ND%d" % n)
-        select(T.Iv[:, n], T.zero[:], [[-1, 128]], A.not_equal, power(8 + n), 0, 1, "zero", "Iv%d" % n)
-    act(cW, cM, F.Exp, "cM", "cW", scale=-math.log(4.0))
-    act(T.Vw[:, O:WT], T.recb[:], F.Exp, "recb Vwp", "Vw", scale=4.0, bias=3.0)
-    ts(T.NDH[:], T.Dm[:], -9e28, A.mult, "Dm", "NDH", s2=9e28, o1=A.add)
-    ts(cG, cZ, 1.0 / 16, A.mult, "cZ", "cG")
-    ts(cD, cM, float(WT), A.add, "cM", "cD")
-    ts(T.BO4[:], T.Rb[:, 0:128], cG, A.is_equal, "Rb cG", "BO4", s2=4.0, o1=A.mult)
-    ts(T.W4[:], T.Rb[:, 0:128], cG, A.is_equal, "Rb cG cW", "W4", s2=cW, o1=A.mult)
-    ts(T.A1[:, 1:32:2], T.Id[:, 0:256:16], cD, A.add, "Id0 cD", "dum")
-
-    def late_constants():
-        ts(cZ, cZ, 15.0, A.add, "cZ", "cZ")
-        ts(cK, cM, 16.0, A.mult, "cM", "cK", s2=7.5, o1=A.add)
-        ts(T.Gs[:], T.Id[:, 0:8], cG, A.is_equal, "Id0 cG", "Gs", s2=16.0, o1=A.mult)
-        ts(T.Zw[:], T.Id[:, 0:144], cZ, A.is_equal, "Id0 cZ", "Zw")
-        ts(T.G1[:], T.Id[:, 0:8], cG, A.is_equal, "Id0 cG", "G1")
-        ts(T.RL2[:], T.Id[:, 0:256:16], 15.0, A.add, "Id0", "RL2")
-        ts(cT, cW, 32.0, A.mult, "cW", "cT")
-        ts(T.offs[:, 0:1], cM, 16.0, A.mult, "cM", "off0")
-        ts(T.bas[:], T.Id[:, 0:8], cK, A.add, "Id0 cK", "bas", s2=-7.5, o1=A.add)
-        ts(T.sm[:, 0:8], T.Id[:, 0:8], 0.0, A.mult, "Id0 cM", "h", s2=cM, o1=A.add)
-        ts(T.K16[:], T.Id[:, 0:32], LA / 16.0, A.is_lt, "Id0", "K16", s2=16.0, o1=A.mult)
-        ts(T.RL[:], T.sm[:, 0:8], 2.0, A.mult, "h", "RL", s2=1.0, o1=A.add)
-        fill(T.seg[:], 1.0, "seg")
-        ts(T.E[:], T.Rj[:], cM, A.is_equal, "Rj cM", "E")
-        fill(T.seg[:, 0:256:16], 0.0, "seg")
+    select(T.seg[:], T.zero[:], [[0, 16], [1, 16]], A.is_equal, 1.0, 0, 0, "zero", "seg")
+    select(T.K16[:], T.zero[:, 0:32], [[1, 32]], A.is_ge, 16.0, -(LA // 16), 0, "zero", "K16")
+    select(T.In[:], T.zero[:, 0:128], [[-1, 128]], A.not_equal, -128.0, 0, 1, "zero", "In")
 
     def constants(n):
-        act(T.DTH[:, n], T.NDH[:], F.Silu, "NDH", "DTH%d" % n, bias=0.8 * power(8 + n - 3))
-        if n == NR - 1:
-            act(T.D12[:], T.Dm[:], F.Copy, "Dm", "D12", scale=12.0)
+        if n > 0:
+            select(T.Is[:, n - 1], T.zero[:, 0:128], [[-1, 128]], A.not_equal, math.exp(-4.0 * n), 0, 1, "zero", "Is%d" % n)
+        if n < NR - 1:
+            select(T.LT[:, n], Ib, [[0, 8], [1, 16]], A.is_equal, 0.0, -n, 0, "Ib", "LT%d" % n)
+            select(T.ND[:, n], Ib, [[0, 8], [1, 16]], A.not_equal, 0.0, -n, 0, "Ib", "ND%d" % n)
+            select(T.Iv[:, n], T.zero[:, 0:128], [[-1, 128]], A.not_equal, power(8 + n), 0, 1, "zero", "Iv%d" % n)
+
+    constants(0)
+    constants(1)
+    act(cW, cM, F.Exp, "cM", "cW", scale=-math.log(4.0))
+    for col, name, src, key, scale, bias in ((cG, "cG", cZ, "cZ", 1.0 / 16, 0.0), (cY, "cY", cZ, "cZ", 1.0, 15.0), (cD, "cD", cM, "cM", 1.0, float(WT)),
+                                             (cK, "cK", cM, "cM", 16.0, 7.5), (cX, "cX", cM, "cM", 16.0, 0.0), (cT, "cT", cW, "cW", 32.0, 0.0)):
+        act(col, src, F.Copy, key, name, scale=scale, bias=bias)
+    act(T.Vw[:, O:WT], T.recb[:], F.Exp, "recb Vwp", "Vw", scale=4.0, bias=3.0)
+    act(T.NDH[:], T.Dm[:], F.Copy, "Dm", "NDH", scale=-9e28, bias=9e28)
+    act(T.A1[:, 1:32:2], T.Id[:, 0:256:16], F.Identity, "Id0 cD", "dum", bias=cD)
+    act(T.bas[:], T.Id[:, 0:8], F.Identity, "Id0 cX", "bas", bias=cX)
+    act(T.sm[:, 0:8], T.Id[:, 0:8], F.Identity, "Id0 cM", "h", scale=0.0, bias=cM)
+    ts(T.BO4[:], T.Rb[:, 0:128], cG, A.is_equal, "Rb cG", "BO4", s2=4.0, o1=A.mult)
+    ts(T.W4[:], T.Rb[:, 0:128], cG, A.is_equal, "Rb cG cW", "W4", s2=cW, o1=A.mult)
+
+    def late_constants():
+        ts(cH, cM, 8.0, A.is_ge, "cM", "cH", s2=128.0, o1=A.mult)
+        ts(T.Gs[:], T.Id[:, 0:8], cG, A.is_equal, "Id0 cG", "Gs", s2=16.0, o1=A.mult)
+        ts(T.Zw[:], T.Id[:, 0:144], cY, A.is_equal, "Id0 cY", "Zw")
+        ts(T.Zj[:], T.Id[:, 0:240], -112.0, A.add, "Id0 cM", "Zj", s2=cM, o1=A.is_equal)
+        ts(T.RL2[:], T.Id[:, 15:128:16], cH, A.add, "Id0 cH", "RL2")
+        cp("v", T.offs[:, 0:1], cX, "cX", "off0")
+        ts(T.RL[:], T.sm[:, 0:8], 2.0, A.mult, "h", "RL", s2=1.0, o1=A.add)
+        ts(T.E[:], T.Rj[:], cG, A.is_equal, "Rj cG", "E")
+
+    act(T.DTH[:], T.NDH[:], F.Silu, "NDH", "DTH", bias=0.8 * power(5))
 
     inst, dum = T.Z[:, A0 + 1:A0 + 32:2], T.A1[:, 1:32:2]
     Pc, Pf, Po, Py, Pb = T.P6[:, 0:16], T.P6[:, 32:48], T.P6[:, 48:64], T.P1[:, 256:257], T.P7[:, 0:16]
     SUMS = ((T.P0, 0, 0, LA, "pS", "P0"), (T.P5, 256, LA, 256, "pT", "P5"))
+    ASKED = ((T.P1, "pA", "P1"), (T.P7, "pQ", "P7"))
     for t in range(NR):
         first, last = t == 0, t == NR - 1
         cu, rcv, scl, rep, rrv = [T["%s%d" % (n, t)] for n in ("cu", "rcv", "scl", "rep", "rrv")]
-        cuk, rcvk, sclk, repk, rrvk = ["%s%d" % (n, t) for n in ("cu", "rcv", "scl", "rep", "rrv")]
+        cuk, sclk = "cu%d" % t, "scl%d" % t
         p = T.cores[(rank - 1 - t % 5) % 6]
-        lastw[rcvk] = ("rl%d" % t, 8)
-        lastw[rrvk] = ("rr%d" % t, 8)
-        ASK = ASKF if first else ASKL if last else ASKS
+        for x in "lab":
+            lastw["r" + x] = ("r%s%d" % (x, t), 8)
 
         def kin(out, lst, r, w):
             if first:
@@ -280,16 +285,27 @@ def rank_program(g, core, T, topo):
 
         def ask_mm(k):
             a, b = ASK[k]
+            P, key, bk = ASKED[k // 3]
             for m in range(16):
-                mm(T.P1[:, a:b], Ib, T.Vq[:, 16 * a + m:16 * b:16], m == 0, m == 15, "Ib Vq%d" % k, "pA", "P1")
+                mm(P[:, a:b], Ib, T.Vq[:, 16 * a + m:16 * b:16], m == 0, m == 15, "Ib Vq%d" % k, key, bk)
+
+        def reply(x):
+            a, b = SUMS[x][2:4]
+            P, key, bk = ASKED[x]
+            cp("s", rep[:, a:b], P[:, a:b], key, "rep%d%d" % (t, x), bk)
+            send(rrv[:, a:b], rep[:, a:b], "r%s%d" % ("ab"[x], t), p, "rep%d%d" % (t, x))
 
         def own(k):
             a, b = OWN[k]
-            cp("s", T.Vg[:, 16 * a:16 * b], T.Vw[:, 0:WT].indirect(T.kc[:, a:b]), "Vw kc", "Vg%d" % k)
+            if a < LA:
+                cp("s", T.Vg[:, 16 * a:16 * b], T.Vw[:, 0:WT].indirect(T.kc[:, a:b]), "Vw kc", "Vg%d" % k)
+                return
+            for x, y in ((0, MB), (MB, 16)):
+                cp("s", T.Vg[:, 16 * a + NB * x:16 * a + NB * y], T.Vw[:, 0:WT].indirect(T.ktb[:, NB // 16 * x:NB // 16 * y]), "Vw ktb", "Vh%d" % x)
 
         def add(x, a, b, rhs, start, stop, r):
             P, o, _, _, key, bk = SUMS[x]
-            mm(P[:, o + a:o + b], Ib, rhs, start, stop, "Ib " + r, key, bk)
+            mm(P[:, o + a:o + b], T.Is[:, t - 1] if t else Ib, rhs, start, stop, "Ib Is%d %s" % (t, r), key, bk)
 
         def own_mm(k):
             a, b = OWN[k]
@@ -297,17 +313,20 @@ def rank_program(g, core, T, topo):
             if a in (0, LA):
                 add(x, a, SUMS[x][3], T.VC[:, a:SUMS[x][3]], True, False, "VC")
             for m in range(16):
-                add(x, a, b, T.Vg[:, 16 * a + m:16 * b:16], False, False, "Vg%d" % k)
+                if x:
+                    add(x, a, b, T.Vg[:, 16 * a + NB * m:16 * a + NB * (m + 1)], False, False, "Vh%d" % (0 if m < MB else MB))
+                else:
+                    add(x, a, b, T.Vg[:, 16 * a + m:16 * b:16], False, False, "Vg%d" % k)
 
         def bars(x):
             P, o, a, b, key, bk = SUMS[x]
-            add(x, a, b, rrv[:, a:b], False, True, rrvk)
-            bar = 0.8 * power(8 + t - 2)
-            tt(T.UU[:, 256 + a:256 + b], P[:, o + a:o + b], T.DTH[:, t, a:b], A.is_ge, key + " DTH%d" % t, "U3%d" % x, bk)
+            add(x, a, b, rrv[:, a:b], False, True, "r" + "ab"[x])
+            bar = 0.8 * power(6)
             if x == 0:
                 act(T.UU[:, a:b], P[:, o + a:o + b], F.Sign, key, "U20", bk, scale=1.0 / bar, bias=-1.0)
             else:
                 ts(T.UU[:, a:b], P[:, o + a:o + b], bar, A.is_ge, key, "U21", bk, s2=2.0, o1=A.mult)
+            tt(T.UU[:, 256 + a:256 + b], P[:, o + a:o + b], T.DTH[:, a:b], A.is_ge, key + " DTH", "U3%d" % x, bk)
 
         def kins():
             kin(T.kc[:], cu[:], cuk, "kc")
@@ -329,7 +348,11 @@ def rank_program(g, core, T, topo):
                 mm(T.P5[:, 16 * b + 16:256], T.BO4[:], T.EQ[:, b, 16:256 - 16 * b], False, b == 14, "BO4 EQ15", "pcnt", "P5")
 
         def riches():
-            cp("s", T.XC[:], T.Xw[:].indirect(cu[:]), "Xw Xwp " + cuk, "XC")
+            cp("s", T.XC[:, 0:256], T.Xw[:].indirect(cu[:]), "Xw Xwp " + cuk, "XC")
+            for n in (256, 512):
+                select(T.XC[:, n:2 * n], T.XC[:, 0:n], [[0, n]], A.is_gt, 0.0, 1, 0, "XC", "XC")
+            if 0 < t < NR - 1:
+                constants(t + 1)
 
         def new_mm():
             mm(T.P4[:, 0:256], T.ND[:, t], T.kc16[:], True, False, "ND%d kc16" % t, "pnK", "P4")
@@ -343,48 +366,47 @@ def rank_program(g, core, T, topo):
                 mm(T.P2[:, 0:256], Ib, T.Cm[:], True, False, "Ib Cm", "pKey", "P2")
             for m in range(m0, m1):
                 for h in range(2):
-                    mm(T.P2[:, 128 * h + m:128 * h + 128:16], T.Dx[:, m, 128 * h:128 * h + 128], T.Gs[:], False, m == 15 and h == 1,
-                       "Gs Dx%d" % m, "pKey", "P2")
+                    a = 256 * (m % 4) + 128 * h
+                    mm(T.P2[:, 128 * h + m:128 * h + 128:16], T.Dx[:, m // 4, a:a + 128], T.Gs[:], False, m == 15 and h == 1,
+                       "Gs Dx%d" % (m // 4), "pKey", "P2")
 
         cp("v", T.crow[:], T.Id[:].indirect(cu[:]), "Id Id0 " + cuk, "crow")
         if first:
-            constants(0)
             equal(0, 16)
-            kins()
             late_constants()
+            kins()
+            ts(T.Kw[:, O:WT], T.K0[:, O:WT], float(O), A.add, "K0 Kwp", "Kw")
         else:
             kins()
             equal(0, EQA)
         cp("v", T.kts[:], PK[:, 8:16], "pM", "kts", "P3")
+        cp("v", T.ktb[:], PK[:, 8:16, :, LA // 16:16], "pM", "ktb", "P3")
         cp("s", T.VC[:], T.Vw[:, 0:WT].indirect(cu[:]), "Vw " + cuk, "VC")
         if not first:
             riches()
-            equal(EQA, EQB)
-        kin(T.kcq[:], rcv[:], rcvk, "kcq")
+            equal(EQA, 16)
+        kin(T.kcq[:], rcv[:], "rl", "kcq")
         own(0)
         if first:
             riches()
             own(1)
         for k in range(4):
             ask(k)
-        if not first:
-            equal(EQB, 16)
         for h in range(2):
             mm(PK[:, 4 * h:4 * h + 4], T.kc16[:, 128 * h:128 * h + 128], Ib, True, True, "kc16 Ib", "pK", "P3")
         if not last:
             new_mm()
-        own_mm(0)
-        ask_mm(0)
         equal_mm()
-        for k in range(1, 4):
-            ask_mm(k)
+        own_mm(0)
+        ask_mm(1)
+        ask_mm(0)
+        ask_mm(2)
+        reply(0)
+        ask_mm(3)
         cp("s", T.cn[:], T.P5[:, 0:256], "pcnt", "cn", "P5")
-        cp("s", rep[:], T.P1[:, 0:256], "pA", repk, "P1")
-        send(rrv[:], rep[:], "rr%d" % t, p, repk)
-        if last:
-            act(T.lnb[:], T.Vw[:, O:WT], F.Ln, "Vw", "lnb", scale=math.exp(-33.0))
-        for m in range(16):
-            tt(T.Dx[:, m], T.Xw[:].indirect(T.kts[:, 16 * m:16 * m + 16]), T.XC[:], A.max, "Xw kts XC", "Dx%d" % m)
+        reply(1)
+        for k in range(4):
+            tt(T.Dx[:, k], T.Xw[:].indirect(T.kts[:, 64 * k:64 * k + 64]), T.XC[:], A.max, "Xw kts XC", "Dx%d" % k)
         for j in range(16):
             mm(Pc, T.Zw[:, 15 - j:143 - j], T.cn[:, j:256:16], j == 0, j == 15, "Zw cn", "pC", "P6")
         for k in range(2 if first else 1, 4):
@@ -392,35 +414,36 @@ def rank_program(g, core, T, topo):
         score_mm(0, 8)
         own_mm(1)
         score_mm(8, 16)
-        ts(T.NC[:, 0:16], Pc, cT, A.is_ge, "pC cT", "NC", "P6", s2=-128.0, o1=A.mult)
-        ts(T.NC[:, 16:32], Pc, cT, A.is_ge, "pC cT", "NC1", "P6")
+        ts(T.NC[:], Pc, cT, A.is_ge, "pC cT", "NC", "P6")
         own_mm(2)
         mm(T.P6[:, 32:64], Ib, T.K16[:], True, False, "Ib K16", "pF", "P6")
-        mm(T.P6[:, 32:64], Ib, T.NC[:], False, False, "Ib NC NC1", "pF", "P6")
-        if first:
-            ts(T.Kw[:, O:WT], T.K0[:, O:WT], float(O), A.add, "K0 Kwp", "Kw")
-        if last:
-            ts(T.Rw[:, O:WT], T.lnb[:], 30.0, A.add, "lnb Rwp", "Rw", s2=0.25, o1=A.mult)
+        mm(Pf, T.In[:], T.NC[:], False, False, "In NC", "pF", "P6")
+        mm(Po, Ib, T.NC[:], False, False, "Ib NC", "pF", "P6")
         key = T.P2[:, 0:256]
         scan(T.y[:], T.seg[:], key, A.mult, A.max, "seg pKey", "y", "P2")
-        if last:
-            tt(T.nR[:], T.Rw[:, 0:WT].indirect(cu[:]), T.D12[:], A.max, "Rw D12 " + cuk, "nR")
         tt(T.eqn[:], key, T.y[:], A.is_equal, "pKey y", "eqn", "P2")
         tt(T.ek[:], PK[:, 0:8], T.eqn[:], A.mult, "pK eqn", "ek", "P3")
-        ts(T.neq[:], T.eqn[:], -1.0, A.mult, "eqn", "neq", s2=1.0, o1=A.add)
         bars(0)
+        if last:
+            ts(T.neq[:], T.eqn[:], -1.0, A.mult, "eqn", "neq", s2=1.0, o1=A.add)
+        else:
+            act(T.neq[:], T.eqn[:], F.Copy, "eqn", "neq", scale=-1.0, bias=1.0)
         own_mm(3)
-        scan(T.s2[:], T.neq[:], T.ek[:], A.mult, A.add, "neq ek", "s2")
         if not last:
             cp("s", T.nK[:], T.P4[:, 0:256], "pnK", "nK", "P4")
             cp("s", T.nV[:], T.P4[:, 256:512], "pnV", "nV", "P4")
-            constants(t + 1)
+            if first:
+                act(T.D12[:], T.Dm[:], F.Copy, "Dm", "D12", scale=12.0)
+        else:
+            for k in range(2):
+                act(T.lnb[:, k * H:k * H + H], T.Vw[:, O + k * H:O + k * H + H], F.Ln, "Vw", "lnb%d" % k, scale=math.exp(-33.0))
         bars(1)
         for j in range(16):
             mm(T.P6[:, 32:64], T.Zw[:, 15 - j:143 - j], T.UU[:, j:512:16], False, j == 15, "Zw U20 U21 U30 U31", "pF", "P6")
+        scan(T.s2[:], T.neq[:], T.ek[:], A.mult, A.add, "neq ek", "s2")
         tt(T.Bx[:], T.s2[:].indirect(T.RL2[:]), T.E[:], A.mult, "s2 RL2 E", "Bx")
-        for h in range(2):
-            mm(T.P7[:, 8 * h:8 * h + 8], T.Bx[:, 128 * h:128 * h + 128], T.G1[:], True, True, "Bx G1", "pB", "P7")
+        for k in range(8):
+            mm(Pb, T.Zj[:, 112 - 16 * k:240 - 16 * k], T.Bx[:, 16 * k:16 * k + 16], k == 0, k == 7, "Bx Zj", "pB", "P7")
         h, t12, cand = T.sm[:, 0:16], T.sm[:, 16:32], T.sm[:, 32:48]
         tn, tnext, moved = T.Z[:, torn:torn + 16], T.Z[:, torn + 1:torn + 17], T.Z[:, B0 + 4:B0 + 52:3]
         ts(h, Pf, 16.0, A.is_lt, "pF", "h", "P6")
@@ -457,15 +480,18 @@ def rank_program(g, core, T, topo):
         else:
             cp("v", T.St[:], T.SL[:], "SL", "St")
             swap()
-            cp("v", T.Rw[:].indirect(scl[:]), T.nR[:], "nR " + sclk, "Rw")
-            dma("y", "dout", T.yr[:, :], T.Rw[:, O:WT], r="Rw")
-            cp("v", T.Si[:], PK[:, 0:8], "pK", "Si", "P3")
-            turn(T.Sh[:], T.Si[:], "Si", "Sh")
-            rotate(True)
+            for k in range(2):
+                ts(T.Rw[:, O + k * H:O + k * H + H], T.lnb[:, k * H:k * H + H], 30.0, A.add, "lnb%d Rwp" % k, "Rw%d" % k, s2=0.25, o1=A.mult)
+                if k == 0:
+                    cp("v", T.Si[:], PK[:, 0:8], "pK", "Si", "P3")
+                    turn(T.Sh[:], T.Si[:], "Si", "Sh")
+                    rotate(True)
             act(T.ysb[:], T.P1[:, 0:256], F.Copy, "pA", "ysb", "P1", bias=-float(O))
             dma("s", "dout", T.ys[:, :], T.ysb[:], r="ysb")
+            tt(T.nR[:], T.Rw[:, 0:WT].indirect(cu[:]), T.D12[:], A.max, "Rw0 Rw1 D12 " + cuk, "nR")
+            cp("v", T.Rw[:].indirect(scl[:]), T.nR[:], "nR " + sclk, "Rw")
+            dma("y", "dout", T.yr[:, :], T.Rw[:, O:WT], r="Rw")
     for s in ("v", "s", "t", "g", "dsl", "dk", "dr", "dx", "loc", "dout"):
         wait("g", (s, cnt[s]))
-    for t in range(NR):
-        wait("g", ("rl%d" % t, 8))
-        wait("g", ("rr%d" % t, 8))
+    for s in REMOTE:
+        wait("g", (s, 8))

import math
from concourse.mybir import dt, AluOpType, AxisListType, ActivationFunctionType

W, NR, O = 1408, 5, 32
WT = O + W
WD = WT + 256
OWN = ((0, 96), (96, 128), (128, 192), (192, 256))
LA = OWN[-1][0]
NB, MB = 256 - LA, 12
ASK = ((0, 80), (80, 136), (136, LA), (LA, 256))
EQA = 10
H = W // 2


def power(r):
    return math.exp(4.0 * r + 3.0)


def sb(dtype, *shape):
    return ("sbuf", [128] + list(shape), dtype)


SCRATCH = {
    "K0": sb("int32", WT), "Kw": sb("float32", WD), "Vw": sb("float32", WD), "Xw": sb("bfloat16", WT), "Id": sb("float32", WT),
    "recb": sb("bfloat16", W), "lnb": sb("bfloat16", W), "Rw": sb("bfloat16", WD),
    "S0": sb("int32", 256), "Sh": sb("float16", 256), "Si": sb("float16", 256), "St": sb("float16", 8, 2, 16),
    "SL": sb("float32", 256), "ysb": sb("float32", 256),
    "pi": sb("int32", 4), "col": sb("float32", 16), "bas": sb("bfloat16", 8), "Rb": sb("float32", 256), "Rj": sb("float32", 128),
    "Ib": sb("bfloat16", 4, 2, 16), "Wc": sb("bfloat16", 8, 32), "Wr": sb("bfloat16", 16, 128), "Ax": sb("bfloat16", 4, 4, 2, 16),
    "zero": sb("bfloat16", 256), "E": sb("bfloat16", 128), "Dm": sb("bfloat16", 256), "D12": sb("bfloat16", 256),
    "NDH": sb("float32", 256), "DTH": sb("float32", 256), "Is": sb("bfloat16", 4, 128), "Iv": sb("bfloat16", 4, 128), "ND": sb("bfloat16", 4, 128),
    "LT": sb("bfloat16", 4, 128), "Zw": sb("bfloat16", 144), "BO4": sb("bfloat16", 128), "W4": sb("bfloat16", 128),
    "Gs": sb("bfloat16", 8), "Zj": sb("bfloat16", 240), "In": sb("bfloat16", 128), "K16": sb("bfloat16", 32),
    "Cm": sb("bfloat16", 256), "seg": sb("bfloat16", 256), "RL": sb("uint16", 8), "RL2": sb("uint16", 8), "offs": sb("uint16", 16),
    "kc": sb("uint16", 256), "kcq": sb("uint16", 256), "kts": sb("uint16", 256), "ktb": sb("uint16", NB),
    "kc16": sb("float16", 256), "kt": sb("float16", 8, 2, 16),
    "crow": sb("float16", 256), "XC": sb("bfloat16", 1024), "VC": sb("bfloat16", 256),
    "Vg": sb("bfloat16", 4096), "Vq": sb("bfloat16", 4096), "Dx": sb("bfloat16", 4, 1024),
    "EQ": sb("bfloat16", 16, 256), "cn": sb("bfloat16", 256), "NC": sb("bfloat16", 16), "UU": sb("bfloat16", 512),
    "nK": sb("float32", 256), "nV": sb("float32", 256), "nR": sb("bfloat16", 256),
    "y": sb("float32", 256), "eqn": sb("bfloat16", 256), "neq": sb("bfloat16", 256), "ek": sb("float16", 256), "s2": sb("float32", 256),
    "Bx": sb("float16", 128), "Z": sb("float32", 160), "A1": sb("float32", 32), "Ao": sb("float32", 32), "Bo": sb("float32", 48),
    "sm": sb("float32", 64), "fi": sb("int32", 32), "kk": sb("int32", 1), "nirep": sb("bfloat16", 128),
}
for _t in range(NR):
    for _n in ("cu", "rcv", "scl"):
        SCRATCH["%s%d" % (_n, _t)] = sb("uint16", 16)
    for _n in ("rep", "rrv"):
        SCRATCH["%s%d" % (_n, _t)] = sb("bfloat16", 256)
for _k in range(8):
    SCRATCH["P%d" % _k] = ("psum", [128, 16, 2, 16] if _k == 3 else [128, 512], "float32")
REMOTE = ["r%s%d" % (x, t) for t in range(NR) for x in "lab"]
SEMAPHORES = ["v", "s", "t", "g", "dsl", "dk", "dr", "dx", "loc", "dout"] + REMOTE


def rank_program(g, core, T, topo):
    rank = T.rank_of(core)
    if rank is None:
        return
    A, F = AluOpType, ActivationFunctionType
    queues = {"v": g.vector, "s": g.scalar, "t": g.tensor, "g": g, "y": g.sync}
    cnt = {}
    seen = {q: {} for q in queues}
    snap = {}
    lastw, readers, bank = {}, {}, {}

    def wait(q, tok):
        sem, val = tok
        if seen[q].get(sem, 0) >= val:
            return
        queues[q].wait_ge(T.sem[sem], val)
        seen[q][sem] = val
        for s, x in snap.get(tok, {}).items():
            if seen[q].get(s, 0) < x:
                seen[q][s] = x

    def deps(q, r, w, bk):
        need = {}

        def add(tok):
            if tok is not None and need.get(tok[0], 0) < tok[1]:
                need[tok[0]] = tok[1]
        for k in r:
            tok = lastw.get(k)
            if tok is not None and not (q == "t" and tok[0] == "t"):
                add(tok)
        for k in w:
            tok = lastw.get(k)
            if tok is not None and not (q == "t" and tok[0] == "t"):
                add(tok)
            for x, tok in readers.get(k, {}).items():
                if x != q:
                    add(tok)
        for b in bk:
            for x, tok in bank.get(b, {}).items():
                if x != q:
                    add(tok)
        for s in sorted(need):
            wait(q, (s, need[s]))

    def note(q, tok, r, w, bk):
        snap[tok] = dict(seen[q])
        for k in r:
            readers.setdefault(k, {})[q] = tok
        for k in w:
            lastw[k] = tok
            readers[k] = {}
        for b in bk:
            bank.setdefault(b, {})[q] = tok

    def op(q, fn, r, w, bk):
        r, w, bk = r.split(), w.split(), bk.split()
        deps(q, r, w, bk)
        fn(queues[q]).then_inc(T.sem[q], 1)
        cnt[q] = cnt.get(q, 0) + 1
        note(q, (q, cnt[q]), r, w, bk)

    def dma(q, sem, out, in_, r="", w=""):
        deps(q, r.split(), w.split(), ())
        queues[q].dma_start(out, in_).then_inc(T.sem[sem], 16)
        cnt[sem] = cnt.get(sem, 0) + 16
        for k in w.split():
            lastw[k] = (sem, cnt[sem])

    def mm(out, lhsT, rhs, start, stop, r, w, bk):
        op("t", lambda e: e.matmul(out, lhsT, rhs, start, stop), r, w, bk)

    def cp(q, out, in_, r, w, bk=""):
        if q == "s":
            op("s", lambda e: e.activation(out, in_, F.Copy), r, w, bk)
        else:
            op("v", lambda e: e.tensor_copy(out, in_), r, w, bk)

    def tt(out, a, b, o, r, w, bk=""):
        op("v", lambda e: e.tensor_tensor(out, a, b, o), r, w, bk)

    def ts(out, a, s1, o0, r, w, bk="", s2=None, o1=None):
        if o1 is None:
            op("v", lambda e: e.tensor_scalar(out, a, s1, None, o0), r, w, bk)
        else:
            op("v", lambda e: e.tensor_scalar(out, a, s1, s2, o0, o1), r, w, bk)

    def scan(out, a, b, o0, o1, r, w, bk=""):
        op("v", lambda e: e.tensor_tensor_scan(out, a, b, 0.0, o0, o1), r, w, bk)

    def act(out, in_, f, r, w, bk="", bias=0.0, scale=1.0):
        op("s", lambda e: e.activation(out, in_, f, bias=bias, scale=scale), r, w, bk)

    def scatter(out, in_, r, w):
        op("s", lambda e: e.activation(out, in_, F.Silu), r, w, "")

    def fill(ap, val, w):
        op("v", lambda e: e.memset(ap, val), "", w, "")

    def iota(out, pat, base, cm, w):
        if out.dtype == dt.int32:
            op("g", lambda e: e.iota(out, pat, base, cm), "", w, "")
        else:
            op("g", lambda e: e.iota(out, pat, base, cm, allow_small_or_imprecise_dtypes=True), "", w, "")

    def select(out, in_, pat, o, other, base, cm, r, w):
        op("g", lambda e: e.affine_select(out, in_, pat, o, other, base, cm), r, w, "")

    def turn(out, in_, r, w):
        op("v", lambda e: e.transpose(out, in_), r, w, "")

    def send(out, in_, rsem, dst, r):
        deps("g", r.split(), (), ())
        eng = topo.engines(core, dst)[:8]
        rid, pid = topo.addr(dst, core)
        g.remote_dma(out, in_, T.sem[rsem], T.sem.loc, pid, rid, sum(1 << e for e in eng))
        cnt["loc"] = cnt.get("loc", 0) + len(eng)

    PK, Ib = T.P3, T.Ib[:]

    def swap():
        for z in range(2):
            for y in range(2):
                mm(PK[:, 0:8, z, :], T.Ax[:, 2 * z + y], T.St[:, :, y, :], y == 0, y == 1, "Ax%d St" % (2 * z + y), "pK", "P3")

    def rotate(back):
        for j in range(16):
            r = (-5 * j if back else 5 * j) % 16
            mm(T.P1[:, j:256:16], T.Wr[:, r] if r else Ib, T.Sh[:, j:256:16], True, True, "Ib Wr%d Sh" % r, "pA", "P1")

    dma("y", "dsl", T.S0[:], T.slips[:, :], w="S0")
    dma("y", "dr", T.recb[:], T.rec[:, :], w="recb")
    dma("y", "dk", T.K0[:, O:WT], T.kin[:, :], w="K0")
    dma("y", "dx", T.Xw[:, O:WT], T.wealth[:, :], w="Xw")

    cP, cM, cG, cZ, cY, cW, cT, cK, cX, cD, cH = [T.col[:, k:k + 1] for k in range(11)]
    A0, torn, B0, B1 = 0, 32, 52, 104
    iota(T.pi[:, 0:2], [[0, 2]], 0, 1, "pi")
    iota(T.Id[:, 0:256], [[1, 256]], 0, 0, "Id0")
    iota(T.Rb[:], [[1, 16], [0, 16]], 0, 0, "Rb")
    iota(T.Id[:, 256:WT], [[1, WT - 256]], 256, 0, "Id")
    for n in ("K0", "Kw", "Vw", "Xw", "Rw"):
        fill(T[n][:, 0:O], 0 if n == "K0" else 32.0, n + "p")
    fill(T.Ax[:], 0.0, "Ax0 Ax1 Ax2 Ax3")
    cp("v", cP, T.pi[:, 0:1], "pi", "cP")
    ts(T.pi[:, 2:3], T.pi[:, 0:1], 15, A.bitwise_and, "pi", "pm")
    ts(Ib, T.Id[:, 0:128], cP, A.is_equal, "Id0 cP", "Ib")
    cp("v", cM, T.pi[:, 2:3], "pm", "cM")
    for k in range(2):
        cp("v", T.Wc[:, :, 16 * k:16 * k + 16], Ib, "Ib", "Wc%d" % k)
    for r in range(1, 16):
        cp("s" if r % 3 == 0 else "v", T.Wr[:, r], T.Wc[:, :, r:r + 16], "Wc0 Wc1", "Wr%d" % r)
    fill(T.zero[:], 0.0, "zero")
    tt(cZ, cP, cM, A.subtract, "cP cM", "cZ")
    fill(T.Z[:], 0.0, "inst torn mv UB c")
    ts(T.Sh[:], T.S0[:], float(O), A.add, "S0", "Sh")
    rotate(False)
    for k in range(4):
        cp("v", T.Ax[:, k, :, k % 2, :], T.Ib[:, :, k // 2, :], "Ib", "Ax%d" % k)
    cp("v", T.Si[:], T.P1[:, 0:256], "pA", "Si", "P1")
    turn(T.St[:], T.Si[:], "Si", "St")
    swap()
    ts(T.Dm[:], T.Rb[:], cM, A.is_equal, "Rb cM", "Dm")
    cp("v", T.cu0[:], PK[:, 0:8, :, 0], "pK", "cu0", "P3")
    send(T.rcv0[:], T.cu0[:], "rl0", T.cores[(rank + 1) % 6], "cu0")
    c = T.Z[:, B1 + 5:B1 + 52:3]
    cp("v", c, PK[:, 0:8, :, 0], "pK", "c", "P3")
    cp("v", T.SL[:], PK[:, 0:8], "pK", "SL", "P3")
    iota(T.Rj[:], [[0, 16], [1, 8]], 0, 0, "Rj")
    iota(T.Cm[:], [[0, 16], [-1, 16]], 15, 0, "Cm")
    select(T.seg[:], T.zero[:], [[0, 16], [1, 16]], A.is_equal, 1.0, 0, 0, "zero", "seg")
    select(T.K16[:], T.zero[:, 0:32], [[1, 32]], A.is_ge, 16.0, -(LA // 16), 0, "zero", "K16")
    select(T.In[:], T.zero[:, 0:128], [[-1, 128]], A.not_equal, -128.0, 0, 1, "zero", "In")

    def constants(n):
        if n > 0:
            select(T.Is[:, n - 1], T.zero[:, 0:128], [[-1, 128]], A.not_equal, math.exp(-4.0 * n), 0, 1, "zero", "Is%d" % n)
        if n < NR - 1:
            select(T.LT[:, n], Ib, [[0, 8], [1, 16]], A.is_equal, 0.0, -n, 0, "Ib", "LT%d" % n)
            select(T.ND[:, n], Ib, [[0, 8], [1, 16]], A.not_equal, 0.0, -n, 0, "Ib", "ND%d" % n)
            select(T.Iv[:, n], T.zero[:, 0:128], [[-1, 128]], A.not_equal, power(8 + n), 0, 1, "zero", "Iv%d" % n)

    constants(0)
    constants(1)
    act(cW, cM, F.Exp, "cM", "cW", scale=-math.log(4.0))
    for col, name, src, key, scale, bias in ((cG, "cG", cZ, "cZ", 1.0 / 16, 0.0), (cY, "cY", cZ, "cZ", 1.0, 15.0), (cD, "cD", cM, "cM", 1.0, float(WT)),
                                             (cK, "cK", cM, "cM", 16.0, 7.5), (cX, "cX", cM, "cM", 16.0, 0.0), (cT, "cT", cW, "cW", 32.0, 0.0)):
        act(col, src, F.Copy, key, name, scale=scale, bias=bias)
    act(T.Vw[:, O:WT], T.recb[:], F.Exp, "recb Vwp", "Vw", scale=4.0, bias=3.0)
    act(T.NDH[:], T.Dm[:], F.Copy, "Dm", "NDH", scale=-9e28, bias=9e28)
    act(T.A1[:, 1:32:2], T.Id[:, 0:256:16], F.Identity, "Id0 cD", "dum", bias=cD)
    act(T.bas[:], T.Id[:, 0:8], F.Identity, "Id0 cX", "bas", bias=cX)
    act(T.sm[:, 0:8], T.Id[:, 0:8], F.Identity, "Id0 cM", "h", scale=0.0, bias=cM)
    ts(T.BO4[:], T.Rb[:, 0:128], cG, A.is_equal, "Rb cG", "BO4", s2=4.0, o1=A.mult)
    ts(T.W4[:], T.Rb[:, 0:128], cG, A.is_equal, "Rb cG cW", "W4", s2=cW, o1=A.mult)

    def late_constants():
        ts(cH, cM, 8.0, A.is_ge, "cM", "cH", s2=128.0, o1=A.mult)
        ts(T.Gs[:], T.Id[:, 0:8], cG, A.is_equal, "Id0 cG", "Gs", s2=16.0, o1=A.mult)
        ts(T.Zw[:], T.Id[:, 0:144], cY, A.is_equal, "Id0 cY", "Zw")
        ts(T.Zj[:], T.Id[:, 0:240], -112.0, A.add, "Id0 cM", "Zj", s2=cM, o1=A.is_equal)
        ts(T.RL2[:], T.Id[:, 15:128:16], cH, A.add, "Id0 cH", "RL2")
        cp("v", T.offs[:, 0:1], cX, "cX", "off0")
        ts(T.RL[:], T.sm[:, 0:8], 2.0, A.mult, "h", "RL", s2=1.0, o1=A.add)
        ts(T.E[:], T.Rj[:], cG, A.is_equal, "Rj cG", "E")

    act(T.DTH[:], T.NDH[:], F.Silu, "NDH", "DTH", bias=0.8 * power(5))

    inst, dum = T.Z[:, A0 + 1:A0 + 32:2], T.A1[:, 1:32:2]
    Pc, Pf, Po, Py, Pb = T.P6[:, 0:16], T.P6[:, 32:48], T.P6[:, 48:64], T.P1[:, 256:257], T.P7[:, 0:16]
    SUMS = ((T.P0, 0, 0, LA, "pS", "P0"), (T.P5, 256, LA, 256, "pT", "P5"))
    ASKED = ((T.P1, "pA", "P1"), (T.P7, "pQ", "P7"))
    for t in range(NR):
        first, last = t == 0, t == NR - 1
        cu, rcv, scl, rep, rrv = [T["%s%d" % (n, t)] for n in ("cu", "rcv", "scl", "rep", "rrv")]
        cuk, sclk = "cu%d" % t, "scl%d" % t
        p = T.cores[(rank - 1 - t % 5) % 6]
        for x in "lab":
            lastw["r" + x] = ("r%s%d" % (x, t), 8)

        def kin(out, lst, r, w):
            if first:
                ts(out, T.K0[:].indirect(lst), float(O), A.add, "K0 K0p " + r, w)
            else:
                ts(out, T.Kw[:, 0:WT].indirect(lst), 0.25, A.add, "Kw " + r, w)

        def ask(k):
            a, b = ASK[k]
            cp("s" if k else "v", T.Vq[:, 16 * a:16 * b], T.Vw[:, 0:WT].indirect(T.kcq[:, a:b]), "Vw kcq", "Vq%d" % k)

        def ask_mm(k):
            a, b = ASK[k]
            P, key, bk = ASKED[k // 3]
            for m in range(16):
                mm(P[:, a:b], Ib, T.Vq[:, 16 * a + m:16 * b:16], m == 0, m == 15, "Ib Vq%d" % k, key, bk)

        def reply(x):
            a, b = SUMS[x][2:4]
            P, key, bk = ASKED[x]
            cp("s", rep[:, a:b], P[:, a:b], key, "rep%d%d" % (t, x), bk)
            send(rrv[:, a:b], rep[:, a:b], "r%s%d" % ("ab"[x], t), p, "rep%d%d" % (t, x))

        def own(k):
            a, b = OWN[k]
            if a < LA:
                cp("s", T.Vg[:, 16 * a:16 * b], T.Vw[:, 0:WT].indirect(T.kc[:, a:b]), "Vw kc", "Vg%d" % k)
                return
            for x, y in ((0, MB), (MB, 16)):
                cp("s", T.Vg[:, 16 * a + NB * x:16 * a + NB * y], T.Vw[:, 0:WT].indirect(T.ktb[:, NB // 16 * x:NB // 16 * y]), "Vw ktb", "Vh%d" % x)

        def add(x, a, b, rhs, start, stop, r):
            P, o, _, _, key, bk = SUMS[x]
            mm(P[:, o + a:o + b], T.Is[:, t - 1] if t else Ib, rhs, start, stop, "Ib Is%d %s" % (t, r), key, bk)

        def own_mm(k):
            a, b = OWN[k]
            x = 1 if a == LA else 0
            if a in (0, LA):
                add(x, a, SUMS[x][3], T.VC[:, a:SUMS[x][3]], True, False, "VC")
            for m in range(16):
                if x:
                    add(x, a, b, T.Vg[:, 16 * a + NB * m:16 * a + NB * (m + 1)], False, False, "Vh%d" % (0 if m < MB else MB))
                else:
                    add(x, a, b, T.Vg[:, 16 * a + m:16 * b:16], False, False, "Vg%d" % k)

        def bars(x):
            P, o, a, b, key, bk = SUMS[x]
            add(x, a, b, rrv[:, a:b], False, True, "r" + "ab"[x])
            bar = 0.8 * power(6)
            if x == 0:
                act(T.UU[:, a:b], P[:, o + a:o + b], F.Sign, key, "U20", bk, scale=1.0 / bar, bias=-1.0)
            else:
                ts(T.UU[:, a:b], P[:, o + a:o + b], bar, A.is_ge, key, "U21", bk, s2=2.0, o1=A.mult)
            tt(T.UU[:, 256 + a:256 + b], P[:, o + a:o + b], T.DTH[:, a:b], A.is_ge, key + " DTH", "U3%d" % x, bk)

        def kins():
            kin(T.kc[:], cu[:], cuk, "kc")
            cp("v", T.kc16[:], T.kc[:], "kc", "kc16")
            tt(T.A1[:, 0:32:2], c, dum, A.subtract, "c dum", "dc")
            turn(T.kt[:], T.kc16[:], "kc16", "kt")
            for B in range(8):
                for z in range(2):
                    for y in range(2):
                        mm(PK[:, 8:16, :, 2 * B + z], T.Ax[:, 2 * z + y], T.kt[:, B, y, :], y == 0, y == 1, "Ax%d kt" % (2 * z + y), "pM", "P3")

        def equal(b0, b1):
            for b in range(b0, b1):
                ts(T.EQ[:, b, 0:256 - 16 * b], T.crow[:, 16 * b:256], T.Z[:, B1 + 5 + 3 * b:B1 + 6 + 3 * b], A.is_equal, "crow c", "EQ%d" % b)

        def equal_mm():
            mm(T.P5[:, 0:256], T.W4[:], T.EQ[:, :, 0:16], True, False, "W4 EQ15", "pcnt", "P5")
            for b in range(15):
                mm(T.P5[:, 16 * b + 16:256], T.BO4[:], T.EQ[:, b, 16:256 - 16 * b], False, b == 14, "BO4 EQ15", "pcnt", "P5")

        def riches():
            cp("s", T.XC[:, 0:256], T.Xw[:].indirect(cu[:]), "Xw Xwp " + cuk, "XC")
            for n in (256, 512):
                select(T.XC[:, n:2 * n], T.XC[:, 0:n], [[0, n]], A.is_gt, 0.0, 1, 0, "XC", "XC")
            if 0 < t < NR - 1:
                constants(t + 1)

        def new_mm():
            mm(T.P4[:, 0:256], T.ND[:, t], T.kc16[:], True, False, "ND%d kc16" % t, "pnK", "P4")
            mm(T.P4[:, 0:256:2], T.LT[:, t], T.crow[:, 1:256:2], False, False, "LT%d crow" % t, "pnK", "P4")
            mm(T.P4[:, 1:256:2], T.LT[:, t], T.crow[:, 0:256:2], False, True, "LT%d crow" % t, "pnK", "P4")
            mm(T.P4[:, 256:512], Ib, T.VC[:], True, False, "Ib VC", "pnV", "P4")
            mm(T.P4[:, 256:512], T.Iv[:, t], T.Dm[:], False, True, "Iv%d Dm" % t, "pnV", "P4")

        def score_mm(m0, m1):
            if m0 == 0:
                mm(T.P2[:, 0:256], Ib, T.Cm[:], True, False, "Ib Cm", "pKey", "P2")
            for m in range(m0, m1):
                for h in range(2):
                    a = 256 * (m % 4) + 128 * h
                    mm(T.P2[:, 128 * h + m:128 * h + 128:16], T.Dx[:, m // 4, a:a + 128], T.Gs[:], False, m == 15 and h == 1,
                       "Gs Dx%d" % (m // 4), "pKey", "P2")

        cp("v", T.crow[:], T.Id[:].indirect(cu[:]), "Id Id0 " + cuk, "crow")
        if first:
            equal(0, 16)
            late_constants()
            kins()
            ts(T.Kw[:, O:WT], T.K0[:, O:WT], float(O), A.add, "K0 Kwp", "Kw")
        else:
            kins()
            equal(0, EQA)
        cp("v", T.kts[:], PK[:, 8:16], "pM", "kts", "P3")
        cp("v", T.ktb[:], PK[:, 8:16, :, LA // 16:16], "pM", "ktb", "P3")
        cp("s", T.VC[:], T.Vw[:, 0:WT].indirect(cu[:]), "Vw " + cuk, "VC")
        if not first:
            riches()
            equal(EQA, 16)
        kin(T.kcq[:], rcv[:], "rl", "kcq")
        own(0)
        if first:
            riches()
            own(1)
        for k in range(4):
            ask(k)
        for h in range(2):
            mm(PK[:, 4 * h:4 * h + 4], T.kc16[:, 128 * h:128 * h + 128], Ib, True, True, "kc16 Ib", "pK", "P3")
        if not last:
            new_mm()
        equal_mm()
        own_mm(0)
        ask_mm(1)
        ask_mm(0)
        ask_mm(2)
        reply(0)
        ask_mm(3)
        cp("s", T.cn[:], T.P5[:, 0:256], "pcnt", "cn", "P5")
        reply(1)
        for k in range(4):
            tt(T.Dx[:, k], T.Xw[:].indirect(T.kts[:, 64 * k:64 * k + 64]), T.XC[:], A.max, "Xw kts XC", "Dx%d" % k)
        for j in range(16):
            mm(Pc, T.Zw[:, 15 - j:143 - j], T.cn[:, j:256:16], j == 0, j == 15, "Zw cn", "pC", "P6")
        for k in range(2 if first else 1, 4):
            own(k)
        score_mm(0, 8)
        own_mm(1)
        score_mm(8, 16)
        ts(T.NC[:], Pc, cT, A.is_ge, "pC cT", "NC", "P6")
        own_mm(2)
        mm(T.P6[:, 32:64], Ib, T.K16[:], True, False, "Ib K16", "pF", "P6")
        mm(Pf, T.In[:], T.NC[:], False, False, "In NC", "pF", "P6")
        mm(Po, Ib, T.NC[:], False, False, "Ib NC", "pF", "P6")
        key = T.P2[:, 0:256]
        scan(T.y[:], T.seg[:], key, A.mult, A.max, "seg pKey", "y", "P2")
        tt(T.eqn[:], key, T.y[:], A.is_equal, "pKey y", "eqn", "P2")
        tt(T.ek[:], PK[:, 0:8], T.eqn[:], A.mult, "pK eqn", "ek", "P3")
        bars(0)
        if last:
            ts(T.neq[:], T.eqn[:], -1.0, A.mult, "eqn", "neq", s2=1.0, o1=A.add)
        else:
            act(T.neq[:], T.eqn[:], F.Copy, "eqn", "neq", scale=-1.0, bias=1.0)
        own_mm(3)
        if not last:
            cp("s", T.nK[:], T.P4[:, 0:256], "pnK", "nK", "P4")
            cp("s", T.nV[:], T.P4[:, 256:512], "pnV", "nV", "P4")
            if first:
                act(T.D12[:], T.Dm[:], F.Copy, "Dm", "D12", scale=12.0)
        else:
            for k in range(2):
                act(T.lnb[:, k * H:k * H + H], T.Vw[:, O + k * H:O + k * H + H], F.Ln, "Vw", "lnb%d" % k, scale=math.exp(-33.0))
        bars(1)
        for j in range(16):
            mm(T.P6[:, 32:64], T.Zw[:, 15 - j:143 - j], T.UU[:, j:512:16], False, j == 15, "Zw U20 U21 U30 U31", "pF", "P6")
        scan(T.s2[:], T.neq[:], T.ek[:], A.mult, A.add, "neq ek", "s2")
        tt(T.Bx[:], T.s2[:].indirect(T.RL2[:]), T.E[:], A.mult, "s2 RL2 E", "Bx")
        for k in range(8):
            mm(Pb, T.Zj[:, 112 - 16 * k:240 - 16 * k], T.Bx[:, 16 * k:16 * k + 16], k == 0, k == 7, "Bx Zj", "pB", "P7")
        h, t12, cand = T.sm[:, 0:16], T.sm[:, 16:32], T.sm[:, 32:48]
        tn, tnext, moved = T.Z[:, torn:torn + 16], T.Z[:, torn + 1:torn + 17], T.Z[:, B0 + 4:B0 + 52:3]
        ts(h, Pf, 16.0, A.is_lt, "pF", "h", "P6")
        ts(t12, Pf, 24.0, A.is_ge, "pF", "t12", "P6")
        tt(inst, h, Po, A.is_gt, "h pF", "inst", "P6")
        ts(T.fi[:, 0:16], Pf, 0.5, A.mult, "pF", "fi", "P6")
        if not last:
            cp("s", T.nirep[:], T.Z[:, A0:A0 + 32].indirect(T.RL[:]), "inst RL", "nirep")
            mm(Py, Ib, T.bas[:, t + 1:t + 2], True, False, "Ib bas", "pY", "P1")
            mm(Py, T.nirep[:], T.seg[:, 1:2], False, True, "nirep seg", "pY", "P1")
        scan(T.Ao[:], T.Z[:, A0:A0 + 32], T.A1[:], A.mult, A.add, "inst dc dum", "Ao")
        tt(tn, t12, inst, A.add, "t12 inst", "torn")
        cp("v", scl[:], T.Ao[:, 1:32:2], "Ao", sclk)
        ts(T.fi[:, 16:32], T.fi[:, 0:16], -31, A.bitwise_and, "fi", "odd")
        if not last:
            scatter(T.Kw[:].indirect(scl[:]), T.nK[:], "nK " + sclk, "Kw")
            scatter(T.Vw[:].indirect(scl[:]), T.nV[:], "nV " + sclk, "Vw")
        tt(T.Z[:, B1 + 4:B1 + 51:3], Pb, c, A.subtract, "pB c", "d1", "P7")
        tt(cand, T.fi[:, 16:32], tn, A.is_gt, "odd torn", "cand")
        tt(T.Z[:, B1 + 3:B1 + 50:3], T.Z[:, B1 + 2:B1 + 48:3], Pb, A.subtract, "pB c", "d2", "P7")
        tt(moved, cand, tnext, A.mult, "cand torn", "mv")
        if not last:
            ts(T.kk[:], Py, cK, A.subtract, "pY cK", "kk", "P1", s2=1.0 / 16, o1=A.mult)
        tt(T.Z[:, B0 + 2:B0 + 48:3], tn, moved, A.add, "torn mv", "UB")
        if not last:
            ts(T.offs[:, 2 * t + 2:2 * t + 3], T.kk[:], -16.0, A.mult, "kk pY", "off%d" % (t + 1), "P1", s2=Py, o1=A.add)
        scan(T.Bo[:], T.Z[:, B0:B0 + 48], T.Z[:, B1 + 3:B1 + 51], A.mult, A.add, "mv UB c d1 d2", "Bo")
        cp("v", T.SL[:].indirect(T.offs[:, 2 * t:2 * t + 1]), T.Bo[:, 2:48:3], "Bo off%d" % t, "SL")
        if not last:
            n = t + 1
            cp("v", T["cu%d" % n][:], T.SL[:].indirect(T.offs[:, 2 * n:2 * n + 1]), "SL off%d" % n, "cu%d" % n)
            send(T["rcv%d" % n][:], T["cu%d" % n][:], "rl%d" % n, T.cores[(rank + 1 + n % 5) % 6], "cu%d" % n)
            cp("v", c, T.SL[:].indirect(T.offs[:, 2 * n:2 * n + 1]), "SL off%d" % n, "c")
        else:
            cp("v", T.St[:], T.SL[:], "SL", "St")
            swap()
            for k in range(2):
                ts(T.Rw[:, O + k * H:O + k * H + H], T.lnb[:, k * H:k * H + H], 30.0, A.add, "lnb%d Rwp" % k, "Rw%d" % k, s2=0.25, o1=A.mult)
                if k == 0:
                    cp("v", T.Si[:], PK[:, 0:8], "pK", "Si", "P3")
                    turn(T.Sh[:], T.Si[:], "Si", "Sh")
                    rotate(True)
            act(T.ysb[:], T.P1[:, 0:256], F.Copy, "pA", "ysb", "P1", bias=-float(O))
            dma("s", "dout", T.ys[:, :], T.ysb[:], r="ysb")
            tt(T.nR[:], T.Rw[:, 0:WT].indirect(cu[:]), T.D12[:], A.max, "Rw0 Rw1 D12 " + cuk, "nR")
            cp("v", T.Rw[:].indirect(scl[:]), T.nR[:], "nR " + sclk, "Rw")
            dma("y", "dout", T.yr[:, :], T.Rw[:, O:WT], r="Rw")
    for s in ("v", "s", "t", "g", "dsl", "dk", "dr", "dx", "loc", "dout"):
        wait("g", (s, cnt[s]))
    for s in REMOTE:
        wait("g", (s, 8))
